import numpy as np, ml_dtypes
CORES = [5,29,101,125,133,157,229,253]
N = 8
import mx_ref
BF = ml_dtypes.bfloat16
def gcols(t, e):
    v = np.concatenate([t.reshape(8, 16, -1, 4), np.zeros((8, 16, 1, 4), BF)], axis=2)
    return np.ascontiguousarray(np.stack([v[g][:, e[g]] for g in range(8)])).reshape(128, -1)
def tile(rs):
    return np.stack(rs, axis=2).reshape(128, -1).astype(BF)
def pick(q, e):
    c = np.concatenate([q[0].reshape(128, -1, 4), np.zeros((128, 1, 4), np.uint8)], axis=1); s = np.concatenate([q[1], np.ones((16, 1), np.uint8)], axis=1)
    return (np.ascontiguousarray(c[:, e].reshape(128, -1)), np.ascontiguousarray(s[:, e]))
def join(*qs):
    return (np.concatenate([q[0] for q in qs], axis=1), np.concatenate([q[1] for q in qs], axis=1))
def put(q, e, v):
    c, s = q[0].reshape(128, -1, 4).copy(), q[1].copy(); c[:, e] = v[0].reshape(128, -1, 4); s[:, e] = v[1]
    return (c.reshape(128, -1), s)
def pk(c, s):
    return (np.ascontiguousarray(c), mx_ref.live(s))
def emit(q):
    return q[0], q[1]
def packed(v, rng):
    q = [mx_ref.quantize(np.ascontiguousarray(v[r])) for r in range(N)]
    return np.stack([a for a, b in q]), np.stack([mx_ref.plane(b, rng) for a, b in q])
def values_of_codes():
    e, c = np.zeros((128, 128, 4), np.float32), np.zeros((128, 2, 4), np.uint8)
    e[np.arange(128), np.arange(128), 0] = 1
    c[:127, :, 0] = np.arange(256).reshape(2, 128).T[:127]
    return mx_ref.matmul(mx_ref.quantize(e.reshape(128, 512).astype(BF)), (c.reshape(128, 8), np.full((16, 2), 127, np.uint8))).T.reshape(-1).astype(np.float64)
CODE_VALUE, SCALE_VALUE = values_of_codes(), 2.0 ** (np.arange(256) - 127.0)
def decode(q):
    return (CODE_VALUE[q[0]].reshape(16, 8, -1, 4) * SCALE_VALUE[q[1]][:, None, :, None] + 0.0).reshape(128, -1).astype(np.float32)
def f(rng, *shape):
    return mx_ref.flush((rng.standard_normal(shape, dtype=np.float32) * np.exp2(rng.integers(-2, 3, shape[:-1] + (1,)))).astype(BF))
def wide(rng, *shape, cols=0):
    v = rng.standard_normal(shape, dtype=np.float32) * np.exp2(rng.integers(-12, 13, shape)).astype(np.float32)
    if cols: v *= np.repeat(np.exp2(rng.integers(-cols, cols + 1, shape[:-2] + (1, shape[-1] // 4))) * (rng.random(shape[:-2] + (1, shape[-1] // 4)) > 0.0625), 4, axis=-1).astype(np.float32)
    return mx_ref.flush(v.astype(BF))
C, A, R = 256, 64, 3
HOP = [2, 5, 3]
def lengths(p):
    z = p + np.float32(0.0)
    return 1 + (z[::16] > 0) + 2 * (z[1::16] > 0)
def walk(n):
    m, k, now = np.zeros((8, N * C + 4), bool), np.zeros((8, N * C), np.int64), np.full(8, -1)
    m[:, 0] = True
    for p in range(N * C):
        if p % C == 0: now = np.full(8, -1)
        now = now + m[:, p]
        k[:, p] = now
        m[np.arange(8), p + n[:, p]] |= m[:, p]
    return m[:, :N * C], k
def big(v):
    v = v.astype(np.float32)
    v[np.abs(v) < np.float32(2.0 ** -16)] = 0
    return v.astype(BF)
def numbers_of(rng):
    return {"x": big(f(rng, N, 128, 4 * C)), "u": np.array(f(rng, N, 128, 512)), "v": np.array(f(rng, N, 128, 512))}
def layers(rng):
    return big(f(rng, N, 128, 2048)).reshape(N, 8, 16, 4, 8, 16, 4)
def weights(rng, w):
    c, p = packed(w.reshape(N, 128, 2048), rng)
    return {"wc": c, "ws": p}
def setup_inputs(rng):
    return {**numbers_of(rng), **weights(rng, layers(rng))}
def setup_inputs_chains(rng):
    d = numbers_of(rng)
    k = rng.permutation(N) % 4
    unit = np.exp2(np.array([-28.0, -10.0, 0.0, 26.0])[k]).astype(np.float32)[:, None, None]
    by = np.exp2(np.array([-30.0, 0.0, 0.0, 30.0])[k]).astype(np.float32).astype(BF)
    o = rng.permutation(8)
    n = np.array([4, 4, 4, 3, 3, 2, 2, 1])[o]
    e = np.zeros((2, N, 8, C), np.float32)
    e[0] = np.where(n % 2 == 0, 8, -8)[None, :, None]
    e[1] = np.where(n > 2, 8, -8)[None, :, None]
    e[0, 0, :, 0] = np.where(o % 2 == 1, -1.0, -0.5)
    e[1, 0, :, 0] = np.where(o == 2, 1.0, 1.5)
    e[1, 1, o == 1, 3] = -8
    e[1, 2, o == 1, 1] = -8
    x = d["x"].reshape(N, 8, 16, C, 4)
    x[:, :, :8] = 0
    x[:, :, 0, :, 0] = (e[0] * unit).astype(BF)
    x[:, :, 1, :, 0] = (e[1] * unit).astype(BF)
    x[:, :, 2, :, 0] = unit.astype(BF)
    u = d["u"].reshape(N, 128, 128, 4)
    u[:, :, ::16] = 0
    u[:, :, 1::16] = 0
    w = layers(rng)
    w[:, :, :8] = 0
    w[:, :, :, :, :, :8] = 0
    for g in range(8):
        u[:, 16 * g, 16 * g, 0] = by
        u[:, 16 * g + 1, 16 * g + 1, 0] = by
        w[:, g, 2, 0, g, 0, 0] = 32
        w[:, g, 2, 0, g, 1, 0] = -32
    return {"x": x.reshape(N, 128, 4 * C), "u": u.reshape(N, 128, 512), "v": d["v"], **weights(rng, w)}
def setup_inputs_copies(rng):
    d = numbers_of(rng)
    o = rng.permutation(N)
    x = d["x"].reshape(N, 8, 16, C, 4)
    for r in range(N):
        k = rng.permutation(C) % 2 if r == o[1] else np.zeros(C, int)
        a = x[r][:, :8, :2].copy()
        x[r][:, :8] = a[:, :, k]
    x[o[0], :, :8] = 0
    u = d["u"].reshape(N, 8, 16, 128, 4)
    u[:, :, 8:, ::16] = 0
    u[:, :, 8:, 1::16] = 0
    w = layers(rng)
    w[:, :, 8:, :, :, :8] = 0
    return {"x": x.reshape(N, 128, 4 * C), "u": u.reshape(N, 128, 512), "v": d["v"], **weights(rng, w)}
def setup_inputs_spread(rng):
    d = setup_inputs(rng)
    d["x"] = big(wide(rng, N, 128, 4 * C, cols=6))
    return d
def check_inputs(d):
    b = []
    for k in ("x", "u", "v"):
        a = np.abs(d[k].astype(np.float32))
        if not (np.isfinite(a).all() and ((a == 0) | (a >= 2.0 ** -30) & (a <= 2.0 ** 30)).all()): b.append("a value of " + k)
    if ((d["wc"] & 127) == 127).any(): b.append("a code of wc is no number")
    for r in range(N):
        a = np.max(np.abs(CODE_VALUE[d["wc"][r]]).reshape(16, 8, 512, 4), axis=(1, 3)) * SCALE_VALUE[mx_ref.live(d["ws"][r])]
        if not ((a == 0) | (a >= 0.875 * 2.0 ** -30) & (a <= 1.125 * 2.0 ** 30)).all(): b.append("the largest size of a block of W")
    return b
def reference(x, u, v, wc, ws):
    qu = [mx_ref.quantize(u[r]) for r in range(N)]
    lay = [pk(wc[r], ws[r]) for r in range(N)]
    now = [x[r] for r in range(N)]
    first = [None] * N
    for t in range(R):
        q = [mx_ref.quantize(now[r]) for r in range(N)]
        n = np.concatenate([lengths(mx_ref.matmul(qu[r], q[r])) for r in range(N)], axis=1)
        mark, body = walk(n)
        for r in range(N):
            own = slice(C * r, C * r + C)
            s = np.argsort(~mark[:, own], axis=1, kind="stable")[:, :A]
            last = np.minimum(s + np.take_along_axis(n[:, own], s, axis=1) - 1, C - 1)
            val = decode(q[r]).astype(BF)
            pack = ((gcols(val, s).astype(np.float32) + gcols(val, last).astype(np.float32)) * np.float32(0.5)).astype(BF)
            sent = mx_ref.quantize(pack)
            w = lay[(r + HOP[t]) % N]
            h = tile([mx_ref.matmul(pick(w, np.arange(128 * b, 128 * b + 128)), sent) * np.float32(0.03125) for b in range(4)])
            came = decode(mx_ref.quantize(h)).astype(BF)
            k = body[:, own]
            now[r] = (now[r].astype(np.float32) + gcols(came, np.where(k < 0, -1, k % A)).astype(np.float32)).astype(BF)
            first[r] = s
    y, ol = np.zeros((N, 128, C), np.float32), np.zeros((N, 8, A), np.float32)
    oc, osc = np.zeros((N, 128, 4 * C), np.uint8), np.zeros((N, 16, C), np.uint8)
    for r in range(N):
        q = mx_ref.quantize(now[r])
        y[r] = mx_ref.matmul(mx_ref.quantize(v[r]), q)
        ol[r] = first[r]
        oc[r], osc[r] = emit(q)
    return {"y": y, "ol": ol, "oc": oc, "osc": osc}

@@ -1,0 +1,570 @@
+from concourse.bass import DstId, RemoteDMATransfer
+from concourse.mybir import dt, AluOpType, ActivationFunctionType
+
+A = AluOpType
+ACT = ActivationFunctionType
+N, C, R, HOP = 8, 256, 3, [2, 5, 3]
+Q, S, BF, F, I, U = "float8_e4m3fn_x4", "uint8", "bfloat16", "float32", "int32", "uint16"
+
+
+def _sb(n, d):
+    return ("sbuf", [128, n], d)
+
+
+SCRATCH = {
+    "xn": _sb(1024, BF), "un": _sb(512, BF), "vn": _sb(512, BF), "ta": _sb(1024, BF), "tb": _sb(1024, BF), "tn": _sb(1024, BF),
+    "qx": _sb(256, Q), "sx": _sb(256, S), "qu": _sb(128, Q), "su": _sb(128, S), "qv": _sb(128, Q), "sv": _sb(128, S),
+    "qo": _sb(256, Q), "so": _sb(256, S), "qw": _sb(512, Q), "sw": _sb(512, S), "qp": _sb(512, Q), "sp": _sb(512, S),
+    "rq": _sb(256, Q), "rs": _sb(256, S), "ez": _sb(520, BF), "qe": _sb(512, Q), "se": _sb(512, S),
+    "qm": _sb(768, Q), "sm": _sb(768, S), "zt": _sb(512, BF), "ft": _sb(512, BF), "ht": _sb(512, BF),
+    "ci": _sb(8, I), "cj": _sb(2, I), "cf": _sb(8, F), "cc": _sb(16, F), "ku": _sb(112, U), "r256": _sb(256, F), "jrow": _sb(256, F),
+    "io3": _sb(256, F), "k64": _sb(640, F), "bt": _sb(288, BF), "tt": _sb(544, BF), "ga": _sb(40, F),
+    "nbo": _sb(32, U), "yo": _sb(8, F),
+    "off1": _sb(32, U), "x1": _sb(320, F), "wm": _sb(64, F), "wsn": _sb(64, F), "off2": _sb(32, U), "ca": _sb(128, F),
+    "y2": _sb(144, F), "y3": _sb(32, F), "off3": _sb(2, U), "ex": _sb(16, F), "z": _sb(272, F), "la": _sb(64, F), "lu": _sb(16, U),
+    "wf": _sb(512, F), "wi": _sb(256, I), "cand": _sb(128, F), "selo": _sb(32, U), "ll": _sb(32, U), "sc": _sb(928, F),
+    "st": _sb(128, F), "fl": _sb(16, U), "vv": _sb(1024, BF), "vl": _sb(1024, BF), "ff": _sb(1024, BF), "dh": _sb(320, BF),
+    "ud": _sb(128, F), "ut": _sb(128, F), "ln": _sb(16, U), "ys": _sb(256, F), "olb": _sb(64, F),
+}
+for _t in range(R):
+    SCRATCH["qt%d" % _t] = _sb(256, Q)
+    SCRATCH["pt%d" % _t] = _sb(256, S)
+    SCRATCH["lq%d" % _t] = _sb(192, Q)
+    SCRATCH["ls%d" % _t] = _sb(384, S)
+    SCRATCH["mo%d" % _t] = _sb(2, U)
+    SCRATCH["mr%d" % _t] = _sb(2, U)
+    SCRATCH["ml%d" % _t] = _sb(16, U)
+SCRATCH["qt3"] = _sb(256, Q)
+SCRATCH["pt3"] = _sb(256, S)
+for _t in range(8):
+    SCRATCH["ps%d" % _t] = ("psum", [128, 512], F)
+SEMAPHORES = ["v", "a", "p", "gp", "dx", "du", "dv", "dwc", "dws", "out", "sent", "wp", "rw", "qo", "nbo", "yo",
+              "m0", "m1", "m2", "r0", "r1", "r2", "e0", "e1", "e2"]
+
+
+def bits(engines):
+    m = 0
+    for e in engines:
+        m |= 1 << e
+    return m
+
+
+def share(engines, n):
+    k = 1
+    while 2 * k * n <= len(engines):
+        k *= 2
+    sizes = [k] * n
+    left = len(engines) - k * n
+    for i in range(n):
+        if left >= k:
+            sizes[i] += k
+            left -= k
+    out, at = [], 0
+    for s in sizes:
+        out.append(engines[at:at + s])
+        at += s
+    return out
+
+
+def plan(r, t, cores, topo):
+    c = cores[r]
+    wd = cores[(r - HOP[2]) % N]
+    rel = [k for k in topo.cores_of(c) if k != c and topo.may_write(k, wd)]
+    near = [k for k in rel if topo.die(k) == topo.die(c)]
+    far = [k for k in rel if topo.die(k) != topo.die(c)]
+    up = [d for d in range(N) if d != r and (r < d or (t == 0 and r < (d - HOP[0]) % N))]
+    direct = [d for d in up if topo.may_write(c, cores[d])]
+    cross = [d for d in up if d not in direct]
+    off = topo.engines(c, cores[(r + HOP[0]) % N])
+    on = topo.engines(c, near[0])
+    use = near[:len(cross)]
+    first = list(zip(use, share(on, len(use)))) if use else []
+    dirs = list(zip(direct, share(off, len(direct)))) if direct else []
+    second = {}
+    for i, k in enumerate(use):
+        ds = cross[i::len(use)]
+        second[k] = list(zip(ds, share(topo.engines(k, cores[ds[0]]), len(ds))))
+    return {"wd": wd, "near": near, "far": far, "first": first, "dirs": dirs, "second": second, "off": off}
+
+
+def transfer(topo, src_core, dst_core, engines, sem, src, dst):
+    rid, pid = topo.addr(dst_core, src_core)
+    return RemoteDMATransfer(dst_ids=[DstId(rid=rid, pnc=pid)], dma_engine_mask=bits(engines), remote_sem=sem, src=src, dst=dst)
+
+
+def u8(ap):
+    return ap.bitcast(dt.uint8)
+
+
+def relay_program(g, core, T, topo, r):
+    cores = list(T.cores)
+    p = plan(r, 0, cores, topo)
+    sent = 0
+    half = len(topo.engines(cores[r], core)) // 2
+    if core in p["far"] or core in p["near"]:
+        eng = topo.engines(core, p["wd"])
+        g.wait_ge(T.sem.rw, half)
+        if core in p["far"]:
+            k = p["far"].index(core)
+            tr = transfer(topo, core, p["wd"], eng, T.sem.wp, u8(T.rq[:, 0:256]), u8(T.qp[:, 256 * k:256 * k + 256]))
+        else:
+            k = p["near"].index(core)
+            tr = transfer(topo, core, p["wd"], eng, T.sem.wp, T.rs[:, 0:256], T.sp[:, 256 * k:256 * k + 256])
+        g.remote_dma_fused([tr], local_sem=T.sem.sent)
+        sent += len(eng)
+    for t in range(R):
+        p = plan(r, t, cores, topo)
+        if core in p["second"]:
+            g.wait_ge(T.sem["r%d" % t], len(dict(p["first"])[core]))
+            trs = [transfer(topo, core, cores[d], e, T.sem["m%d" % t], T["mr%d" % t][:, 0:2], T["ml%d" % t][:, 2 * r:2 * r + 2])
+                   for d, e in p["second"][core]]
+            g.remote_dma_fused(trs, local_sem=T.sem.sent)
+            sent += sum(len(e) for d, e in p["second"][core])
+    if sent:
+        g.wait_ge(T.sem.sent, sent)
+
+
+def rank_program(g, core, T, topo):
+    r = T.rank_of(core)
+    cores = list(T.cores)
+    if r is None:
+        mates = [c for c in topo.cores_of(core) if c in cores]
+        if mates:
+            relay_program(g, core, T, topo, cores.index(mates[0]))
+        return
+    plans = [[plan(k, t, cores, topo) for k in range(N)] for t in range(R)]
+    me = plans[0][r]
+    qs = {"v": g.vector, "a": g.scalar, "p": g.tensor, "gp": g, "s": g.sync}
+    count = {"v": 0, "a": 0, "p": 0, "gp": 0}
+    clock = {k: {} for k in qs}
+    log = {}
+
+    def V(name, a, b, s=1):
+        return (name, a, b, s)
+
+    def ap(v):
+        if v[0] == "ind":
+            return ap(v[1]).indirect(ap(v[2]))
+        if v[3] == 1:
+            return T[v[0]][:, v[1]:v[2]]
+        return T[v[0]][:, v[1]:v[2]:v[3]]
+
+    def ind(win, off):
+        return ("ind", win, off)
+
+    def meets(x, y):
+        if x[2] <= y[1] or y[2] <= x[1]:
+            return False
+        return not (x[3] == y[3] and x[3] > 1 and (x[1] - y[1]) % x[3] != 0)
+
+    def wait(q, tok):
+        sem, val, known = tok
+        if clock[q].get(sem, 0) < val:
+            qs[q].wait_ge(T.sem[sem], val)
+            clock[q][sem] = val
+        for k, x in known.items():
+            if clock[q].get(k, 0) < x:
+                clock[q][k] = x
+
+    def before(q, outs, ins, after):
+        toks = list(after)
+        for v, w in [(o, True) for o in outs] + [(i, False) for i in ins]:
+            bank = v[0].startswith("ps")
+            for pv, pw, pq, tok in log.get(v[0], []):
+                if (bank and pq != q) or ((w or pw) and meets(v, pv)):
+                    toks.append(tok)
+        toks.sort(key=lambda t: -t[1])
+        for tok in toks:
+            wait(q, tok)
+
+    def note(q, outs, ins, tok):
+        for v, w in [(o, True) for o in outs] + [(i, False) for i in ins]:
+            log.setdefault(v[0], []).append((v, w, q, tok))
+
+    def flat(vs):
+        out = []
+        for v in vs:
+            if isinstance(v, tuple):
+                out += [v[1], v[2]] if v[0] == "ind" else [v]
+        return out
+
+    def op(q, call, outs, ins, after=()):
+        outs, ins = list(outs), flat(ins)
+        before(q, outs, ins, after)
+        count[q] += 1
+        call().then_inc(T.sem[q], 1)
+        tok = (q, count[q], dict(clock[q]))
+        note(q, outs, ins, tok)
+        return tok
+
+    def arg(x):
+        return ap(x) if isinstance(x, tuple) else x
+
+    def ts(o, i, s1, o0, s2=None, o1=None):
+        if o1 is None:
+            return op("v", lambda: g.vector.tensor_scalar(ap(o), ap(i), arg(s1), None, o0), [o], [i, s1])
+        return op("v", lambda: g.vector.tensor_scalar(ap(o), ap(i), arg(s1), arg(s2), o0, o1), [o], [i, s1, s2])
+
+    def tt(o, a, b, o0, after=()):
+        return op("v", lambda: g.vector.tensor_tensor(ap(o), ap(a), ap(b), o0), [o], [a, b], after)
+
+    def cp(o, i, after=()):
+        return op("v", lambda: g.vector.tensor_copy(ap(o), ap(i)), [o], [i], after)
+
+    def fill(o, c):
+        return op("v", lambda: g.vector.memset(ap(o), c), [o], [])
+
+    def scan(o, a, b, o0, o1):
+        return op("v", lambda: g.vector.tensor_tensor_scan(ap(o), ap(a), ap(b), 0.0, o0, o1), [o], [a, b])
+
+    def turn(o, i):
+        return op("v", lambda: g.vector.transpose(ap(o), ap(i)), [o], [i])
+
+    def quant(c, s, i):
+        return op("v", lambda: g.vector.quantize_mx(ap(c), ap(s), ap(i)), [c, s], [i])
+
+    def act(o, i, scale=None, bias=None, func=None):
+        if bias is not None:
+            return op("a", lambda: g.scalar.activation(ap(o), ap(i), func or ACT.Identity, bias=arg(bias), scale=arg(scale)), [o], [i, bias, scale])
+        if scale is not None:
+            return op("a", lambda: g.scalar.activation(ap(o), ap(i), ACT.Copy, scale=arg(scale)), [o], [i, scale])
+        return op("a", lambda: g.scalar.activation(ap(o), ap(i), func or ACT.Copy), [o], [i])
+
+    def mm(o, lc, ls, rc, rs, after=()):
+        return op("p", lambda: g.tensor.matmul_mx(ap(o), ap(lc), ap(ls), ap(rc), ap(rs), True, True), [o], [lc, ls, rc, rs], after)
+
+    def iota(o, pattern, mult, flag=True):
+        if flag:
+            return op("gp", lambda: g.iota(ap(o), pattern, 0, mult, allow_small_or_imprecise_dtypes=True), [o], [])
+        return op("gp", lambda: g.iota(ap(o), pattern, 0, mult), [o], [])
+
+    def load(q, sem, v, src, codes=False):
+        qs[q].dma_start(u8(ap(v)) if codes else ap(v), src).then_inc(T.sem[sem], 16)
+        note(q, [v], [], (sem, 16, {}))
+
+    stores = [0]
+
+    def store(q, dst, src_ap, v):
+        before(q, [], [v], ())
+        qs[q].dma_start(dst, src_ap).then_inc(T.sem.out, 16)
+        stores[0] += 16
+
+    sent = [0]
+
+    def send(trs, ins, engines):
+        before("gp", [], ins, ())
+        g.remote_dma_fused(trs, local_sem=T.sem.sent)
+        sent[0] += engines
+
+    load("a", "dws", V("sw", 0, 512), T.ws[:])
+    load("s", "dx", V("xn", 0, 1024), T.x[:])
+    load("a", "du", V("un", 0, 512), T.u[:])
+
+    iota(V("ci", 0, 1), [[0, 1]], 1, False)
+    iota(V("cj", 0, 1), [[0, 1]], 17, False)
+    iota(V("r256", 0, 256), [[1, 256]], 0)
+    E64, M8, I16, XP = V("io3", 0, 64), V("io3", 64, 128), V("io3", 128, 192), V("io3", 192, 256)
+    iota(E64, [[1, 4], [0, 16]], 0)
+    iota(M8, [[0, 8], [1, 8]], 0)
+    iota(I16, [[0, 4], [1, 16]], 0)
+
+    def col(name, k):
+        return V(name, k, k + 1)
+
+    def row(n):
+        return V("r256", 0, n)
+
+    for k, m in ((1, 15), (2, 16), (3, 3), (4, 7), (6, 9)):
+        ts(col("ci", k), col("ci", 0), m, A.bitwise_and)
+    ts(col("ci", 5), col("cj", 0), 16, A.bitwise_and)
+    fill(V("ez", 0, 520), 0.0)
+    cp(V("cf", 0, 7), V("ci", 0, 7))
+    fill(V("bt", 0, 288), 0.0)
+    P_, Qc, H16, Q4, Q7, PAR, Q9 = [col("cf", k) for k in range(7)]
+    Q16, WC, C4, RB, XB, GB, DB, Q0, LC, LM, RA, QH, Q15, CA, XA = [col("cc", k) for k in range(15)]
+    PERM, LA, RL, REP, REP15, GL, DUP, XL = (V("ku", 0, 16), V("ku", 16, 17), V("ku", 20, 24), V("ku", 24, 28),
+                                             V("ku", 28, 32), V("ku", 32, 33), V("ku", 40, 48), V("ku", 48, 112))
+    K = [V("k64", 64 * k, 64 * k + 64) for k in range(9)]
+    EM, KEEP8, DIAG, KEEP16, HK, NK, POW, FIX, DUMP = K
+    C16, GATE, Q64 = V("k64", 576, 592), V("k64", 592, 596), V("k64", 596, 597)
+    act(Q16, Qc, 16.0)
+    act(WC, Qc, 16.0, 16.0)
+    act(RA, Qc, 0.125)
+    act(V("x1", 256, 320), E64, 262144.0, 0.5)
+    act(RB, Q7, 7.875, RA)
+    act(KEEP8, M8, func=ACT.Sign)
+    act(V("ca", 64, 128), row(64), 0.0)
+    act(V("y2", 128, 136), row(8), 0.0)
+    act(V("y2", 136, 144, 2), row(4), 2.0)
+    act(V("y2", 137, 144, 2), row(4))
+    act(CA, Q7, 2.0, -47.0)
+    ts(V("ez", 3, 515, 4), row(128), P_, A.is_equal, 0.5, A.mult)
+    ts(PERM, row(16), Q16, A.add)
+    ts(LA, PAR, 17.0 / 16.0, A.mult, Qc, A.add)
+    for b in range(4):
+        quant(V("qe", 128 * b, 128 * b + 128), V("se", 128 * b, 128 * b + 128), V("ez", 3 - b, 515 - b))
+    fill(V("off1", 0, 32), 0)
+    ts(EM, M8, Q7, A.is_equal)
+    ts(DIAG, I16, Qc, A.is_equal)
+    ts(RL, row(4), 2.0, A.mult, RB, A.add)
+    ts(GATE, row(4), Q4, A.is_ge)
+    cp(REP, row(4))
+    QU, SU = V("qu", 0, 128), V("su", 0, 128)
+    QX, SX, Q0T, S0T = V("qx", 0, 256), V("sx", 0, 256), V("qt0", 0, 256), V("pt0", 0, 256)
+    quant(QX, SX, V("xn", 0, 1024))
+    op("v", lambda: g.vector.tensor_copy(ap(Q0T).bitcast(dt.uint32), ap(QX).bitcast(dt.uint32).indirect(ap(PERM))), [Q0T], [QX, PERM])
+    op("a", lambda: g.scalar.activation(ap(S0T), ap(SX).indirect(ap(PERM)), ACT.Copy), [S0T], [SX, PERM])
+    quant(QU, SU, V("un", 0, 512))
+    fill(V("ft", 256, 512), 0.0)
+    fill(V("ht", 256, 512), 0.0)
+    act(V("ex", 0, 16), row(16), 0.0)
+    act(V("ca", 64, 128, 16), row(4), -16.0, 48.0)
+    act(C4, Q4, 14.0, CA)
+    act(V("y3", 16, 32), row(16), 0.0)
+    act(KEEP16, I16, func=ACT.Sign)
+    act(Q15, Qc, 1.0, -14.0, ACT.Relu)
+    act(C16, row(16), 16.0)
+    act(XA, Q4, -15.0)
+    act(GB, Q4, 32.0, H16)
+    act(DB, Qc, 1.0, 656.0)
+    act(XB, Qc, 16.0, XA)
+    act(Q0, Qc, -1.0, 1.0, ACT.Relu)
+    act(HK, KEEP16, 0.5)
+    act(NK, KEEP16, -1.0, 1.0)
+    act(LC, Q15, 255.0, -255.0)
+    act(LM, Q15, -1000.0, 1255.0)
+    act(Q64, Qc, 1.0, 64.0)
+    act(DUMP, I16, 16.0, DB)
+    act(QH, Qc, 1.0, H16)
+    act(V("z", 0, 16), row(16), 16.0)
+    act(V("sc", 128, 256), row(128), 0.0)
+    act(V("wf", 256, 320), row(64), 0.0)
+
+    ahead, behind = cores[(r + HOP[0]) % N], cores[(r - HOP[0]) % N]
+    off = me["off"]
+    halves = share(off, 2)
+    on = topo.engines(core, me["near"][0])
+    two = share(on, 2)
+
+    def one(to, sem, src, dst, v):
+        send([transfer(topo, core, to, off, T.sem[sem], src, dst)], [v], len(off))
+
+    send([transfer(topo, core, k, two[i], T.sem.rw, T.sw[:, 256 * i:256 * i + 256], T.rs[:, 0:256]) for i, k in enumerate(me["near"])],
+         [V("sw", 0, 512)], len(on))
+    iota(XP, [[4, 16], [256, 4]], 0)
+    iota(V("jrow", 0, 256), [[1, 16], [16, 16]], 0)
+    one(ahead, "qo", u8(ap(Q0T)), u8(T.qo[:, 0:256]), Q0T)
+    one(ahead, "qo", ap(S0T), T.so[:, 0:256], S0T)
+    wait("s", ("qo", 2 * len(off), {}))
+    load("s", "dwc", V("qw", 0, 512), T.wc[:], codes=True)
+    load("s", "dv", V("vn", 0, 512), T.v[:])
+    src = plans[0][(r + HOP[2]) % N]
+    w_here = ("wp", sum(len(topo.engines(k, core)) for k in src["near"] + src["far"]), {})
+
+    def maps(t):
+        n = 0
+        for p in plans[t]:
+            n += sum(len(e) for d, e in p["dirs"] if d == r)
+            n += sum(len(e) for rel in p["second"].values() for d, e in rel if d == r)
+        return ("m%d" % t, n, {})
+
+    ES = [(V("qe", 128 * b, 128 * b + 128), V("se", 128 * b, 128 * b + 128)) for b in range(4)]
+
+    def exchange(m, a, to):
+        send([transfer(topo, core, to, halves[0], T.sem["e%d" % m], u8(T.qm[:, a:a + 64]), u8(T["lq%d" % m][:, 128:192])),
+              transfer(topo, core, to, halves[1], T.sem["e%d" % m], T.sm[:, a:a + 256], T["ls%d" % m][:, 128:384])],
+             [V("qm", a, a + 64), V("sm", a, a + 256)], len(off))
+        return V("lq%d" % m, 64, 192), V("ls%d" % m, 64, 192), ("e%d" % m, len(off), {})
+
+    L0, L1, L2 = V("la", 0, 16), V("la", 16, 32), V("la", 32, 48)
+    W0, BITS, LCN, TL, TS, TB, KP, D1 = [V("wf", 64 * k, 64 * k + 64) for k in range(8)]
+    YI, KI, AI, BI = [V("wi", 64 * k, 64 * k + 64) for k in range(4)]
+
+    def lasts(nb, after):
+        cp(V("la", 48, 64), V(nb, 0, 32, 2), after)
+        tt(L0, V("la", 48, 64), C16, A.add)
+        ts(L1, L0, 256.0, A.is_ge, LC, A.mult)
+        tt(L2, L0, L1, A.add)
+        ts(V("lu", 0, 16), L2, LM, A.min)
+        for b in range(4):
+            act(V("vl", 256 * b, 256 * b + 256), ind(V("vv", 256 * b, 256 * b + 256), V("lu", 0, 16)))
+
+    def lists(masks, starts, bodies, after=()):
+        tt(W0, ind(masks, REP), POW, A.mult, after)
+        ts(YI, W0, -0.5, A.add)
+        ts(BI, YI, 1, A.bitwise_and)
+        cp(BITS, BI)
+        scan(LCN, KEEP16, BITS, A.mult, A.add)
+        if starts:
+            ts(D1, BITS, -1024.0, A.mult)
+        turn(TL, LCN)
+        if starts:
+            tt(D1, D1, DUMP, A.add)
+        scan(V("wf", 257, 320), V("wf", 192, 255), V("k64", 193, 256), A.add, A.mult)
+        turn(TB, TS)
+        tt(KP, ind(TB, REP15), LCN, A.add)
+        ts(KI, KP, 63.0, A.add)
+        if starts:
+            ts(BI, KI, 496, A.bitwise_and)
+        if bodies:
+            ts(AI, KI, 63, A.bitwise_and)
+        if starts:
+            tt(W0, KI, BI, A.add)
+        if bodies:
+            tt(V("cand", 64, 128), AI, FIX, A.add)
+        if starts:
+            tt(V("cand", 0, 64), W0, D1, A.max)
+
+    def entry(t, upto, at):
+        def named(k):
+            return col("mo%d" % t, 0) if k == r else col("ml%d" % t, 2 * k)
+        if upto == 0:
+            return V("z", 0, 16)
+        wait("v", maps(t))
+        last = 0
+        for k in range(upto - 1, 0, -1):
+            cp(V("z", at, at + 16), ind(V("z", last, last + 16), named(k)))
+            last, at = at, at + 16
+        return ind(V("z", last, last + 16), named(0))
+
+    old, new = "ta", "tb"
+    for t in range(R):
+        QT, PT = V("qt%d" % t, 0, 256), V("pt%d" % t, 0, 256)
+        mm(V("ps0", 0, 256), QU, SU, QT, PT)
+        if t == 0:
+            QT, PT = V("qo", 0, 256), V("so", 0, 256)
+        for b in range(4):
+            mm(V("ps%d" % (b + 1), 0, 256), ES[b][0], ES[b][1], QT, PT, [("qo", 2 * len(off), {})] if t == 0 else [])
+        ts(V("bt", 16, 272), V("ps0", 0, 256), 0.0, A.is_gt, WC, A.mult)
+        turn(V("tt", 0, 256), V("bt", 16, 272))
+        turn(V("tt", 256, 544), V("bt", 0, 288))
+        for b in range(4):
+            act(V("vv", 256 * b, 256 * b + 256), V("ps%d" % (b + 1), 0, 256))
+        if t == R - 1:
+            act(V("tn", 0, 1024), ind(V(old, 0, 1024), XL))
+        tt(V("ga", 0, 34), V("tt", 0, 544, 16), V("tt", 1, 544, 16), A.add)
+        ts(V("off1", 0, 32, 2), ind(V("ga", 0, 34), LA), Qc, A.add)
+        if t == 0:
+            one(ahead, "nbo", T.off1[:, 0:32], T.nbo[:, 0:32], V("off1", 0, 32))
+        for i in range(15, -1, -1):
+            ts(V("x1", 16 * i, 16 * i + 16), ind(V("x1", 16 * i + 16, 16 * i + 80), col("off1", 2 * i)), float(2 ** i), A.add)
+        tt(V("wm", 0, 64), ind(V("x1", 0, 64), RL), EM, A.mult)
+        tt(V("ca", 0, 64), V("x1", 0, 64), DIAG, A.mult)
+        scan(V("wsn", 0, 64), KEEP8, V("wm", 0, 64), A.mult, A.add)
+        ts(V("off2", 0, 16, 2), V("wsn", 7, 64, 8), 2.0 ** -17, A.mult, Q9, A.add)
+        for b in range(7, -1, -1):
+            tt(V("y2", 16 * b, 16 * b + 16), ind(V("y2", 16 * b + 16, 16 * b + 32), col("off2", 2 * b)), V("ca", b, 128, 8), A.add)
+        scan(V("ex", 0, 4), V("y2", 8, 16, 2), GATE, A.max, A.mult)
+        cp(V("y3", 16, 24), V("y2", 0, 16, 2))
+        ts(col("off3", 0), col("ex", 3), C4, A.add)
+        tt(V("y3", 0, 16), ind(V("y2", 0, 16), col("off3", 0)), V("y3", 16, 32), A.add)
+        p = plans[t][r]
+        mo = T["mo%d" % t][:, 0:2]
+        if p["first"] or p["dirs"]:
+            scan(V("ex", 8, 12), V("y3", 4, 8), GATE, A.max, A.mult)
+            ts(V("mo%d" % t, 0, 2), V("ex", 11, 13), col("ex", 3), A.subtract)
+        if p["first"]:
+            send([transfer(topo, core, k, e, T.sem["r%d" % t], mo, T["mr%d" % t][:, 0:2]) for k, e in p["first"]],
+                 [V("mo%d" % t, 0, 2)], sum(len(e) for k, e in p["first"]))
+        if t == 0:
+            one(ahead, "yo", T.y3[:, 0:4], T.yo[:, 0:4], V("y3", 0, 4))
+        if p["dirs"]:
+            send([transfer(topo, core, cores[d], e, T.sem["m%d" % t], mo, T["ml%d" % t][:, 2 * r:2 * r + 2]) for d, e in p["dirs"]],
+                 [V("mo%d" % t, 0, 2)], sum(len(e) for k, e in p["dirs"]))
+        if t == 0:
+            send([transfer(topo, core, k, two[i], T.sem.rw, u8(T.qw[:, 256 * i:256 * i + 256]), u8(T.rq[:, 0:256]))
+                  for i, k in enumerate(me["far"])], [V("qw", 0, 512)], len(on))
+            lasts("nbo", [("nbo", len(off), {})])
+            tt(FIX, I16, E64, A.is_lt)
+            scan(POW, HK, NK, A.mult, A.add)
+            ts(REP15, row(4), 16.0, A.mult, 15.0, A.add)
+            ts(FIX, FIX, Q0, A.mult, H16, A.subtract)
+            cp(GL, GB)
+            ts(XL, XP, XB, A.add)
+            lists(V("y3", 0, 8), False, True)
+        else:
+            lasts("off1", ())
+            lists(V("y3", 0, 8), True, True)
+        if t == R - 1:
+            cp(V("ud", 0, 128), ind(V("cand", 0, 128), DUP))
+            turn(V("ut", 0, 128), V("ud", 0, 128))
+        for b in range(4):
+            tt(V("ff", 256 * b, 256 * b + 256), V("vl", 256 * b, 256 * b + 256), V("ps%d" % (b + 1), 0, 256), A.add)
+        if t == 0:
+            lists(V("yo", 0, 4), True, False, [("yo", len(off), {})])
+        e16 = entry(t, (r - HOP[0]) % N if t == 0 else r, 16)
+        ts(V("selo", 0, 16), e16, Qc, A.add)
+        ts(V("ll", 0, 16), ind(V("cand", 0, 64), V("selo", 0, 1)), H16, A.add)
+        op("v", lambda: g.vector.tensor_copy(ap(ind(V("sc", 0, 928), V("ll", 0, 16))), ap(row(256))),
+           [V("sc", 0, 928)], [V("ll", 0, 16), row(256)])
+        turn(V("st", 0, 128), V("sc", 128, 256))
+        cp(V("fl", 0, 16), ind(V("st", 0, 128), GL))
+        FL, UL = V("fl", 0, 4), V("ll", 16, 32)
+        for b in range(4):
+            (act if b % 2 else cp)(V("ft", b, 256, 4), ind(V("ff", 256 * b, 256 * b + 256), FL))
+        a = [384, 128, 512][t]
+        fc, fs = V("qm", a, a + 128), V("sm", a, a + 128)
+        quant(fc, fs, V("ft", 0, 512))
+        wc, ws, lo, after = "qp", "sp", 0, [w_here]
+        if t == 0:
+            wc, ws, after = "qw", "sw", []
+        if t == 1:
+            fc, fs, tok = exchange(1, a, ahead)
+            lo, after = 64, [tok, w_here]
+            for m in (1, 2):
+                quant(V("lq%d" % m, 0, 128), V("ls%d" % m, 0, 128), V("zt", 0, 512))
+            ts(V("selo", 16, 32), e16, Q64, A.add)
+            ts(UL, ind(V("cand", 0, 128), V("selo", 16, 17)), H16, A.add)
+        if t == R - 1:
+            UL = V("ln", 0, 16)
+            ts(V("selo", 16, 32), e16, 2.0, A.mult, QH, A.add)
+            ts(UL, ind(V("ut", 0, 128), V("selo", 16, 17)), H16, A.add)
+        for b in range(4):
+            mm(V("ps%d" % (b + 1), 0, 128), V(wc, 128 * b, 128 * b + 128), V(ws, 128 * b, 128 * b + 128), fc, fs, after)
+        for b in range(4):
+            ts(V("ht", b, 256, 4), V("ps%d" % (b + 1), lo, lo + 64), 0.03125, A.mult)
+        a = [256, 0, 640][t]
+        hc, hs = V("qm", a, a + 128), V("sm", a, a + 128)
+        quant(hc, hs, V("ht", 0, 512))
+        after, lo = [], 0
+        if t < 2:
+            hc, hs, tok = exchange(2 * t, a, behind)
+            after, lo = [tok], 64
+        if t == 0:
+            act(V(old, 0, 1024), ind(V("xn", 0, 1024), XL))
+            fill(V("zt", 0, 512), 0.0)
+            e16 = entry(t, r, 144)
+            quant(V("lq0", 0, 128), V("ls0", 0, 128), V("zt", 0, 512))
+            ts(V("selo", 16, 32), e16, Q64, A.add)
+            fill(V("dh", 0, 320), 0.0)
+            ts(UL, ind(V("cand", 0, 128), V("selo", 16, 17)), H16, A.add)
+        if t == 1:
+            quant(V("qv", 0, 128), V("sv", 0, 128), V("vn", 0, 512))
+            ts(V("ku", 40, 48, 2), row(4), 16.0, A.mult, Q64, A.add)
+            ts(V("ku", 41, 48, 2), row(4), 16.0, A.mult, Q64, A.add)
+        banks = ["ps5", "ps6", "ps7", "ps0"]
+        for b in range(4):
+            mm(V(banks[b], 0, 128), ES[b][0], ES[b][1], hc, hs, after)
+        ts(V("dh", 0, 64), V(banks[0], lo, lo + 64), 2.0, A.mult)
+        for b in range(1, 4):
+            act(V("dh", 80 * b, 80 * b + 64), V(banks[b], lo, lo + 64), 2.0)
+        if t == R - 1:
+            old = "tn"
+            act(V("olb", 0, 64), ind(V("jrow", 0, 256), FL))
+            store("s", T.ol[:], T.olb[0:128:16, 0:64], V("olb", 0, 64))
+        for b in range(4):
+            tt(V(new, b, 1024, 4), ind(V("dh", 80 * b, 80 * b + 80), UL), V(old, b, 1024, 4), A.add)
+        quant(V("qt%d" % (t + 1), 0, 256), V("pt%d" % (t + 1), 0, 256), V(new, 0, 1024))
+        old, new = new, "ta" if new == "tb" else "tb"
+
+    QN, SN = V("qt3", 0, 256), V("pt3", 0, 256)
+    mm(V("ps1", 0, 256), V("qv", 0, 128), V("sv", 0, 128), QN, SN)
+    store("s", T.oc[:], u8(ap(QN)), QN)
+    for k in range(4):
+        store("a", T.osc[4 * k:4 * k + 4, 0:256], T.pt3[32 * k:32 * k + 4, 0:256], SN)
+    cp(V("ys", 0, 256), V("ps1", 0, 256))
+    store("s", T.y[:], T.ys[:, 0:256], V("ys", 0, 256))
+    for q in ("v", "a", "p", "gp"):
+        g.wait_ge(T.sem[q], count[q])
+    g.wait_ge(T.sem.sent, sent[0])
+    g.wait_ge(T.sem.out, stores[0])

@@ -17,13 +17,15 @@ SCRATCH = {
     "qo": _sb(256, Q), "so": _sb(256, S), "qw": _sb(512, Q), "sw": _sb(512, S), "qp": _sb(512, Q), "sp": _sb(512, S),
     "rq": _sb(256, Q), "rs": _sb(256, S), "ez": _sb(520, BF), "qe": _sb(512, Q), "se": _sb(512, S),
     "qm": _sb(768, Q), "sm": _sb(768, S), "zt": _sb(512, BF), "ft": _sb(512, BF), "ht": _sb(512, BF),
-    "ci": _sb(8, I), "cj": _sb(2, I), "cf": _sb(8, F), "cc": _sb(16, F), "ku": _sb(112, U), "r256": _sb(256, F), "jrow": _sb(256, F),
-    "io3": _sb(256, F), "k64": _sb(640, F), "bt": _sb(288, BF), "tt": _sb(544, BF), "ga": _sb(40, F),
-    "nbo": _sb(32, U), "yo": _sb(8, F),
-    "off1": _sb(32, U), "x1": _sb(320, F), "wm": _sb(64, F), "wsn": _sb(64, F), "off2": _sb(32, U), "ca": _sb(128, F),
+    "ci": _sb(8, I), "cj": _sb(2, I), "cf": _sb(8, F), "cc": _sb(24, F), "ku": _sb(128, U), "r256": _sb(256, F), "jrow": _sb(256, F),
+    "io3": _sb(288, F), "k64": _sb(640, F), "bt": _sb(288, BF), "tt": _sb(544, BF), "ga": _sb(40, F), "gq": _sb(16, F),
+    "nbo": _sb(32, U), "yo": _sb(8, F), "offq": _sb(16, U), "offw": _sb(16, U), "xe": _sb(528, BF), "xm": _sb(512, F),
+    "xr": _sb(256, F), "xs": _sb(128, F), "pw": _sb(256, F),
+    "off1": _sb(32, U), "x1": _sb(64, F), "wm": _sb(64, F), "wsn": _sb(64, F), "off2": _sb(32, U), "ca": _sb(128, F),
     "y2": _sb(144, F), "y3": _sb(32, F), "off3": _sb(2, U), "ex": _sb(16, F), "z": _sb(272, F), "la": _sb(64, F), "lu": _sb(16, U),
-    "wf": _sb(512, F), "wi": _sb(256, I), "cand": _sb(128, F), "selo": _sb(32, U), "ll": _sb(32, U), "sc": _sb(928, F),
-    "st": _sb(128, F), "fl": _sb(16, U), "vv": _sb(1024, BF), "vl": _sb(1024, BF), "ff": _sb(1024, BF), "dh": _sb(320, BF),
+    "wf": _sb(512, F), "wi": _sb(256, I), "wg": _sb(512, F), "wj": _sb(256, I), "eu": _sb(16, U), "zb": _sb(80, F),
+    "cand": _sb(128, F), "selo": _sb(32, U), "ll": _sb(32, U), "sc": _sb(576, F),
+    "st": _sb(160, F), "fl": _sb(16, U), "vv": _sb(1024, BF), "vl": _sb(1024, BF), "ff": _sb(1024, BF), "dh": _sb(320, BF),
     "ud": _sb(128, F), "ut": _sb(128, F), "ln": _sb(16, U), "ys": _sb(256, F), "olb": _sb(64, F),
 }
 for _t in range(R):
@@ -264,9 +266,11 @@ def rank_program(g, core, T, topo):
     iota(V("cj", 0, 1), [[0, 1]], 17, False)
     iota(V("r256", 0, 256), [[1, 256]], 0)
     E64, M8, I16, XP = V("io3", 0, 64), V("io3", 64, 128), V("io3", 128, 192), V("io3", 192, 256)
-    iota(E64, [[1, 4], [0, 16]], 0)
+    A16, RP = V("io3", 256, 272), V("io3", 272, 288)
     iota(M8, [[0, 8], [1, 8]], 0)
     iota(I16, [[0, 4], [1, 16]], 0)
+    iota(A16, [[0, 4], [16, 4]], 0)
+    iota(RP, [[16, 4], [64, 4]], 0)
 
     def col(name, k):
         return V(name, k, k + 1)
@@ -274,30 +278,36 @@ def rank_program(g, core, T, topo):
     def row(n):
         return V("r256", 0, n)
 
-    for k, m in ((1, 15), (2, 16), (3, 3), (4, 7), (6, 9)):
+    for k, m in ((1, 15), (2, 16), (3, 3), (4, 7), (6, 9), (7, 20)):
         ts(col("ci", k), col("ci", 0), m, A.bitwise_and)
     ts(col("ci", 5), col("cj", 0), 16, A.bitwise_and)
     fill(V("ez", 0, 520), 0.0)
-    cp(V("cf", 0, 7), V("ci", 0, 7))
+    cp(V("cf", 0, 8), V("ci", 0, 8))
     fill(V("bt", 0, 288), 0.0)
-    P_, Qc, H16, Q4, Q7, PAR, Q9 = [col("cf", k) for k in range(7)]
-    Q16, WC, C4, RB, XB, GB, DB, Q0, LC, LM, RA, QH, Q15, CA, XA = [col("cc", k) for k in range(15)]
-    PERM, LA, RL, REP, REP15, GL, DUP, XL = (V("ku", 0, 16), V("ku", 16, 17), V("ku", 20, 24), V("ku", 24, 28),
-                                             V("ku", 28, 32), V("ku", 32, 33), V("ku", 40, 48), V("ku", 48, 112))
+    P_, Qc, H16, Q4, Q7, PAR, Q9, Q20 = [col("cf", k) for k in range(8)]
+    Q16, WC, C4, RB, XB, GB, DB, Q0, LC, LM, RA, QH, Q15, CA, XA, GA, PA, PB, PC, PD = [col("cc", k) for k in range(20)]
+    PERM, LA, LQ, RL, REP, REP15, GL, LW, DUP, XL, RO = (
+        V("ku", 0, 16), V("ku", 16, 17), V("ku", 18, 19), V("ku", 20, 24), V("ku", 24, 28), V("ku", 28, 32), V("ku", 32, 33),
+        V("ku", 34, 35), V("ku", 40, 48), V("ku", 48, 112), V("ku", 112, 128))
     K = [V("k64", 64 * k, 64 * k + 64) for k in range(9)]
     EM, KEEP8, DIAG, KEEP16, HK, NK, POW, FIX, DUMP = K
     C16, GATE, Q64 = V("k64", 576, 592), V("k64", 592, 596), V("k64", 596, 597)
     act(Q16, Qc, 16.0)
-    act(WC, Qc, 16.0, 16.0)
+    act(PA, Q20, 1.0, -10.0, ACT.Abs)
+    act(PB, Qc, 0.25)
+    act(WC, Qc, 64.0, 64.0)
     act(RA, Qc, 0.125)
-    act(V("x1", 256, 320), E64, 262144.0, 0.5)
+    act(PC, Q4, 3.75, PB)
+    act(V("xm", 256, 512), row(256), 0.0)
+    act(PD, PA, -4.25, PC)
     act(RB, Q7, 7.875, RA)
-    act(KEEP8, M8, func=ACT.Sign)
-    act(V("ca", 64, 128), row(64), 0.0)
-    act(V("y2", 128, 136), row(8), 0.0)
-    act(V("y2", 136, 144, 2), row(4), 2.0)
-    act(V("y2", 137, 144, 2), row(4))
-    act(CA, Q7, 2.0, -47.0)
+    act(V("xe", 0, 16), row(16), 0.0)
+    for e in range(4):
+        act(V("xe", 272 + 64 * e, 336 + 64 * e), row(64), 0.0, 16.0 * e)
+        act(V("xm", 304 + 64 * e, 320 + 64 * e), row(16), 0.0, 262144.0 * e + 0.5)
+        act(V("pw", 16 * e, 16 * e + 16), row(16), 0.0, 16.0 ** e)
+    for j in range(1, 4):
+        act(V("pw", 64 * j, 64 * j + 64), V("pw", 0, 64), 2.0 ** j)
     ts(V("ez", 3, 515, 4), row(128), P_, A.is_equal, 0.5, A.mult)
     ts(PERM, row(16), Q16, A.add)
     ts(LA, PAR, 17.0 / 16.0, A.mult, Qc, A.add)
@@ -306,8 +316,11 @@ def rank_program(g, core, T, topo):
     fill(V("off1", 0, 32), 0)
     ts(EM, M8, Q7, A.is_equal)
     ts(DIAG, I16, Qc, A.is_equal)
+    ts(LQ, PD, 42.5, A.add)
+    ts(LW, PD, 42.5, A.add, 16.0, A.mult)
     ts(RL, row(4), 2.0, A.mult, RB, A.add)
     ts(GATE, row(4), Q4, A.is_ge)
+    ts(RO, RP, Qc, A.add)
     cp(REP, row(4))
     QU, SU = V("qu", 0, 128), V("su", 0, 128)
     QX, SX, Q0T, S0T = V("qx", 0, 256), V("sx", 0, 256), V("qt0", 0, 256), V("pt0", 0, 256)
@@ -317,28 +330,36 @@ def rank_program(g, core, T, topo):
     quant(QU, SU, V("un", 0, 512))
     fill(V("ft", 256, 512), 0.0)
     fill(V("ht", 256, 512), 0.0)
-    act(V("ex", 0, 16), row(16), 0.0)
-    act(V("ca", 64, 128, 16), row(4), -16.0, 48.0)
-    act(C4, Q4, 14.0, CA)
-    act(V("y3", 16, 32), row(16), 0.0)
+    act(KEEP8, M8, func=ACT.Sign)
+    act(V("ca", 64, 128), row(64), 0.0)
+    act(V("y2", 128, 136), row(8), 0.0)
+    act(V("y2", 136, 144, 2), row(4), 2.0)
+    act(V("y2", 137, 144, 2), row(4))
     act(KEEP16, I16, func=ACT.Sign)
-    act(Q15, Qc, 1.0, -14.0, ACT.Relu)
-    act(C16, row(16), 16.0)
     act(XA, Q4, -15.0)
-    act(GB, Q4, 32.0, H16)
-    act(DB, Qc, 1.0, 656.0)
-    act(XB, Qc, 16.0, XA)
+    act(GA, PAR, 5.0)
+    act(CA, Q7, 2.0, -47.0)
     act(Q0, Qc, -1.0, 1.0, ACT.Relu)
     act(HK, KEEP16, 0.5)
     act(NK, KEEP16, -1.0, 1.0)
+    act(XB, Qc, 16.0, XA)
+    act(GB, Q4, 16.0, GA)
+    act(V("ca", 64, 128, 16), row(4), -16.0, 48.0)
+    act(C4, Q4, 14.0, CA)
+    act(V("ex", 0, 16), row(16), 0.0)
+    act(V("y3", 16, 32), row(16), 0.0)
+    act(Q15, Qc, 1.0, -14.0, ACT.Relu)
+    act(DB, Qc, 1.0, 320.0)
+    act(C16, row(16), 16.0)
+    act(Q64, Qc, 1.0, 64.0)
     act(LC, Q15, 255.0, -255.0)
     act(LM, Q15, -1000.0, 1255.0)
-    act(Q64, Qc, 1.0, 64.0)
     act(DUMP, I16, 16.0, DB)
     act(QH, Qc, 1.0, H16)
     act(V("z", 0, 16), row(16), 16.0)
-    act(V("sc", 128, 256), row(128), 0.0)
+    act(V("sc", 48, 144), row(96), 0.0)
     act(V("wf", 256, 320), row(64), 0.0)
+    act(V("wg", 256, 320), row(64), 0.0)
 
     ahead, behind = cores[(r + HOP[0]) % N], cores[(r - HOP[0]) % N]
     off = me["off"]
@@ -351,8 +372,8 @@ def rank_program(g, core, T, topo):
 
     send([transfer(topo, core, k, two[i], T.sem.rw, T.sw[:, 256 * i:256 * i + 256], T.rs[:, 0:256]) for i, k in enumerate(me["near"])],
          [V("sw", 0, 512)], len(on))
+    iota(E64, [[1, 4], [0, 16]], 0)
     iota(XP, [[4, 16], [256, 4]], 0)
-    iota(V("jrow", 0, 256), [[1, 16], [16, 16]], 0)
     one(ahead, "qo", u8(ap(Q0T)), u8(T.qo[:, 0:256]), Q0T)
     one(ahead, "qo", ap(S0T), T.so[:, 0:256], S0T)
     wait("s", ("qo", 2 * len(off), {}))
@@ -376,56 +397,67 @@ def rank_program(g, core, T, topo):
              [V("qm", a, a + 64), V("sm", a, a + 256)], len(off))
         return V("lq%d" % m, 64, 192), V("ls%d" % m, 64, 192), ("e%d" % m, len(off), {})
 
-    L0, L1, L2 = V("la", 0, 16), V("la", 16, 32), V("la", 32, 48)
-    W0, BITS, LCN, TL, TS, TB, KP, D1 = [V("wf", 64 * k, 64 * k + 64) for k in range(8)]
-    YI, KI, AI, BI = [V("wi", 64 * k, 64 * k + 64) for k in range(4)]
+    def weave(*chains):
+        for k in range(max(len(c) for c in chains)):
+            for c in chains:
+                if k < len(c):
+                    c[k]()
 
     def lasts(nb, after):
-        cp(V("la", 48, 64), V(nb, 0, 32, 2), after)
-        tt(L0, V("la", 48, 64), C16, A.add)
-        ts(L1, L0, 256.0, A.is_ge, LC, A.mult)
-        tt(L2, L0, L1, A.add)
-        ts(V("lu", 0, 16), L2, LM, A.min)
-        for b in range(4):
-            act(V("vl", 256 * b, 256 * b + 256), ind(V("vv", 256 * b, 256 * b + 256), V("lu", 0, 16)))
+        L0, L1, L2, L3 = [V("la", 16 * k, 16 * k + 16) for k in range(4)]
 
-    def lists(masks, starts, bodies, after=()):
-        tt(W0, ind(masks, REP), POW, A.mult, after)
-        ts(YI, W0, -0.5, A.add)
-        ts(BI, YI, 1, A.bitwise_and)
-        cp(BITS, BI)
-        scan(LCN, KEEP16, BITS, A.mult, A.add)
+        def fetch():
+            ts(V("lu", 0, 16), L2, LM, A.min)
+            for b in range(4):
+                act(V("vl", 256 * b, 256 * b + 256), ind(V("vv", 256 * b, 256 * b + 256), V("lu", 0, 16)))
+        return [lambda: cp(L3, V(nb, 0, 32, 2), after), lambda: tt(L0, L3, C16, A.add), lambda: ts(L1, L0, 256.0, A.is_ge, LC, A.mult),
+                lambda: tt(L2, L0, L1, A.add), fetch]
+
+    def lists(masks, starts, bodies, wf, wi, after=()):
+        W0, BITS, LCN, TL, TS, TB, LP, D1 = [V(wf, 64 * k, 64 * k + 64) for k in range(8)]
+        YI, KI, AI, BI = [V(wi, 64 * k, 64 * k + 64) for k in range(4)]
+        c = [lambda: tt(W0, ind(masks, REP), POW, A.mult, after), lambda: ts(YI, W0, -0.5, A.add), lambda: ts(BI, YI, 1, A.bitwise_and),
+             lambda: cp(BITS, BI), lambda: scan(LCN, KEEP16, BITS, A.mult, A.add)]
         if starts:
-            ts(D1, BITS, -1024.0, A.mult)
-        turn(TL, LCN)
+            c += [lambda: ts(D1, BITS, -1024.0, A.mult)]
+        c += [lambda: turn(TL, LCN), lambda: ts(LP, LCN, 63.0, A.add),
+              lambda: scan(V(wf, 257, 320), V(wf, 192, 255), V("k64", 193, 256), A.add, A.mult)]
         if starts:
-            tt(D1, D1, DUMP, A.add)
-        scan(V("wf", 257, 320), V("wf", 192, 255), V("k64", 193, 256), A.add, A.mult)
-        turn(TB, TS)
-        tt(KP, ind(TB, REP15), LCN, A.add)
-        ts(KI, KP, 63.0, A.add)
+            c += [lambda: tt(D1, D1, DUMP, A.add)]
+        c += [lambda: turn(TB, TS), lambda: tt(KI, ind(TB, REP15), LP, A.add)]
         if starts:
-            ts(BI, KI, 496, A.bitwise_and)
+            c += [lambda: tt(V("cand", 0, 64), KI, D1, A.max)]
         if bodies:
-            ts(AI, KI, 63, A.bitwise_and)
-        if starts:
-            tt(W0, KI, BI, A.add)
-        if bodies:
-            tt(V("cand", 64, 128), AI, FIX, A.add)
-        if starts:
-            tt(V("cand", 0, 64), W0, D1, A.max)
+            c += [lambda: ts(AI, KI, 63, A.bitwise_and), lambda: tt(V("cand", 64, 128), AI, FIX, A.add)]
+        return c
+
+    def sums():
+        return [lambda b=b: tt(V("ff", 256 * b, 256 * b + 256), V("vl", 256 * b, 256 * b + 256), V("ps%d" % (b + 1), 0, 256), A.add)
+                for b in range(4)]
 
     def entry(t, upto, at):
         def named(k):
             return col("mo%d" % t, 0) if k == r else col("ml%d" % t, 2 * k)
+
+        def chain(ks, first, name, at):
+            out, last = [], first
+            for k in ks:
+                o = V(name, at, at + 16)
+                out.append(lambda o=o, last=last, k=k: cp(o, ind(last, named(k))))
+                last, at = o, at + 16
+            return out, last
         if upto == 0:
             return V("z", 0, 16)
         wait("v", maps(t))
-        last = 0
-        for k in range(upto - 1, 0, -1):
-            cp(V("z", at, at + 16), ind(V("z", last, last + 16), named(k)))
-            last, at = at, at + 16
-        return ind(V("z", last, last + 16), named(0))
+        if upto < 4:
+            c, last = chain(range(upto - 1, 0, -1), V("z", 0, 16), "z", at)
+            weave(c)
+            return ind(last, named(0))
+        low = upto // 2
+        a, last = chain(range(upto - 1, low - 1, -1), V("z", 0, 16), "z", at)
+        b, lb = chain(range(low - 1, 0, -1), row(16), "zb", 0)
+        weave(a, b + [lambda: cp(V("eu", 0, 16), ind(lb, named(0)))])
+        return ind(last, col("eu", 0))
 
     old, new = "ta", "tb"
     for t in range(R):
@@ -440,24 +472,42 @@ def rank_program(g, core, T, topo):
         turn(V("tt", 256, 544), V("bt", 0, 288))
         for b in range(4):
             act(V("vv", 256 * b, 256 * b + 256), V("ps%d" % (b + 1), 0, 256))
-        if t == R - 1:
-            act(V("tn", 0, 1024), ind(V(old, 0, 1024), XL))
         tt(V("ga", 0, 34), V("tt", 0, 544, 16), V("tt", 1, 544, 16), A.add)
-        ts(V("off1", 0, 32, 2), ind(V("ga", 0, 34), LA), Qc, A.add)
+        tt(V("gq", 0, 16), ind(V("ga", 0, 34), LQ), A16, A.add)
+        ts(V("off1", 0, 32, 2), ind(V("ga", 0, 34), LA), 0.25, A.mult, Qc, A.add)
+        ts(V("offq", 0, 16), V("gq", 0, 16), Qc, A.add)
         if t == 0:
             one(ahead, "nbo", T.off1[:, 0:32], T.nbo[:, 0:32], V("off1", 0, 32))
-        for i in range(15, -1, -1):
-            ts(V("x1", 16 * i, 16 * i + 16), ind(V("x1", 16 * i + 16, 16 * i + 80), col("off1", 2 * i)), float(2 ** i), A.add)
-        tt(V("wm", 0, 64), ind(V("x1", 0, 64), RL), EM, A.mult)
+            iota(V("jrow", 0, 256), [[1, 16], [16, 16]], 0)
+        for j in range(3, -1, -1):
+            o = V("offq", 4 * j, 4 * j + 4)
+            cp(V("xe", 16 + 64 * j, 80 + 64 * j), ind(V("xe", 80 + 64 * j, 336 + 64 * j), o))
+            tt(V("xm", 64 * j, 64 * j + 64), ind(V("xm", 64 * j + 64, 64 * j + 320), o), V("pw", 64 * j, 64 * j + 64), A.add)
+        turn(V("tt", 0, 256), V("xe", 16, 272))
+        turn(V("tt", 256, 544), V("xe", 0, 288))
+        cp(V("xr", 0, 256), ind(V("xm", 0, 256), RO))
+        side = lasts("off1", ())
+        if t == 0:
+            side = [lambda: tt(FIX, I16, E64, A.is_lt), lambda: scan(POW, HK, NK, A.mult, A.add), lambda: cp(GL, GB),
+                    lambda: ts(REP15, row(4), 16.0, A.mult, 15.0, A.add), lambda: ts(FIX, FIX, Q0, A.mult), lambda: ts(XL, XP, XB, A.add)]
+        weave([lambda: ts(V("offw", 0, 16), ind(V("tt", 0, 544), LW), Qc, A.add),
+               lambda: tt(V("xs", 0, 64), ind(V("xr", 192, 256), V("offw", 8, 12)), V("xr", 128, 192), A.add),
+               lambda: tt(V("xs", 64, 128), ind(V("xs", 0, 64), V("offw", 4, 8)), V("xr", 64, 128), A.add),
+               lambda: tt(V("x1", 0, 64), ind(V("xs", 64, 128), V("offw", 0, 4)), V("xr", 0, 64), A.add),
+               lambda: tt(V("wm", 0, 64), ind(V("x1", 0, 64), RL), EM, A.mult)], side[:4])
         tt(V("ca", 0, 64), V("x1", 0, 64), DIAG, A.mult)
-        scan(V("wsn", 0, 64), KEEP8, V("wm", 0, 64), A.mult, A.add)
-        ts(V("off2", 0, 16, 2), V("wsn", 7, 64, 8), 2.0 ** -17, A.mult, Q9, A.add)
+        weave([lambda: scan(V("wsn", 0, 64), KEEP8, V("wm", 0, 64), A.mult, A.add),
+               lambda: ts(V("off2", 0, 16, 2), V("wsn", 7, 64, 8), 2.0 ** -17, A.mult, Q9, A.add)], side[4:])
+        if t == R - 1:
+            act(V("tn", 0, 1024), ind(V(old, 0, 1024), XL))
         for b in range(7, -1, -1):
             tt(V("y2", 16 * b, 16 * b + 16), ind(V("y2", 16 * b + 16, 16 * b + 32), col("off2", 2 * b)), V("ca", b, 128, 8), A.add)
         scan(V("ex", 0, 4), V("y2", 8, 16, 2), GATE, A.max, A.mult)
         cp(V("y3", 16, 24), V("y2", 0, 16, 2))
         ts(col("off3", 0), col("ex", 3), C4, A.add)
         tt(V("y3", 0, 16), ind(V("y2", 0, 16), col("off3", 0)), V("y3", 16, 32), A.add)
+        if t == 0:
+            one(ahead, "yo", T.y3[:, 0:4], T.yo[:, 0:4], V("y3", 0, 4))
         p = plans[t][r]
         mo = T["mo%d" % t][:, 0:2]
         if p["first"] or p["dirs"]:
@@ -466,42 +516,36 @@ def rank_program(g, core, T, topo):
         if p["first"]:
             send([transfer(topo, core, k, e, T.sem["r%d" % t], mo, T["mr%d" % t][:, 0:2]) for k, e in p["first"]],
                  [V("mo%d" % t, 0, 2)], sum(len(e) for k, e in p["first"]))
-        if t == 0:
-            one(ahead, "yo", T.y3[:, 0:4], T.yo[:, 0:4], V("y3", 0, 4))
         if p["dirs"]:
             send([transfer(topo, core, cores[d], e, T.sem["m%d" % t], mo, T["ml%d" % t][:, 2 * r:2 * r + 2]) for d, e in p["dirs"]],
                  [V("mo%d" % t, 0, 2)], sum(len(e) for k, e in p["dirs"]))
         if t == 0:
             send([transfer(topo, core, k, two[i], T.sem.rw, u8(T.qw[:, 256 * i:256 * i + 256]), u8(T.rq[:, 0:256]))
                   for i, k in enumerate(me["far"])], [V("qw", 0, 512)], len(on))
-            lasts("nbo", [("nbo", len(off), {})])
-            tt(FIX, I16, E64, A.is_lt)
-            scan(POW, HK, NK, A.mult, A.add)
-            ts(REP15, row(4), 16.0, A.mult, 15.0, A.add)
-            ts(FIX, FIX, Q0, A.mult, H16, A.subtract)
-            cp(GL, GB)
-            ts(XL, XP, XB, A.add)
-            lists(V("y3", 0, 8), False, True)
+            own = lists(V("y3", 0, 8), False, True, "wf", "wi")
+            weave(lasts("nbo", [("nbo", len(off), {})]), own[:8])
+            weave(lists(V("yo", 0, 4), True, False, "wg", "wj", [("yo", len(off), {})]), own[8:] + sums())
         else:
-            lasts("off1", ())
-            lists(V("y3", 0, 8), True, True)
+            weave(lists(V("y3", 0, 8), True, True, "wf", "wi"), sums())
         if t == R - 1:
             cp(V("ud", 0, 128), ind(V("cand", 0, 128), DUP))
             turn(V("ut", 0, 128), V("ud", 0, 128))
-        for b in range(4):
-            tt(V("ff", 256 * b, 256 * b + 256), V("vl", 256 * b, 256 * b + 256), V("ps%d" % (b + 1), 0, 256), A.add)
-        if t == 0:
-            lists(V("yo", 0, 4), True, False, [("yo", len(off), {})])
         e16 = entry(t, (r - HOP[0]) % N if t == 0 else r, 16)
         ts(V("selo", 0, 16), e16, Qc, A.add)
-        ts(V("ll", 0, 16), ind(V("cand", 0, 64), V("selo", 0, 1)), H16, A.add)
-        op("v", lambda: g.vector.tensor_copy(ap(ind(V("sc", 0, 928), V("ll", 0, 16))), ap(row(256))),
-           [V("sc", 0, 928)], [V("ll", 0, 16), row(256)])
-        turn(V("st", 0, 128), V("sc", 128, 256))
-        cp(V("fl", 0, 16), ind(V("st", 0, 128), GL))
+        cp(V("ll", 0, 16), ind(V("cand", 0, 64), V("selo", 0, 1)))
+        op("v", lambda: g.vector.tensor_copy(ap(ind(V("sc", 0, 576), V("ll", 0, 16))), ap(row(256))),
+           [V("sc", 0, 576)], [V("ll", 0, 16), row(256)])
         FL, UL = V("fl", 0, 4), V("ll", 16, 32)
+        if t == R - 1:
+            UL = V("ln", 0, 16)
+            ts(V("selo", 16, 32), e16, 2.0, A.mult, QH, A.add)
+        turn(V("st", 0, 64), V("sc", 64, 128))
+        turn(V("st", 64, 160), V("sc", 48, 144))
+        if t == R - 1:
+            cp(UL, ind(V("ut", 0, 128), V("selo", 16, 17)))
+        cp(V("fl", 0, 16), ind(V("st", 0, 160), GL))
         for b in range(4):
-            (act if b % 2 else cp)(V("ft", b, 256, 4), ind(V("ff", 256 * b, 256 * b + 256), FL))
+            (act if b == 3 else cp)(V("ft", b, 256, 4), ind(V("ff", 256 * b, 256 * b + 256), FL))
         a = [384, 128, 512][t]
         fc, fs = V("qm", a, a + 128), V("sm", a, a + 128)
         quant(fc, fs, V("ft", 0, 512))
@@ -514,11 +558,7 @@ def rank_program(g, core, T, topo):
             for m in (1, 2):
                 quant(V("lq%d" % m, 0, 128), V("ls%d" % m, 0, 128), V("zt", 0, 512))
             ts(V("selo", 16, 32), e16, Q64, A.add)
-            ts(UL, ind(V("cand", 0, 128), V("selo", 16, 17)), H16, A.add)
-        if t == R - 1:
-            UL = V("ln", 0, 16)
-            ts(V("selo", 16, 32), e16, 2.0, A.mult, QH, A.add)
-            ts(UL, ind(V("ut", 0, 128), V("selo", 16, 17)), H16, A.add)
+            cp(UL, ind(V("cand", 0, 128), V("selo", 16, 17)))
         for b in range(4):
             mm(V("ps%d" % (b + 1), 0, 128), V(wc, 128 * b, 128 * b + 128), V(ws, 128 * b, 128 * b + 128), fc, fs, after)
         for b in range(4):
@@ -537,7 +577,7 @@ def rank_program(g, core, T, topo):
             quant(V("lq0", 0, 128), V("ls0", 0, 128), V("zt", 0, 512))
             ts(V("selo", 16, 32), e16, Q64, A.add)
             fill(V("dh", 0, 320), 0.0)
-            ts(UL, ind(V("cand", 0, 128), V("selo", 16, 17)), H16, A.add)
+            cp(UL, ind(V("cand", 0, 128), V("selo", 16, 17)))
         if t == 1:
             quant(V("qv", 0, 128), V("sv", 0, 128), V("vn", 0, 512))
             ts(V("ku", 40, 48, 2), row(4), 16.0, A.mult, Q64, A.add)

@@ -18,11 +18,12 @@ SCRATCH = {
     "rq": _sb(256, Q), "rs": _sb(256, S), "ez": _sb(520, BF), "qe": _sb(512, Q), "se": _sb(512, S),
     "qm": _sb(768, Q), "sm": _sb(768, S), "zt": _sb(512, BF), "ft": _sb(512, BF), "ht": _sb(512, BF),
     "ci": _sb(8, I), "cj": _sb(2, I), "cf": _sb(8, F), "cc": _sb(24, F), "ku": _sb(128, U), "r256": _sb(256, F), "jrow": _sb(256, F),
-    "io3": _sb(288, F), "k64": _sb(640, F), "bt": _sb(288, BF), "tt": _sb(544, BF), "ga": _sb(40, F), "gq": _sb(16, F),
-    "nbo": _sb(32, U), "yo": _sb(8, F), "offq": _sb(16, U), "offw": _sb(16, U), "xe": _sb(528, BF), "xm": _sb(512, F),
+    "io3": _sb(288, F), "k64": _sb(672, F), "bt": _sb(288, BF), "tt": _sb(544, BF), "ga": _sb(40, F), "gq": _sb(16, F),
+    "nbo": _sb(32, U), "yo": _sb(16, F), "offq": _sb(16, U), "offw": _sb(16, U), "xe": _sb(528, BF), "xm": _sb(512, F),
     "xr": _sb(256, F), "xs": _sb(128, F), "pw": _sb(256, F),
-    "off1": _sb(32, U), "x1": _sb(64, F), "wm": _sb(64, F), "wsn": _sb(64, F), "off2": _sb(32, U), "ca": _sb(128, F),
-    "y2": _sb(144, F), "y3": _sb(32, F), "off3": _sb(2, U), "ex": _sb(16, F), "z": _sb(272, F), "la": _sb(64, F), "lu": _sb(16, U),
+    "off1": _sb(32, U), "x1": _sb(64, F), "wm": _sb(64, F), "wsn": _sb(64, F), "off2": _sb(32, U), "ca": _sb(64, F),
+    "yp": _sb(80, F), "ye": _sb(80, F), "yb": _sb(32, F), "rp": _sb(128, F), "rx": _sb(128, F), "off3": _sb(2, U), "ex": _sb(24, F),
+    "z": _sb(272, F), "la": _sb(64, F), "lu": _sb(16, U),
     "wf": _sb(512, F), "wi": _sb(256, I), "wg": _sb(512, F), "wj": _sb(256, I), "eu": _sb(16, U), "zb": _sb(80, F),
     "cand": _sb(128, F), "selo": _sb(32, U), "ll": _sb(32, U), "sc": _sb(576, F),
     "st": _sb(160, F), "fl": _sb(16, U), "vv": _sb(1024, BF), "vl": _sb(1024, BF), "ff": _sb(1024, BF), "dh": _sb(320, BF),
@@ -265,9 +266,8 @@ def rank_program(g, core, T, topo):
     iota(V("ci", 0, 1), [[0, 1]], 1, False)
     iota(V("cj", 0, 1), [[0, 1]], 17, False)
     iota(V("r256", 0, 256), [[1, 256]], 0)
-    E64, M8, I16, XP = V("io3", 0, 64), V("io3", 64, 128), V("io3", 128, 192), V("io3", 192, 256)
+    E64, I16, XP = V("io3", 0, 64), V("io3", 128, 192), V("io3", 192, 256)
     A16, RP = V("io3", 256, 272), V("io3", 272, 288)
-    iota(M8, [[0, 8], [1, 8]], 0)
     iota(I16, [[0, 4], [1, 16]], 0)
     iota(A16, [[0, 4], [16, 4]], 0)
     iota(RP, [[16, 4], [64, 4]], 0)
@@ -278,33 +278,32 @@ def rank_program(g, core, T, topo):
     def row(n):
         return V("r256", 0, n)
 
-    for k, m in ((1, 15), (2, 16), (3, 3), (4, 7), (6, 9), (7, 20)):
+    for k, m in ((1, 15), (2, 16), (3, 3), (4, 20)):
         ts(col("ci", k), col("ci", 0), m, A.bitwise_and)
     ts(col("ci", 5), col("cj", 0), 16, A.bitwise_and)
     fill(V("ez", 0, 520), 0.0)
-    cp(V("cf", 0, 8), V("ci", 0, 8))
+    cp(V("cf", 0, 6), V("ci", 0, 6))
     fill(V("bt", 0, 288), 0.0)
-    P_, Qc, H16, Q4, Q7, PAR, Q9, Q20 = [col("cf", k) for k in range(8)]
-    Q16, WC, C4, RB, XB, GB, DB, Q0, LC, LM, RA, QH, Q15, CA, XA, GA, PA, PB, PC, PD = [col("cc", k) for k in range(20)]
+    P_, Qc, H16, Q4, Q20, PAR = [col("cf", k) for k in range(6)]
+    Q16, WC, C4, RB, XB, GB, DB, Q0, LC, LM, QH, Q15, CA, XA, GA, PA, PB, PC, PD = [col("cc", k) for k in range(19)]
     PERM, LA, LQ, RL, REP, REP15, GL, LW, DUP, XL, RO = (
         V("ku", 0, 16), V("ku", 16, 17), V("ku", 18, 19), V("ku", 20, 24), V("ku", 24, 28), V("ku", 28, 32), V("ku", 32, 33),
         V("ku", 34, 35), V("ku", 40, 48), V("ku", 48, 112), V("ku", 112, 128))
-    K = [V("k64", 64 * k, 64 * k + 64) for k in range(9)]
-    EM, KEEP8, DIAG, KEEP16, HK, NK, POW, FIX, DUMP = K
+    DIAG, KEEP16, HK, NK, POW, FIX, DUMP = [V("k64", 64 * k, 64 * k + 64) for k in range(2, 9)]
     C16, GATE, Q64 = V("k64", 576, 592), V("k64", 592, 596), V("k64", 596, 597)
+    DESC, GATE16, LAST, DOWN = [V("k64", 608 + 16 * k, 624 + 16 * k) for k in range(4)]
     act(Q16, Qc, 16.0)
     act(PA, Q20, 1.0, -10.0, ACT.Abs)
     act(PB, Qc, 0.25)
     act(WC, Qc, 64.0, 64.0)
-    act(RA, Qc, 0.125)
+    act(RB, Qc, 4.0)
     act(PC, Q4, 3.75, PB)
     act(V("xm", 256, 512), row(256), 0.0)
     act(PD, PA, -4.25, PC)
-    act(RB, Q7, 7.875, RA)
     act(V("xe", 0, 16), row(16), 0.0)
     for e in range(4):
         act(V("xe", 272 + 64 * e, 336 + 64 * e), row(64), 0.0, 16.0 * e)
-        act(V("xm", 304 + 64 * e, 320 + 64 * e), row(16), 0.0, 262144.0 * e + 0.5)
+        act(V("xm", 304 + 64 * e, 320 + 64 * e), row(16), 0.0, 524288.0 * e + 0.5)
         act(V("pw", 16 * e, 16 * e + 16), row(16), 0.0, 16.0 ** e)
     for j in range(1, 4):
         act(V("pw", 64 * j, 64 * j + 64), V("pw", 0, 64), 2.0 ** j)
@@ -314,14 +313,14 @@ def rank_program(g, core, T, topo):
     for b in range(4):
         quant(V("qe", 128 * b, 128 * b + 128), V("se", 128 * b, 128 * b + 128), V("ez", 3 - b, 515 - b))
     fill(V("off1", 0, 32), 0)
-    ts(EM, M8, Q7, A.is_equal)
+    ts(GATE16, row(16), Qc, A.is_ge)
     ts(DIAG, I16, Qc, A.is_equal)
     ts(LQ, PD, 42.5, A.add)
     ts(LW, PD, 42.5, A.add, 16.0, A.mult)
-    ts(RL, row(4), 2.0, A.mult, RB, A.add)
+    ts(RL, row(4), RB, A.add)
     ts(GATE, row(4), Q4, A.is_ge)
     ts(RO, RP, Qc, A.add)
-    cp(REP, row(4))
+    ts(REP, row(4), 4.0, A.mult)
     QU, SU = V("qu", 0, 128), V("su", 0, 128)
     QX, SX, Q0T, S0T = V("qx", 0, 256), V("sx", 0, 256), V("qt0", 0, 256), V("pt0", 0, 256)
     quant(QX, SX, V("xn", 0, 1024))
@@ -330,33 +329,36 @@ def rank_program(g, core, T, topo):
     quant(QU, SU, V("un", 0, 512))
     fill(V("ft", 256, 512), 0.0)
     fill(V("ht", 256, 512), 0.0)
-    act(KEEP8, M8, func=ACT.Sign)
-    act(V("ca", 64, 128), row(64), 0.0)
-    act(V("y2", 128, 136), row(8), 0.0)
-    act(V("y2", 136, 144, 2), row(4), 2.0)
-    act(V("y2", 137, 144, 2), row(4))
     act(KEEP16, I16, func=ACT.Sign)
     act(XA, Q4, -15.0)
     act(GA, PAR, 5.0)
-    act(CA, Q7, 2.0, -47.0)
     act(Q0, Qc, -1.0, 1.0, ACT.Relu)
+    act(V("ye", 64, 80), row(16), 1.0, 1.0)
     act(HK, KEEP16, 0.5)
     act(NK, KEEP16, -1.0, 1.0)
     act(XB, Qc, 16.0, XA)
     act(GB, Q4, 16.0, GA)
-    act(V("ca", 64, 128, 16), row(4), -16.0, 48.0)
-    act(C4, Q4, 14.0, CA)
-    act(V("ex", 0, 16), row(16), 0.0)
-    act(V("y3", 16, 32), row(16), 0.0)
+    act(V("yp", 64, 80), row(16), 0.0)
+    act(DESC, row(16), -32.0, 480.0)
+    act(LAST, row(16), 0.0)
     act(Q15, Qc, 1.0, -14.0, ACT.Relu)
-    act(DB, Qc, 1.0, 320.0)
+    act(V("ye", 67, 80, 4), row(4))
     act(C16, row(16), 16.0)
-    act(Q64, Qc, 1.0, 64.0)
+    act(V("rp", 0, 128), row(128), 0.0)
+    act(V("rx", 0, 128), row(128), 0.0)
+    act(V("k64", 611, 624, 4), row(4), -128.0, 400.0)
+    act(V("k64", 643, 656, 4), row(4), 0.0, 1.0)
     act(LC, Q15, 255.0, -255.0)
     act(LM, Q15, -1000.0, 1255.0)
-    act(DUMP, I16, 16.0, DB)
+    act(DOWN, row(16), -1.0, 12.0)
+    act(CA, Qc, 32.0, -480.0)
+    act(C4, Q4, 4.0, -12.0)
+    act(V("ex", 16, 24), row(8), 0.0)
+    act(DB, Qc, 1.0, 320.0)
+    act(Q64, Qc, 1.0, 64.0)
     act(QH, Qc, 1.0, H16)
     act(V("z", 0, 16), row(16), 16.0)
+    act(DUMP, I16, 16.0, DB)
     act(V("sc", 48, 144), row(96), 0.0)
     act(V("wf", 256, 320), row(64), 0.0)
     act(V("wg", 256, 320), row(64), 0.0)
@@ -443,21 +445,19 @@ def rank_program(g, core, T, topo):
             out, last = [], first
             for k in ks:
                 o = V(name, at, at + 16)
-                out.append(lambda o=o, last=last, k=k: cp(o, ind(last, named(k))))
+                out.append(lambda o=o, last=last, k=k: cp(o, ind(last, named(k)), [maps(t)]))
                 last, at = o, at + 16
             return out, last
         if upto == 0:
-            return V("z", 0, 16)
-        wait("v", maps(t))
+            return [], V("z", 0, 16)
         if upto < 4:
             c, last = chain(range(upto - 1, 0, -1), V("z", 0, 16), "z", at)
-            weave(c)
-            return ind(last, named(0))
+            return c + [lambda: wait("v", maps(t))], ind(last, named(0))
         low = upto // 2
         a, last = chain(range(upto - 1, low - 1, -1), V("z", 0, 16), "z", at)
         b, lb = chain(range(low - 1, 0, -1), row(16), "zb", 0)
-        weave(a, b + [lambda: cp(V("eu", 0, 16), ind(lb, named(0)))])
-        return ind(last, col("eu", 0))
+        b.append(lambda: cp(V("eu", 0, 16), ind(lb, named(0))))
+        return [lambda k=k: weave(a[k:k + 1], b[k:k + 1]) for k in range(len(a))], ind(last, col("eu", 0))
 
     old, new = "ta", "tb"
     for t in range(R):
@@ -494,70 +494,95 @@ def rank_program(g, core, T, topo):
                lambda: tt(V("xs", 0, 64), ind(V("xr", 192, 256), V("offw", 8, 12)), V("xr", 128, 192), A.add),
                lambda: tt(V("xs", 64, 128), ind(V("xs", 0, 64), V("offw", 4, 8)), V("xr", 64, 128), A.add),
                lambda: tt(V("x1", 0, 64), ind(V("xs", 64, 128), V("offw", 0, 4)), V("xr", 0, 64), A.add),
-               lambda: tt(V("wm", 0, 64), ind(V("x1", 0, 64), RL), EM, A.mult)], side[:4])
+               lambda: tt(V("wm", 0, 64), ind(V("x1", 0, 64), RL), DIAG, A.mult)], side[:4])
         tt(V("ca", 0, 64), V("x1", 0, 64), DIAG, A.mult)
-        weave([lambda: scan(V("wsn", 0, 64), KEEP8, V("wm", 0, 64), A.mult, A.add),
-               lambda: ts(V("off2", 0, 16, 2), V("wsn", 7, 64, 8), 2.0 ** -17, A.mult, Q9, A.add)], side[4:])
+        weave([lambda: scan(V("wsn", 0, 64), KEEP16, V("wm", 0, 64), A.mult, A.add),
+               lambda: ts(V("off2", 0, 8, 2), V("wsn", 15, 64, 16), 2.0 ** -17, A.mult, Q4, A.add)], side[4:])
         if t == R - 1:
             act(V("tn", 0, 1024), ind(V(old, 0, 1024), XL))
-        for b in range(7, -1, -1):
-            tt(V("y2", 16 * b, 16 * b + 16), ind(V("y2", 16 * b + 16, 16 * b + 32), col("off2", 2 * b)), V("ca", b, 128, 8), A.add)
-        scan(V("ex", 0, 4), V("y2", 8, 16, 2), GATE, A.max, A.mult)
-        cp(V("y3", 16, 24), V("y2", 0, 16, 2))
-        ts(col("off3", 0), col("ex", 3), C4, A.add)
-        tt(V("y3", 0, 16), ind(V("y2", 0, 16), col("off3", 0)), V("y3", 16, 32), A.add)
+        early = lasts("nbo", [("nbo", len(off), {})]) if t == 0 else [lambda: None] * 5
+        for b in range(3, 0, -1):
+            cp(V("ye", 16 * b, 16 * b + 16), ind(V("ye", 16 * b + 16, 16 * b + 32), col("off2", 2 * b)))
+            tt(V("yp", 16 * b, 16 * b + 16), ind(V("yp", 16 * b + 16, 16 * b + 32), col("off2", 2 * b)), V("ca", b, 64, 4), A.add)
+            early[3 - b]()
+        E0, P0 = ind(V("ye", 16, 32), col("off2", 0)), ind(V("yp", 16, 32), col("off2", 0))
+        tt(V("ye", 0, 16), E0, DESC, A.add)
+        tt(V("yp", 0, 16), P0, V("ca", 0, 64, 4), A.add)
+        tt(V("rp", 0, 16), P0, V("ca", 0, 64, 4), A.add)
+        scan(V("ex", 0, 16), V("ye", 0, 16), GATE16, A.max, A.mult)
+        tt(V("rx", 0, 16), E0, LAST, A.mult)
+        tt(V("yb", 0, 16), E0, LAST, A.mult)
+        ts(col("off3", 0), col("ex", 15), CA, A.add)
+        early[3]()
+        tt(V("yb", 16, 32), V("yb", 0, 16), DOWN, A.add)
+        for k in range(1, 4):
+            tt(V("rx", 32 * k, 32 * k + 16), ind(V("rx", 32 * k - 32, 32 * k), col("off3", 0)), V("yb", 16 * (k // 3), 16 * (k // 3) + 16), A.add)
+            tt(V("rp", 32 * k, 32 * k + 16), ind(V("rp", 32 * k - 32, 32 * k), col("off3", 0)), V("yp", 0, 16), A.add)
+            if k == 1:
+                early[4]()
+        MK = V("rp", 96, 112)
         if t == 0:
-            one(ahead, "yo", T.y3[:, 0:4], T.yo[:, 0:4], V("y3", 0, 4))
+            one(ahead, "yo", ap(MK), T.yo[:, 0:16], MK)
         p = plans[t][r]
         mo = T["mo%d" % t][:, 0:2]
+        own = lists(MK, t > 0, True, "wf", "wi")
+        out = []
         if p["first"] or p["dirs"]:
-            scan(V("ex", 8, 12), V("y3", 4, 8), GATE, A.max, A.mult)
-            ts(V("mo%d" % t, 0, 2), V("ex", 11, 13), col("ex", 3), A.subtract)
+            out = [lambda: scan(V("ex", 16, 20), V("rx", 96, 112, 4), GATE, A.max, A.mult),
+                   lambda: ts(V("mo%d" % t, 0, 2), V("ex", 19, 21), C4, A.add)]
+        weave(out, own[:2])
         if p["first"]:
             send([transfer(topo, core, k, e, T.sem["r%d" % t], mo, T["mr%d" % t][:, 0:2]) for k, e in p["first"]],
                  [V("mo%d" % t, 0, 2)], sum(len(e) for k, e in p["first"]))
         if p["dirs"]:
             send([transfer(topo, core, cores[d], e, T.sem["m%d" % t], mo, T["ml%d" % t][:, 2 * r:2 * r + 2]) for d, e in p["dirs"]],
                  [V("mo%d" % t, 0, 2)], sum(len(e) for k, e in p["dirs"]))
+        steps, e16 = entry(t, (r - HOP[0]) % N if t == 0 else r, 16)
         if t == 0:
             send([transfer(topo, core, k, two[i], T.sem.rw, u8(T.qw[:, 256 * i:256 * i + 256]), u8(T.rq[:, 0:256]))
                   for i, k in enumerate(me["far"])], [V("qw", 0, 512)], len(on))
-            own = lists(V("y3", 0, 8), False, True, "wf", "wi")
-            weave(lasts("nbo", [("nbo", len(off), {})]), own[:8])
-            weave(lists(V("yo", 0, 4), True, False, "wg", "wj", [("yo", len(off), {})]), own[8:] + sums())
+            theirs = lists(V("yo", 0, 16), True, False, "wg", "wj", [("yo", len(off), {})])
+            weave(own[2:5], sums()[:2])
+            weave(theirs[:8], own[5:10] + sums()[2:])
+            tail, rest = theirs[8:], own[10:]
         else:
-            weave(lists(V("y3", 0, 8), True, True, "wf", "wi"), sums())
-        if t == R - 1:
-            cp(V("ud", 0, 128), ind(V("cand", 0, 128), DUP))
-            turn(V("ut", 0, 128), V("ud", 0, 128))
-        e16 = entry(t, (r - HOP[0]) % N if t == 0 else r, 16)
-        ts(V("selo", 0, 16), e16, Qc, A.add)
+            weave(own[2:8], sums())
+            tail, rest = own[8:13], own[13:]
+        weave(tail, steps + [lambda: ts(V("selo", 0, 16), e16, Qc, A.add)])
+        rest[0]()
         cp(V("ll", 0, 16), ind(V("cand", 0, 64), V("selo", 0, 1)))
+        rest[1]()
         op("v", lambda: g.vector.tensor_copy(ap(ind(V("sc", 0, 576), V("ll", 0, 16))), ap(row(256))),
            [V("sc", 0, 576)], [V("ll", 0, 16), row(256)])
         FL, UL = V("fl", 0, 4), V("ll", 16, 32)
         if t == R - 1:
             UL = V("ln", 0, 16)
-            ts(V("selo", 16, 32), e16, 2.0, A.mult, QH, A.add)
+            cp(V("ud", 0, 128), ind(V("cand", 0, 128), DUP))
         turn(V("st", 0, 64), V("sc", 64, 128))
         turn(V("st", 64, 160), V("sc", 48, 144))
         if t == R - 1:
-            cp(UL, ind(V("ut", 0, 128), V("selo", 16, 17)))
+            turn(V("ut", 0, 128), V("ud", 0, 128))
         cp(V("fl", 0, 16), ind(V("st", 0, 160), GL))
+        if t == R - 1:
+            ts(V("selo", 16, 32), e16, 2.0, A.mult, QH, A.add)
         for b in range(4):
             (act if b == 3 else cp)(V("ft", b, 256, 4), ind(V("ff", 256 * b, 256 * b + 256), FL))
+        if t == R - 1:
+            cp(UL, ind(V("ut", 0, 128), V("selo", 16, 17)))
         a = [384, 128, 512][t]
         fc, fs = V("qm", a, a + 128), V("sm", a, a + 128)
         quant(fc, fs, V("ft", 0, 512))
         wc, ws, lo, after = "qp", "sp", 0, [w_here]
         if t == 0:
             wc, ws, after = "qw", "sw", []
+            steps, e16 = entry(t, r, 144)
+            weave(steps[:2], [lambda: fill(V("zt", 0, 512), 0.0)])
         if t == 1:
             fc, fs, tok = exchange(1, a, ahead)
             lo, after = 64, [tok, w_here]
+            ts(V("selo", 16, 32), e16, Q64, A.add)
             for m in (1, 2):
                 quant(V("lq%d" % m, 0, 128), V("ls%d" % m, 0, 128), V("zt", 0, 512))
-            ts(V("selo", 16, 32), e16, Q64, A.add)
             cp(UL, ind(V("cand", 0, 128), V("selo", 16, 17)))
         for b in range(4):
             mm(V("ps%d" % (b + 1), 0, 128), V(wc, 128 * b, 128 * b + 128), V(ws, 128 * b, 128 * b + 128), fc, fs, after)
@@ -572,11 +597,8 @@ def rank_program(g, core, T, topo):
             after, lo = [tok], 64
         if t == 0:
             act(V(old, 0, 1024), ind(V("xn", 0, 1024), XL))
-            fill(V("zt", 0, 512), 0.0)
-            e16 = entry(t, r, 144)
             quant(V("lq0", 0, 128), V("ls0", 0, 128), V("zt", 0, 512))
-            ts(V("selo", 16, 32), e16, Q64, A.add)
-            fill(V("dh", 0, 320), 0.0)
+            weave(steps[2:] + [lambda: ts(V("selo", 16, 32), e16, Q64, A.add)], [lambda: fill(V("dh", 0, 320), 0.0)])
             cp(UL, ind(V("cand", 0, 128), V("selo", 16, 17)))
         if t == 1:
             quant(V("qv", 0, 128), V("sv", 0, 128), V("vn", 0, 512))
@@ -585,8 +607,9 @@ def rank_program(g, core, T, topo):
         banks = ["ps5", "ps6", "ps7", "ps0"]
         for b in range(4):
             mm(V(banks[b], 0, 128), ES[b][0], ES[b][1], hc, hs, after)
-        ts(V("dh", 0, 64), V(banks[0], lo, lo + 64), 2.0, A.mult)
-        for b in range(1, 4):
+        for b in range(2):
+            ts(V("dh", 80 * b, 80 * b + 64), V(banks[b], lo, lo + 64), 2.0, A.mult)
+        for b in range(2, 4):
             act(V("dh", 80 * b, 80 * b + 64), V(banks[b], lo, lo + 64), 2.0)
         if t == R - 1:
             old = "tn"

@@ -5,6 +5,7 @@ A = AluOpType
 ACT = ActivationFunctionType
 N, C, R, HOP = 8, 256, 3, [2, 5, 3]
 Q, S, BF, F, I, U = "float8_e4m3fn_x4", "uint8", "bfloat16", "float32", "int32", "uint16"
+HEADS = (1, 3)
 
 
 def _sb(n, d):
@@ -17,31 +18,31 @@ SCRATCH = {
     "qo": _sb(256, Q), "so": _sb(256, S), "qw": _sb(512, Q), "sw": _sb(512, S), "qp": _sb(512, Q), "sp": _sb(512, S),
     "rq": _sb(256, Q), "rs": _sb(256, S), "ez": _sb(520, BF), "qe": _sb(512, Q), "se": _sb(512, S),
     "qm": _sb(768, Q), "sm": _sb(768, S), "zt": _sb(512, BF), "ft": _sb(512, BF), "ht": _sb(512, BF),
-    "ci": _sb(8, I), "cj": _sb(2, I), "cf": _sb(8, F), "cc": _sb(24, F), "ku": _sb(128, U), "r256": _sb(256, F), "jrow": _sb(256, F),
-    "io3": _sb(288, F), "k64": _sb(672, F), "bt": _sb(288, BF), "tt": _sb(544, BF), "ga": _sb(40, F), "gq": _sb(16, F),
-    "nbo": _sb(32, U), "yo": _sb(16, F), "offq": _sb(16, U), "offw": _sb(16, U), "xe": _sb(528, BF), "xm": _sb(512, F),
-    "xr": _sb(256, F), "xs": _sb(128, F), "pw": _sb(256, F),
-    "off1": _sb(32, U), "x1": _sb(64, F), "wm": _sb(64, F), "wsn": _sb(64, F), "off2": _sb(32, U), "ca": _sb(64, F),
-    "yp": _sb(80, F), "ye": _sb(80, F), "yb": _sb(32, F), "rp": _sb(128, F), "rx": _sb(128, F), "off3": _sb(2, U), "ex": _sb(24, F),
-    "z": _sb(272, F), "la": _sb(64, F), "lu": _sb(16, U),
-    "wf": _sb(512, F), "wi": _sb(256, I), "wg": _sb(512, F), "wj": _sb(256, I), "eu": _sb(16, U), "zb": _sb(80, F),
-    "cand": _sb(128, F), "selo": _sb(32, U), "ll": _sb(32, U), "sc": _sb(576, F),
-    "st": _sb(160, F), "fl": _sb(16, U), "vv": _sb(1024, BF), "vl": _sb(1024, BF), "ff": _sb(1024, BF), "dh": _sb(320, BF),
-    "ud": _sb(128, F), "ut": _sb(128, F), "ln": _sb(16, U), "ys": _sb(256, F), "olb": _sb(64, F),
+    "ci": _sb(16, I), "kf": _sb(64, F), "cf": _sb(16, F), "cc": _sb(40, F), "ku": _sb(192, U), "r256": _sb(256, F), "jrow": _sb(256, F),
+    "io3": _sb(480, F), "k64": _sb(768, F), "kh": _sb(96, BF), "tx": _sb(448, BF), "tm": _sb(448, BF), "te": _sb(320, BF),
+    "bt": _sb(288, BF), "tt": _sb(544, BF), "gb": _sb(96, BF), "sg": _sb(96, F), "idx": _sb(4, U), "tmp": _sb(16, F), "offm": _sb(16, U),
+    "eo": _sb(96, BF), "et": _sb(160, BF), "offa": _sb(32, U), "xa": _sb(192, BF), "ma": _sb(256, F), "mb": _sb(192, F),
+    "yo": _sb(96, BF), "yt": _sb(160, BF), "offb": _sb(32, U), "dd": _sb(64, F), "xb": _sb(48, BF), "ub": _sb(112, F),
+    "ye": _sb(32, F), "offc": _sb(2, U), "xc": _sb(32, BF),
+    "la": _sb(64, F), "lu": _sb(16, U), "luo": _sb(16, U), "wf": _sb(384, F), "wi": _sb(64, I), "wp": _sb(384, F),
+    "cand": _sb(64, F), "cando": _sb(64, F), "ca": _sb(192, F), "cb": _sb(64, BF), "eu": _sb(16, U), "selo": _sb(16, U), "ll": _sb(16, U),
+    "sc": _sb(2368, F), "st": _sb(160, F), "fl": _sb(16, U), "vv": _sb(1024, BF), "vl": _sb(1024, BF), "ff": _sb(1024, BF),
+    "dh": _sb(512, BF), "ui": _sb(96, I), "ul": _sb(16, U), "ys": _sb(256, F), "olb": _sb(64, F),
 }
 for _t in range(R):
     SCRATCH["qt%d" % _t] = _sb(256, Q)
     SCRATCH["pt%d" % _t] = _sb(256, S)
     SCRATCH["lq%d" % _t] = _sb(192, Q)
     SCRATCH["ls%d" % _t] = _sb(384, S)
-    SCRATCH["mo%d" % _t] = _sb(2, U)
-    SCRATCH["mr%d" % _t] = _sb(2, U)
-    SCRATCH["ml%d" % _t] = _sb(16, U)
+    for _k, _d in (("u", U), ("b", BF)):
+        SCRATCH["mo%s%d" % (_k, _t)] = _sb(16, _d)
+        SCRATCH["mr%s%d" % (_k, _t)] = _sb(4, _d)
+        SCRATCH["ml%s%d" % (_k, _t)] = _sb(64, _d)
 SCRATCH["qt3"] = _sb(256, Q)
 SCRATCH["pt3"] = _sb(256, S)
 for _t in range(8):
     SCRATCH["ps%d" % _t] = ("psum", [128, 512], F)
-SEMAPHORES = ["v", "a", "p", "gp", "dx", "du", "dv", "dwc", "dws", "out", "sent", "wp", "rw", "qo", "nbo", "yo",
+SEMAPHORES = ["v", "a", "p", "gp", "dx", "du", "dv", "dwc", "dws", "out", "sent", "wp", "rw", "qo", "luo", "cando",
               "m0", "m1", "m2", "r0", "r1", "r2", "e0", "e1", "e2"]
 
 
@@ -99,6 +100,12 @@ def u8(ap):
     return ap.bitcast(dt.uint8)
 
 
+def slot(kind, k, t):
+    name = "%s%s%d" % (kind, "b" if k in HEADS else "u", t)
+    at = 0 if kind != "ml" else 16 * k if k in HEADS else 4 * k
+    return (name, at, at + 4, 1)
+
+
 def relay_program(g, core, T, topo, r):
     cores = list(T.cores)
     p = plan(r, 0, cores, topo)
@@ -119,7 +126,8 @@ def relay_program(g, core, T, topo, r):
         p = plan(r, t, cores, topo)
         if core in p["second"]:
             g.wait_ge(T.sem["r%d" % t], len(dict(p["first"])[core]))
-            trs = [transfer(topo, core, cores[d], e, T.sem["m%d" % t], T["mr%d" % t][:, 0:2], T["ml%d" % t][:, 2 * r:2 * r + 2])
+            a, b = slot("mr", r, t), slot("ml", r, t)
+            trs = [transfer(topo, core, cores[d], e, T.sem["m%d" % t], T[a[0]][:, a[1]:a[2]], T[b[0]][:, b[1]:b[2]])
                    for d, e in p["second"][core]]
             g.remote_dma_fused(trs, local_sem=T.sem.sent)
             sent += sum(len(e) for d, e in p["second"][core])
@@ -203,10 +211,10 @@ def rank_program(g, core, T, topo):
     def arg(x):
         return ap(x) if isinstance(x, tuple) else x
 
-    def ts(o, i, s1, o0, s2=None, o1=None):
+    def ts(o, i, s1, o0, s2=None, o1=None, after=()):
         if o1 is None:
-            return op("v", lambda: g.vector.tensor_scalar(ap(o), ap(i), arg(s1), None, o0), [o], [i, s1])
-        return op("v", lambda: g.vector.tensor_scalar(ap(o), ap(i), arg(s1), arg(s2), o0, o1), [o], [i, s1, s2])
+            return op("v", lambda: g.vector.tensor_scalar(ap(o), ap(i), arg(s1), None, o0), [o], [i, s1], after)
+        return op("v", lambda: g.vector.tensor_scalar(ap(o), ap(i), arg(s1), arg(s2), o0, o1), [o], [i, s1, s2], after)
 
     def tt(o, a, b, o0, after=()):
         return op("v", lambda: g.vector.tensor_tensor(ap(o), ap(a), ap(b), o0), [o], [a, b], after)
@@ -226,20 +234,20 @@ def rank_program(g, core, T, topo):
     def quant(c, s, i):
         return op("v", lambda: g.vector.quantize_mx(ap(c), ap(s), ap(i)), [c, s], [i])
 
-    def act(o, i, scale=None, bias=None, func=None):
+    def act(o, i, scale=None, bias=None, func=None, after=()):
         if bias is not None:
-            return op("a", lambda: g.scalar.activation(ap(o), ap(i), func or ACT.Identity, bias=arg(bias), scale=arg(scale)), [o], [i, bias, scale])
+            return op("a", lambda: g.scalar.activation(ap(o), ap(i), func or ACT.Identity, bias=arg(bias), scale=arg(scale)), [o], [i, bias, scale], after)
         if scale is not None:
-            return op("a", lambda: g.scalar.activation(ap(o), ap(i), ACT.Copy, scale=arg(scale)), [o], [i, scale])
-        return op("a", lambda: g.scalar.activation(ap(o), ap(i), func or ACT.Copy), [o], [i])
+            return op("a", lambda: g.scalar.activation(ap(o), ap(i), ACT.Copy, scale=arg(scale)), [o], [i, scale], after)
+        return op("a", lambda: g.scalar.activation(ap(o), ap(i), func or ACT.Copy), [o], [i], after)
 
     def mm(o, lc, ls, rc, rs, after=()):
         return op("p", lambda: g.tensor.matmul_mx(ap(o), ap(lc), ap(ls), ap(rc), ap(rs), True, True), [o], [lc, ls, rc, rs], after)
 
-    def iota(o, pattern, mult, flag=True):
+    def iota(o, pattern, mult=0, base=0, flag=True):
         if flag:
-            return op("gp", lambda: g.iota(ap(o), pattern, 0, mult, allow_small_or_imprecise_dtypes=True), [o], [])
-        return op("gp", lambda: g.iota(ap(o), pattern, 0, mult), [o], [])
+            return op("gp", lambda: g.iota(ap(o), pattern, base, mult, allow_small_or_imprecise_dtypes=True), [o], [])
+        return op("gp", lambda: g.iota(ap(o), pattern, base, mult), [o], [])
 
     def load(q, sem, v, src, codes=False):
         qs[q].dma_start(u8(ap(v)) if codes else ap(v), src).then_inc(T.sem[sem], 16)
@@ -259,109 +267,160 @@ def rank_program(g, core, T, topo):
         g.remote_dma_fused(trs, local_sem=T.sem.sent)
         sent[0] += engines
 
-    load("a", "dws", V("sw", 0, 512), T.ws[:])
-    load("s", "dx", V("xn", 0, 1024), T.x[:])
-    load("a", "du", V("un", 0, 512), T.u[:])
-
-    iota(V("ci", 0, 1), [[0, 1]], 1, False)
-    iota(V("cj", 0, 1), [[0, 1]], 17, False)
-    iota(V("r256", 0, 256), [[1, 256]], 0)
-    E64, I16, XP = V("io3", 0, 64), V("io3", 128, 192), V("io3", 192, 256)
-    A16, RP = V("io3", 256, 272), V("io3", 272, 288)
-    iota(I16, [[0, 4], [1, 16]], 0)
-    iota(A16, [[0, 4], [16, 4]], 0)
-    iota(RP, [[16, 4], [64, 4]], 0)
-
     def col(name, k):
         return V(name, k, k + 1)
 
     def row(n):
         return V("r256", 0, n)
 
-    for k, m in ((1, 15), (2, 16), (3, 3), (4, 20)):
-        ts(col("ci", k), col("ci", 0), m, A.bitwise_and)
-    ts(col("ci", 5), col("cj", 0), 16, A.bitwise_and)
-    fill(V("ez", 0, 520), 0.0)
-    cp(V("cf", 0, 6), V("ci", 0, 6))
+    def weave(*chains):
+        for k in range(max(len(c) for c in chains)):
+            for c in chains:
+                if k < len(c):
+                    c[k]()
+
+    load("s", "dx", V("xn", 0, 1024), T.x[:])
+    load("a", "du", V("un", 0, 512), T.u[:])
+    load("a", "dws", V("sw", 0, 512), T.ws[:])
+
+    iota(V("ci", 0, 1), [[0, 1]], 1, flag=False)
+    iota(V("r256", 0, 64), [[1, 64]])
+    X3, XA, XB, KR = V("tx", 384, 448), V("io3", 0, 64), V("io3", 64, 128), V("io3", 128, 160)
+    I16, D4, EP, XP, XQ, DI = [V("io3", 160 + 64 * k, 224 + 64 * k) for k in range(4)] + [V("wp", 0, 64), V("io3", 416, 480)]
+    iota(X3, [[0, 16], [1, 4]])
+    iota(XA, [[0, 4], [1, 4], [0, 4]])
+    iota(XB, [[0, 4], [-4, 4], [1, 4]], base=1)
+    iota(V("r256", 64, 256), [[1, 192]], base=64)
+    iota(I16, [[0, 4], [1, 16]])
+    iota(KR, [[16, 2], [1, 4], [4, 4]])
+    iota(D4, [[1, 16], [0, 4]])
+    iota(EP, [[1, 4], [-1, 16]])
+    iota(DI, [[0, 16], [512, 4]], base=512)
+    for k, m in enumerate((15, 16, 3, 12, 1, 6, 18, 20, 17)):
+        ts(col("ci", k + 1), col("ci", 0), m, A.bitwise_and)
+    cp(V("cf", 0, 10), V("ci", 0, 10))
+    P_, Qc, H16, Q3, Q12, Q1, Q6, Q18, Q20, Q17 = [col("cf", k) for k in range(10)]
+    (OH0, OH1, OH2, OH3, NAT, RR, PA17, PA18, PA20, G1, T0, T1, T2, T3, T4, T5, T6, T7, T8, T9, LC, LM, CA, XB0, XB1, TOP, Q15, Q257,
+     U0, U1, U2, U3, U4, NMID, HALF) = [col("cc", k) for k in range(35)]
+    PERM, LG, LMI, LA, LB, GL, PC, REP, REPT, REPK, NL, QU16, XL, XM = (
+        V("ku", 0, 16), V("ku", 16, 22), V("ku", 22, 23), V("ku", 24, 26), V("ku", 26, 27), V("ku", 28, 29), V("ku", 30, 34),
+        V("ku", 34, 38), V("ku", 38, 46), V("ku", 46, 50), V("ku", 50, 51), V("ku", 52, 54), V("ku", 64, 128), V("ku", 128, 192))
+    DIAG, KEEP16, HK, NK, POW, DUMP = [V("k64", 64 * k, 64 * k + 64) for k in range(6)]
+    LT, KEEP32 = V("k64", 384, 512), V("k64", 512, 640)
+    C16, DESC, GATE16, EC = [V("k64", 640 + 16 * k, 656 + 16 * k) for k in range(4)]
+    act(T0, Q12, 0.25)
+    act(PA18, Q18, 1.0, -9.0, ACT.Abs)
+    act(RR, Q3, 4.0, T0)
+    act(T1, Q1, -9.0, 1225.0)
+    act(NAT, RR, 16.0)
+    act(V("tm", 384, 448), XA, 0.0, 8.0)
+    act(V("tm", 320, 384), XA, -8.0, 8.0, ACT.Relu)
+    act(V("tx", 192, 256), XA, 0.0)
+    act(V("tm", 192, 256), XA, 0.0, 1.0)
+    act(V("tm", 320, 384), V("tm", 320, 384), 1.0, 4.0)
+    act(V("tx", 272, 288), V("tx", 384, 400))
+    act(V("tx", 288, 304), row(16), 0.0)
+    act(V("tx", 304, 320), row(16), 0.0, 1.0)
+    act(V("tm", 256, 272), V("tm", 320, 336), 1.0, 2.0)
+    act(V("tm", 272, 288), row(16), 0.0, 10.0)
+    act(V("tm", 288, 320), row(32), 0.0, 2.0)
+    tt(XB, XA, XB, A.max)
+    ts(V("cc", 0, 4), row(4), Q3, A.is_equal)
+    ts(V("tx", 320, 384), XB, -1.0, A.add)
+    ts(PERM, row(16), NAT, A.add)
+    act(V("tx", 256, 272), V("tx", 320, 336))
+    act(T2, PA18, -136.0, T1)
+    act(V("tx", 0, 192), V("tx", 256, 448))
+    act(G1, Qc, 8.0, T2)
+    act(V("tm", 0, 192), V("tm", 256, 448), 1.0, 1.0)
     fill(V("bt", 0, 288), 0.0)
-    P_, Qc, H16, Q4, Q20, PAR = [col("cf", k) for k in range(6)]
-    Q16, WC, C4, RB, XB, GB, DB, Q0, LC, LM, QH, Q15, CA, XA, GA, PA, PB, PC, PD = [col("cc", k) for k in range(19)]
-    PERM, LA, LQ, RL, REP, REP15, GL, LW, DUP, XL, RO = (
-        V("ku", 0, 16), V("ku", 16, 17), V("ku", 18, 19), V("ku", 20, 24), V("ku", 24, 28), V("ku", 28, 32), V("ku", 32, 33),
-        V("ku", 34, 35), V("ku", 40, 48), V("ku", 48, 112), V("ku", 112, 128))
-    DIAG, KEEP16, HK, NK, POW, FIX, DUMP = [V("k64", 64 * k, 64 * k + 64) for k in range(2, 9)]
-    C16, GATE, Q64 = V("k64", 576, 592), V("k64", 592, 596), V("k64", 596, 597)
-    DESC, GATE16, LAST, DOWN = [V("k64", 608 + 16 * k, 624 + 16 * k) for k in range(4)]
-    act(Q16, Qc, 16.0)
-    act(PA, Q20, 1.0, -10.0, ACT.Abs)
-    act(PB, Qc, 0.25)
-    act(WC, Qc, 64.0, 64.0)
-    act(RB, Qc, 4.0)
-    act(PC, Q4, 3.75, PB)
-    act(V("xm", 256, 512), row(256), 0.0)
-    act(PD, PA, -4.25, PC)
-    act(V("xe", 0, 16), row(16), 0.0)
-    for e in range(4):
-        act(V("xe", 272 + 64 * e, 336 + 64 * e), row(64), 0.0, 16.0 * e)
-        act(V("xm", 304 + 64 * e, 320 + 64 * e), row(16), 0.0, 524288.0 * e + 0.5)
-        act(V("pw", 16 * e, 16 * e + 16), row(16), 0.0, 16.0 ** e)
-    for j in range(1, 4):
-        act(V("pw", 64 * j, 64 * j + 64), V("pw", 0, 64), 2.0 ** j)
+    fill(V("kh", 0, 96), 2.0)
+    fill(V("kf", 16, 56), 0.0)
+    fill(V("kh", 0, 64, 8), 0.0)
+    fill(V("kh", 34, 64, 8), 0.0)
+    fill(V("kh", 64, 96, 2), 0.0)
+    fill(V("ez", 0, 520), 0.0)
+    TS_ = V("te", 256, 320)
+    SA, SB = V("wf", 0, 64), V("wf", 64, 128)
+    ts(SA, V("tx", 256, 320), OH1, A.mult)
+    ts(SB, V("tx", 320, 384), OH2, A.mult)
+    ts(TS_, V("tx", 384, 448), OH3, A.mult)
+    tt(SA, SA, SB, A.add)
+    ts(V("te", 0, 256), V("tx", 0, 256), OH0, A.mult)
+    tt(TS_, TS_, SA, A.add)
     ts(V("ez", 3, 515, 4), row(128), P_, A.is_equal, 0.5, A.mult)
-    ts(PERM, row(16), Q16, A.add)
-    ts(LA, PAR, 17.0 / 16.0, A.mult, Qc, A.add)
-    for b in range(4):
-        quant(V("qe", 128 * b, 128 * b + 128), V("se", 128 * b, 128 * b + 128), V("ez", 3 - b, 515 - b))
-    fill(V("off1", 0, 32), 0)
-    ts(GATE16, row(16), Qc, A.is_ge)
-    ts(DIAG, I16, Qc, A.is_equal)
-    ts(LQ, PD, 42.5, A.add)
-    ts(LW, PD, 42.5, A.add, 16.0, A.mult)
-    ts(RL, row(4), RB, A.add)
-    ts(GATE, row(4), Q4, A.is_ge)
-    ts(RO, RP, Qc, A.add)
-    ts(REP, row(4), 4.0, A.mult)
+    for k in range(4):
+        tt(V("te", 64 * k, 64 * k + 64), V("te", 64 * k, 64 * k + 64), TS_, A.add)
+    act(T3, Q3, func=ACT.Sign)
+    act(T4, Q12, 2.0, 7.0)
+    act(V("kf", 16, 22, 2), row(3), 0.0, G1)
+    act(T5, Q12, 4.0, Q3)
+    act(col("kf", 22), T3, 32.0, T4)
+    act(V("kf", 17, 22, 2), V("kf", 16, 22, 2), 1.0, 128.0)
+    act(PA20, Q20, 1.0, -10.0, ACT.Abs)
+    act(T8, T5, 1.0, 200.0)
+    act(T7, Q6, 0.5)
+    act(T6, PA18, -40.0, 360.0)
+    act(col("kf", 24), PA20, -20.0, T8)
+    act(col("kf", 25), H16, 5.0, T7)
+    act(col("kf", 26), Q6, 8.0, T6)
     QU, SU = V("qu", 0, 128), V("su", 0, 128)
     QX, SX, Q0T, S0T = V("qx", 0, 256), V("sx", 0, 256), V("qt0", 0, 256), V("pt0", 0, 256)
+    quant(QU, SU, V("un", 0, 512))
     quant(QX, SX, V("xn", 0, 1024))
     op("v", lambda: g.vector.tensor_copy(ap(Q0T).bitcast(dt.uint32), ap(QX).bitcast(dt.uint32).indirect(ap(PERM))), [Q0T], [QX, PERM])
     op("a", lambda: g.scalar.activation(ap(S0T), ap(SX).indirect(ap(PERM)), ACT.Copy), [S0T], [SX, PERM])
-    quant(QU, SU, V("un", 0, 512))
-    fill(V("ft", 256, 512), 0.0)
-    fill(V("ht", 256, 512), 0.0)
+    act(V("k64", 688, 704, 4), row(4), 0.0)
+    for e in range(1, 4):
+        act(V("k64", 688 + e, 704, 4), row(4), 0.0, 192.0 + 64 * e)
+    act(V("eo", 0, 96), row(96), 0.0)
+    act(T9, Q3, 16.0, T0)
+    act(PA17, Q17, 1.0, -8.5, ACT.Abs)
+    act(U0, Q3, 16.0, 680.0)
+    act(V("kf", 30, 34), row(4), 4.0, T9)
+    act(col("kf", 28), PA17, -80.0, U0)
+    act(V("kf", 34, 38), row(4))
+    act(V("kf", 38, 46, 2), row(4), 16.0, 15.0)
+    act(V("kf", 39, 46, 2), row(4), 16.0, 15.0)
+    act(V("kf", 46, 50), row(4), 32.0, 31.0)
+    act(col("kf", 50), RR, 1.0, H16)
+    act(V("kf", 52, 54), row(2), 0.0, Qc)
+    act(V("yo", 0, 96), row(96), 0.0)
+    act(TOP, Q12, 1.0, -11.0, ACT.Relu)
+    act(U1, Qc, 4.0, -56.0)
+    act(DESC, row(16), -4.0, 60.0)
+    act(U2, Q12, 1.0, U1)
     act(KEEP16, I16, func=ACT.Sign)
-    act(XA, Q4, -15.0)
-    act(GA, PAR, 5.0)
-    act(Q0, Qc, -1.0, 1.0, ACT.Relu)
-    act(V("ye", 64, 80), row(16), 1.0, 1.0)
+    act(CA, TOP, -16.0, U2)
     act(HK, KEEP16, 0.5)
-    act(NK, KEEP16, -1.0, 1.0)
-    act(XB, Qc, 16.0, XA)
-    act(GB, Q4, 16.0, GA)
-    act(V("yp", 64, 80), row(16), 0.0)
-    act(DESC, row(16), -32.0, 480.0)
-    act(LAST, row(16), 0.0)
-    act(Q15, Qc, 1.0, -14.0, ACT.Relu)
-    act(V("ye", 67, 80, 4), row(4))
-    act(C16, row(16), 16.0)
-    act(V("rp", 0, 128), row(128), 0.0)
-    act(V("rx", 0, 128), row(128), 0.0)
-    act(V("k64", 611, 624, 4), row(4), -128.0, 400.0)
-    act(V("k64", 643, 656, 4), row(4), 0.0, 1.0)
-    act(LC, Q15, 255.0, -255.0)
-    act(LM, Q15, -1000.0, 1255.0)
-    act(DOWN, row(16), -1.0, 12.0)
-    act(CA, Qc, 32.0, -480.0)
-    act(C4, Q4, 4.0, -12.0)
-    act(V("ex", 16, 24), row(8), 0.0)
-    act(DB, Qc, 1.0, 320.0)
-    act(Q64, Qc, 1.0, 64.0)
-    act(QH, Qc, 1.0, H16)
-    act(V("z", 0, 16), row(16), 16.0)
-    act(DUMP, I16, 16.0, DB)
-    act(V("sc", 48, 144), row(96), 0.0)
-    act(V("wf", 256, 320), row(64), 0.0)
-    act(V("wg", 256, 320), row(64), 0.0)
+    act(NK, KEEP16, -0.5, 0.5)
+
+    def more():
+        act(Q15, Qc, 1.0, -14.0, ACT.Relu)
+        act(U3, TOP, -15.0, -252.0)
+        act(C16, row(16), 16.0)
+        act(LC, Q15, 267.0, U3)
+        act(LM, Q15, -1000.0, 1255.0)
+        act(U4, RR, -0.5, -8.0)
+        act(HALF, RR, -0.5, 8.0)
+        act(NMID, H16, -1.0, U4)
+        act(Q257, Qc, -257.0, 257.0, ACT.Relu)
+        act(V("k64", 416, 448), KR, 1.0, NMID, ACT.Abs)
+        act(KEEP32, row(128), func=ACT.Sign)
+        act(V("k64", 448, 480), V("k64", 416, 448), -1.0, HALF, ACT.Relu)
+        act(V("k64", 544, 640, 32), row(3), 0.0)
+        act(V("k64", 384, 416), V("k64", 448, 480), func=ACT.Sign)
+        act(V("sc", 16, 112), row(96), 0.0)
+        act(V("k64", 416, 448), V("k64", 384, 416))
+        act(V("k64", 448, 480), V("k64", 384, 416))
+        act(V("k64", 480, 512), V("k64", 384, 416))
+
+    def later():
+        return [
+            lambda: cp(V("ku", 16, 28), V("kf", 16, 28)), lambda: ts(DIAG, D4, Qc, A.is_equal), lambda: ts(GATE16, row(16), Qc, A.is_ge),
+            lambda: fill(V("ft", 256, 512), 0.0), lambda: fill(V("ht", 256, 512), 0.0), lambda: cp(V("ku", 28, 56), V("kf", 28, 56))] + [
+            lambda b=b: quant(V("qe", 128 * b, 128 * b + 128), V("se", 128 * b, 128 * b + 128), V("ez", 3 - b, 515 - b)) for b in range(4)] + [
+            lambda: scan(POW, HK, NK, A.mult, A.add), lambda: ts(DUMP, EP, 0.0, A.is_gt, Q257, A.mult), lambda: tt(DUMP, DUMP, DI, A.add)]
 
     ahead, behind = cores[(r + HOP[0]) % N], cores[(r - HOP[0]) % N]
     off = me["off"]
@@ -374,10 +433,10 @@ def rank_program(g, core, T, topo):
 
     send([transfer(topo, core, k, two[i], T.sem.rw, T.sw[:, 256 * i:256 * i + 256], T.rs[:, 0:256]) for i, k in enumerate(me["near"])],
          [V("sw", 0, 512)], len(on))
-    iota(E64, [[1, 4], [0, 16]], 0)
-    iota(XP, [[4, 16], [256, 4]], 0)
     one(ahead, "qo", u8(ap(Q0T)), u8(T.qo[:, 0:256]), Q0T)
     one(ahead, "qo", ap(S0T), T.so[:, 0:256], S0T)
+    iota(XP, [[4, 16], [64, 4]])
+    iota(V("jrow", 0, 256), [[1, 16], [16, 4], [64, 4]])
     wait("s", ("qo", 2 * len(off), {}))
     load("s", "dwc", V("qw", 0, 512), T.wc[:], codes=True)
     load("s", "dv", V("vn", 0, 512), T.v[:])
@@ -394,196 +453,223 @@ def rank_program(g, core, T, topo):
     ES = [(V("qe", 128 * b, 128 * b + 128), V("se", 128 * b, 128 * b + 128)) for b in range(4)]
 
     def exchange(m, a, to):
-        send([transfer(topo, core, to, halves[0], T.sem["e%d" % m], u8(T.qm[:, a:a + 64]), u8(T["lq%d" % m][:, 128:192])),
-              transfer(topo, core, to, halves[1], T.sem["e%d" % m], T.sm[:, a:a + 256], T["ls%d" % m][:, 128:384])],
-             [V("qm", a, a + 64), V("sm", a, a + 256)], len(off))
-        return V("lq%d" % m, 64, 192), V("ls%d" % m, 64, 192), ("e%d" % m, len(off), {})
+        one(to, "e%d" % m, u8(T.qm[:, a:a + 64]), u8(T["lq%d" % m][:, 128:192]), V("qm", a, a + 64))
+        one(to, "e%d" % m, T.sm[:, a:a + 64], T["ls%d" % m][:, 128:192], V("sm", a, a + 64))
+        return V("lq%d" % m, 64, 192), V("ls%d" % m, 64, 192), ("e%d" % m, 2 * len(off), {})
 
-    def weave(*chains):
-        for k in range(max(len(c) for c in chains)):
-            for c in chains:
-                if k < len(c):
-                    c[k]()
-
-    def lasts(nb, after):
+    def lasts():
         L0, L1, L2, L3 = [V("la", 16 * k, 16 * k + 16) for k in range(4)]
+        return [lambda: ts(L3, V("sg", 65, 96, 2), 16.0, A.mult, Qc, A.add), lambda: tt(L0, L3, C16, A.add),
+                lambda: ts(L1, L0, 256.0, A.is_ge, LC, A.mult), lambda: tt(L2, L0, L1, A.add), lambda: ts(V("lu", 0, 16), L2, LM, A.min)]
 
-        def fetch():
-            ts(V("lu", 0, 16), L2, LM, A.min)
-            for b in range(4):
-                act(V("vl", 256 * b, 256 * b + 256), ind(V("vv", 256 * b, 256 * b + 256), V("lu", 0, 16)))
-        return [lambda: cp(L3, V(nb, 0, 32, 2), after), lambda: tt(L0, L3, C16, A.add), lambda: ts(L1, L0, 256.0, A.is_ge, LC, A.mult),
-                lambda: tt(L2, L0, L1, A.add), fetch]
+    def fetch(lu, after=()):
+        for b in range(4):
+            act(V("vl", 256 * b, 256 * b + 256), ind(V("vv", 256 * b, 256 * b + 256), lu), after=after)
 
-    def lists(masks, starts, bodies, wf, wi, after=()):
-        W0, BITS, LCN, TL, TS, TB, LP, D1 = [V(wf, 64 * k, 64 * k + 64) for k in range(8)]
-        YI, KI, AI, BI = [V(wi, 64 * k, 64 * k + 64) for k in range(4)]
-        c = [lambda: tt(W0, ind(masks, REP), POW, A.mult, after), lambda: ts(YI, W0, -0.5, A.add), lambda: ts(BI, YI, 1, A.bitwise_and),
-             lambda: cp(BITS, BI), lambda: scan(LCN, KEEP16, BITS, A.mult, A.add)]
-        if starts:
-            c += [lambda: ts(D1, BITS, -1024.0, A.mult)]
-        c += [lambda: turn(TL, LCN), lambda: ts(LP, LCN, 63.0, A.add),
-              lambda: scan(V(wf, 257, 320), V(wf, 192, 255), V("k64", 193, 256), A.add, A.mult)]
-        if starts:
-            c += [lambda: tt(D1, D1, DUMP, A.add)]
-        c += [lambda: turn(TB, TS), lambda: tt(KI, ind(TB, REP15), LP, A.add)]
-        if starts:
-            c += [lambda: tt(V("cand", 0, 64), KI, D1, A.max)]
-        if bodies:
-            c += [lambda: ts(AI, KI, 63, A.bitwise_and), lambda: tt(V("cand", 64, 128), AI, FIX, A.add)]
-        return c
+    def lists(mk):
+        W0, BITS, NB, LCN, D1, LP = [V("wf", 64 * k, 64 * k + 64) for k in range(6)]
+        RI = V("wi", 0, 64)
+        TA, TB, TC = [V("wp", 128 * k, 128 * k + 128) for k in range(3)]
+        return [lambda: tt(W0, ind(mk, REP), POW, A.mult), lambda: tt(RI, ind(mk, REP), POW, A.mult),
+                lambda: tt(BITS, RI, W0, A.is_gt), lambda: tt(NB, RI, W0, A.is_lt),
+                lambda: scan(LCN, KEEP16, BITS, A.mult, A.add), lambda: tt(D1, NB, DUMP, A.mult),
+                lambda: tt(TA, ind(LCN, REPT), LT, A.mult), lambda: tt(LP, LCN, D1, A.add),
+                lambda: turn(TB, TA), lambda: ts(LP, LP, -1.0, A.add),
+                lambda: scan(TC, KEEP32, TB, A.mult, A.add), lambda: tt(V("cand", 0, 64), ind(TC, REPK), LP, A.add)]
 
     def sums():
         return [lambda b=b: tt(V("ff", 256 * b, 256 * b + 256), V("vl", 256 * b, 256 * b + 256), V("ps%d" % (b + 1), 0, 256), A.add)
                 for b in range(4)]
 
-    def entry(t, upto, at):
+    def entry(t, upto, cand, after=()):
         def named(k):
-            return col("mo%d" % t, 0) if k == r else col("ml%d" % t, 2 * k)
+            return slot("mo" if k == r else "ml", k, t)
 
-        def chain(ks, first, name, at):
-            out, last = [], first
-            for k in ks:
-                o = V(name, at, at + 16)
-                out.append(lambda o=o, last=last, k=k: cp(o, ind(last, named(k)), [maps(t)]))
-                last, at = o, at + 16
-            return out, last
+        def first(k):
+            v = named(k)
+            return V(v[0], v[1], v[1] + 1)
+        here = [maps(t)]
+        SELO, Z = V("selo", 0, 16), V("k64", 640, 644)
         if upto == 0:
-            return [], V("z", 0, 16)
-        if upto < 4:
-            c, last = chain(range(upto - 1, 0, -1), V("z", 0, 16), "z", at)
-            return c + [lambda: wait("v", maps(t))], ind(last, named(0))
-        low = upto // 2
-        a, last = chain(range(upto - 1, low - 1, -1), V("z", 0, 16), "z", at)
-        b, lb = chain(range(low - 1, 0, -1), row(16), "zb", 0)
-        b.append(lambda: cp(V("eu", 0, 16), ind(lb, named(0))))
-        return [lambda k=k: weave(a[k:k + 1], b[k:k + 1]) for k in range(len(a))], ind(last, col("eu", 0))
+            return [lambda: wait("v", here[0])], cand, QU16
+        if upto < 3:
+            return [lambda: ts(SELO, ind(Z if upto == 1 else named(1), first(0)), Qc, A.add, after=here)], cand, V("selo", 0, 2)
+        a = [lambda: cp(V("eu", 0, 16), ind(named(1), first(0)), here),
+             lambda: cp(V("cb", 0, 64), ind(Z if upto == 3 else named(3), named(2))),
+             lambda: ts(SELO, ind(V("cb", 0, 64), col("eu", 0)), Qc, A.add)]
+        b = []
+        for k in range(upto - 1, 3, -1):
+            o = V("ca", 64 * (k - 4), 64 * (k - 4) + 64)
+            b.append(lambda o=o, cand=cand, k=k: cp(o, ind(cand, named(k)), here + list(after)))
+            cand = o
+        b += [lambda: None] * 3
+        return [a[0], a[1], b[0], a[2], b[1], b[2]], cand, V("selo", 0, 2)
+
+    def bodies(t, win, sel):
+        if t < R - 1:
+            return [lambda: cp(V("ui", 0, 16), ind(win, V(sel[0], sel[1], sel[1] + 1))), lambda: ts(V("ui", 32, 48), V("ui", 0, 16), 319, A.bitwise_and),
+                    lambda: ts(V("ul", 0, 16), V("ui", 32, 48), 64.0, A.min)]
+        return [lambda: cp(V("la", 0, 32), ind(win, sel)), lambda: turn(V("la", 32, 64), V("la", 0, 32)),
+                lambda: cp(V("ui", 0, 16), ind(V("la", 32, 64), NL)), lambda: ts(V("ui", 32, 48), V("ui", 0, 16), 319, A.bitwise_and),
+                lambda: ts(V("ul", 0, 16), V("ui", 32, 48), 64.0, A.min)]
+
+    def run(c):
+        for f in c:
+            f()
 
     old, new = "ta", "tb"
     for t in range(R):
+        spare = later() if t == 0 else []
+
+        def gap(n=1):
+            for k in range(min(n, len(spare))):
+                spare.pop(0)()
         QT, PT = V("qt%d" % t, 0, 256), V("pt%d" % t, 0, 256)
         mm(V("ps0", 0, 256), QU, SU, QT, PT)
-        if t == 0:
-            QT, PT = V("qo", 0, 256), V("so", 0, 256)
-        for b in range(4):
-            mm(V("ps%d" % (b + 1), 0, 256), ES[b][0], ES[b][1], QT, PT, [("qo", 2 * len(off), {})] if t == 0 else [])
-        ts(V("bt", 16, 272), V("ps0", 0, 256), 0.0, A.is_gt, WC, A.mult)
+
+        def unpack(QT, PT, after):
+            for b in range(4):
+                mm(V("ps%d" % (b + 1), 0, 256), ES[b][0], ES[b][1], QT, PT, after)
+        if t > 0:
+            unpack(QT, PT, [])
+        gap(4)
+        ts(V("bt", 16, 272), V("ps0", 0, 256), 0.0, A.is_gt)
+        gap()
         turn(V("tt", 0, 256), V("bt", 16, 272))
         turn(V("tt", 256, 544), V("bt", 0, 288))
-        for b in range(4):
-            act(V("vv", 256 * b, 256 * b + 256), V("ps%d" % (b + 1), 0, 256))
-        tt(V("ga", 0, 34), V("tt", 0, 544, 16), V("tt", 1, 544, 16), A.add)
-        tt(V("gq", 0, 16), ind(V("ga", 0, 34), LQ), A16, A.add)
-        ts(V("off1", 0, 32, 2), ind(V("ga", 0, 34), LA), 0.25, A.mult, Qc, A.add)
-        ts(V("offq", 0, 16), V("gq", 0, 16), Qc, A.add)
+        gap()
+        if t > 0:
+            for b in range(4):
+                act(V("vv", 256 * b, 256 * b + 256), V("ps%d" % (b + 1), 0, 256))
+        cp(V("gb", 0, 96), ind(V("tt", 0, 544), LG))
+        gap()
+        scan(V("sg", 0, 96), V("kh", 0, 96), V("gb", 0, 96), A.mult, A.add)
+        gap()
+        cp(V("idx", 0, 4), V("sg", 7, 32, 8))
+        tt(V("tmp", 0, 16), ind(V("sg", 0, 64), LMI), EC, A.add)
+        cp(V("eo", 16, 80), ind(V("te", 0, 256), V("idx", 0, 4)))
+        cp(V("offm", 0, 16), V("tmp", 0, 16))
+        turn(V("et", 0, 64), V("eo", 16, 80))
+        turn(V("et", 64, 160), V("eo", 0, 96))
+        act(V("xa", 128, 192), ind(V("tx", 0, 448), V("offm", 12, 16)))
+        for i in range(3, -1, -1):
+            act(V("ma", 64 * i, 64 * i + 64), ind(V("tm", 0, 448), V("offm", 4 * i, 4 * i + 4)), 16.0 ** i, 0.5 if i == 3 else None)
         if t == 0:
-            one(ahead, "nbo", T.off1[:, 0:32], T.nbo[:, 0:32], V("off1", 0, 32))
-            iota(V("jrow", 0, 256), [[1, 16], [16, 16]], 0)
-        for j in range(3, -1, -1):
-            o = V("offq", 4 * j, 4 * j + 4)
-            cp(V("xe", 16 + 64 * j, 80 + 64 * j), ind(V("xe", 80 + 64 * j, 336 + 64 * j), o))
-            tt(V("xm", 64 * j, 64 * j + 64), ind(V("xm", 64 * j + 64, 64 * j + 320), o), V("pw", 64 * j, 64 * j + 64), A.add)
-        turn(V("tt", 0, 256), V("xe", 16, 272))
-        turn(V("tt", 256, 544), V("xe", 0, 288))
-        cp(V("xr", 0, 256), ind(V("xm", 0, 256), RO))
-        side = lasts("off1", ())
+            more()
+        gap()
+        ts(V("offa", 0, 32), ind(V("et", 0, 160), LA), 16.0, A.mult, Qc, A.add)
+        gap()
+        mk = V("ma", 192, 256)
+        for i in (2, 1):
+            o = V("offa", 4 * i, 4 * i + 4)
+            cp(V("xa", 64 * i - 64, 64 * i), ind(V("xa", 64 * i, 64 * i + 64), o))
+            tt(V("mb", 64 * i, 64 * i + 64), ind(mk, o), V("ma", 64 * i, 64 * i + 64), A.add)
+            mk = V("mb", 64 * i, 64 * i + 64)
+        for e in range(4):
+            cp(V("yo", 16 + e, 80, 4), ind(V("xa", 0, 64), col("offa", 16 + 2 * e)))
+        tt(V("mb", 0, 64), ind(mk, V("offa", 0, 4)), V("ma", 0, 64), A.add)
+        turn(V("yt", 0, 64), V("yo", 16, 80))
+        turn(V("yt", 64, 160), V("yo", 0, 96))
+        tt(V("dd", 0, 64), ind(V("mb", 0, 64), PC), DIAG, A.mult)
+        ts(V("offb", 0, 32, 2), ind(V("yt", 0, 160), LB), Q12, A.add)
+        gap()
         if t == 0:
-            side = [lambda: tt(FIX, I16, E64, A.is_lt), lambda: scan(POW, HK, NK, A.mult, A.add), lambda: cp(GL, GB),
-                    lambda: ts(REP15, row(4), 16.0, A.mult, 15.0, A.add), lambda: ts(FIX, FIX, Q0, A.mult), lambda: ts(XL, XP, XB, A.add)]
-        weave([lambda: ts(V("offw", 0, 16), ind(V("tt", 0, 544), LW), Qc, A.add),
-               lambda: tt(V("xs", 0, 64), ind(V("xr", 192, 256), V("offw", 8, 12)), V("xr", 128, 192), A.add),
-               lambda: tt(V("xs", 64, 128), ind(V("xs", 0, 64), V("offw", 4, 8)), V("xr", 64, 128), A.add),
-               lambda: tt(V("x1", 0, 64), ind(V("xs", 64, 128), V("offw", 0, 4)), V("xr", 0, 64), A.add),
-               lambda: tt(V("wm", 0, 64), ind(V("x1", 0, 64), RL), DIAG, A.mult)], side[:4])
-        tt(V("ca", 0, 64), V("x1", 0, 64), DIAG, A.mult)
-        weave([lambda: scan(V("wsn", 0, 64), KEEP16, V("wm", 0, 64), A.mult, A.add),
-               lambda: ts(V("off2", 0, 8, 2), V("wsn", 15, 64, 16), 2.0 ** -17, A.mult, Q4, A.add)], side[4:])
-        if t == R - 1:
-            act(V("tn", 0, 1024), ind(V(old, 0, 1024), XL))
-        early = lasts("nbo", [("nbo", len(off), {})]) if t == 0 else [lambda: None] * 5
-        for b in range(3, 0, -1):
-            cp(V("ye", 16 * b, 16 * b + 16), ind(V("ye", 16 * b + 16, 16 * b + 32), col("off2", 2 * b)))
-            tt(V("yp", 16 * b, 16 * b + 16), ind(V("yp", 16 * b + 16, 16 * b + 32), col("off2", 2 * b)), V("ca", b, 64, 4), A.add)
-            early[3 - b]()
-        E0, P0 = ind(V("ye", 16, 32), col("off2", 0)), ind(V("yp", 16, 32), col("off2", 0))
-        tt(V("ye", 0, 16), E0, DESC, A.add)
-        tt(V("yp", 0, 16), P0, V("ca", 0, 64, 4), A.add)
-        tt(V("rp", 0, 16), P0, V("ca", 0, 64, 4), A.add)
-        scan(V("ex", 0, 16), V("ye", 0, 16), GATE16, A.max, A.mult)
-        tt(V("rx", 0, 16), E0, LAST, A.mult)
-        tt(V("yb", 0, 16), E0, LAST, A.mult)
-        ts(col("off3", 0), col("ex", 15), CA, A.add)
-        early[3]()
-        tt(V("yb", 16, 32), V("yb", 0, 16), DOWN, A.add)
-        for k in range(1, 4):
-            tt(V("rx", 32 * k, 32 * k + 16), ind(V("rx", 32 * k - 32, 32 * k), col("off3", 0)), V("yb", 16 * (k // 3), 16 * (k // 3) + 16), A.add)
-            tt(V("rp", 32 * k, 32 * k + 16), ind(V("rp", 32 * k - 32, 32 * k), col("off3", 0)), V("yp", 0, 16), A.add)
-            if k == 1:
-                early[4]()
-        MK = V("rp", 96, 112)
-        if t == 0:
-            one(ahead, "yo", ap(MK), T.yo[:, 0:16], MK)
+            unpack(V("qo", 0, 256), V("so", 0, 256), [("qo", 2 * len(off), {})])
+            for b in range(4):
+                act(V("vv", 256 * b, 256 * b + 256), V("ps%d" % (b + 1), 0, 256))
+            spare += lasts()
+        x, m = V("yo", 64, 80), V("dd", 48, 64)
+        for i in (2, 1):
+            o = col("offb", 4 * i)
+            cp(V("xb", 16 * i, 16 * i + 16), ind(x, o))
+            tt(V("ub", 16 * i, 16 * i + 16), ind(m, o), V("dd", 16 * i, 16 * i + 16), A.add)
+            gap()
+            x, m = V("xb", 16 * i, 16 * i + 16), V("ub", 16 * i, 16 * i + 16)
+        o = col("offb", 0)
+        tt(V("ye", 0, 16), ind(x, o), DESC, A.add)
+        cp(V("xb", 0, 16), ind(x, o))
+        scan(V("ye", 16, 32), V("ye", 0, 16), GATE16, A.max, A.mult)
+        tt(V("ub", 0, 16), ind(m, o), V("dd", 0, 16), A.add)
+        ts(col("offc", 0), col("ye", 31), CA, A.add)
+        tt(V("ub", 96, 112), ind(m, o), V("dd", 0, 16), A.add)
+        gap()
+        o = col("offc", 0)
+        x, m = V("xb", 0, 16), V("ub", 96, 112)
+        for i in (0, 1):
+            cp(V("xc", 16 * i, 16 * i + 16), ind(x, o))
+            tt(V("ub", 48 + 16 * i, 64 + 16 * i), ind(m, o), V("ub", 0, 16), A.add)
+            gap(2)
+            x, m = V("xc", 16 * i, 16 * i + 16), V("ub", 48 + 16 * i, 64 + 16 * i)
         p = plans[t][r]
-        mo = T["mo%d" % t][:, 0:2]
-        own = lists(MK, t > 0, True, "wf", "wi")
-        out = []
+        mo = slot("mo", r, t)
         if p["first"] or p["dirs"]:
-            out = [lambda: scan(V("ex", 16, 20), V("rx", 96, 112, 4), GATE, A.max, A.mult),
-                   lambda: ts(V("mo%d" % t, 0, 2), V("ex", 19, 21), C4, A.add)]
-        weave(out, own[:2])
+            wide = V(mo[0], 0, 16)
+            if r in HEADS:
+                ts(wide, ind(x, o), 16.0, A.mult)
+            elif r < 4:
+                cp(wide, ind(x, o))
+            else:
+                ts(wide, ind(x, o), 16.0, A.mult, Qc, A.add)
+        MK = V("ub", 80, 96)
+        tt(MK, ind(m, o), V("ub", 0, 16), A.add)
         if p["first"]:
-            send([transfer(topo, core, k, e, T.sem["r%d" % t], mo, T["mr%d" % t][:, 0:2]) for k, e in p["first"]],
-                 [V("mo%d" % t, 0, 2)], sum(len(e) for k, e in p["first"]))
+            send([transfer(topo, core, k, e, T.sem["r%d" % t], ap(mo), ap(slot("mr", r, t))) for k, e in p["first"]],
+                 [mo], sum(len(e) for k, e in p["first"]))
         if p["dirs"]:
-            send([transfer(topo, core, cores[d], e, T.sem["m%d" % t], mo, T["ml%d" % t][:, 2 * r:2 * r + 2]) for d, e in p["dirs"]],
-                 [V("mo%d" % t, 0, 2)], sum(len(e) for k, e in p["dirs"]))
-        steps, e16 = entry(t, (r - HOP[0]) % N if t == 0 else r, 16)
+            send([transfer(topo, core, cores[d], e, T.sem["m%d" % t], ap(mo), ap(slot("ml", r, t))) for d, e in p["dirs"]],
+                 [mo], sum(len(e) for k, e in p["dirs"]))
+        gap(99)
+        own, CAND = lists(MK), V("cand", 0, 64)
         if t == 0:
+            one(ahead, "luo", T.lu[:, 0:16], T.luo[:, 0:16], V("lu", 0, 16))
+            run(own)
+            one(ahead, "cando", T.cand[:, 0:64], T.cando[:, 0:64], CAND)
             send([transfer(topo, core, k, two[i], T.sem.rw, u8(T.qw[:, 256 * i:256 * i + 256]), u8(T.rq[:, 0:256]))
                   for i, k in enumerate(me["far"])], [V("qw", 0, 512)], len(on))
-            theirs = lists(V("yo", 0, 16), True, False, "wg", "wj", [("yo", len(off), {})])
-            weave(own[2:5], sums()[:2])
-            weave(theirs[:8], own[5:10] + sums()[2:])
-            tail, rest = theirs[8:], own[10:]
+            fetch(V("luo", 0, 16), [("luo", len(off), {})])
+            ts(XB0, Q12, 64.0, A.mult, Q3, A.add)
+            fill(V("zt", 0, 512), 0.0)
+            ts(XL, XP, XB0, A.add)
+            fill(V("dh", 0, 320), 0.0)
+            quant(V("lq0", 0, 128), V("ls0", 0, 128), V("zt", 0, 512))
+            run(sums())
+            theirs = [("cando", len(off), {})]
+            steps, win, sel = entry(t, (r - HOP[0]) % N, V("cando", 0, 64), theirs)
         else:
-            weave(own[2:8], sums())
-            tail, rest = own[8:13], own[13:]
-        weave(tail, steps + [lambda: ts(V("selo", 0, 16), e16, Qc, A.add)])
-        rest[0]()
-        cp(V("ll", 0, 16), ind(V("cand", 0, 64), V("selo", 0, 1)))
-        rest[1]()
-        op("v", lambda: g.vector.tensor_copy(ap(ind(V("sc", 0, 576), V("ll", 0, 16))), ap(row(256))),
-           [V("sc", 0, 576)], [V("ll", 0, 16), row(256)])
-        FL, UL = V("fl", 0, 4), V("ll", 16, 32)
-        if t == R - 1:
-            UL = V("ln", 0, 16)
-            cp(V("ud", 0, 128), ind(V("cand", 0, 128), DUP))
-        turn(V("st", 0, 64), V("sc", 64, 128))
-        turn(V("st", 64, 160), V("sc", 48, 144))
-        if t == R - 1:
-            turn(V("ut", 0, 128), V("ud", 0, 128))
+            weave(lasts(), own[:5])
+            fetch(V("lu", 0, 16))
+            if t == R - 1:
+                act(V("tn", 0, 1024), ind(V(old, 0, 1024), XM))
+            weave(own[5:], [lambda: None] * 3 + sums())
+            theirs = []
+            steps, win, sel = entry(t, r, CAND)
+        run(steps)
+        cp(V("ll", 0, 16), ind(win, V(sel[0], sel[1], sel[1] + 1)), theirs)
+        op("v", lambda: g.vector.tensor_copy(ap(ind(V("sc", 32, 2368), V("ll", 0, 16))), ap(row(256))),
+           [V("sc", 32, 2368)], [V("ll", 0, 16), row(256)])
+        ub = bodies(t, win, sel) if t > 0 else []
+        FL, UL = V("fl", 0, 4), V("ul", 0, 16)
+        run(ub[:1])
+        turn(V("st", 0, 64), V("sc", 32, 96))
+        turn(V("st", 64, 160), V("sc", 16, 112))
+        run(ub[1:2])
         cp(V("fl", 0, 16), ind(V("st", 0, 160), GL))
-        if t == R - 1:
-            ts(V("selo", 16, 32), e16, 2.0, A.mult, QH, A.add)
+        run(ub[2:3])
         for b in range(4):
-            (act if b == 3 else cp)(V("ft", b, 256, 4), ind(V("ff", 256 * b, 256 * b + 256), FL))
-        if t == R - 1:
-            cp(UL, ind(V("ut", 0, 128), V("selo", 16, 17)))
+            (act if b % 2 else cp)(V("ft", b, 256, 4), ind(V("ff", 256 * b, 256 * b + 256), FL))
+        run(ub[3:4])
         a = [384, 128, 512][t]
         fc, fs = V("qm", a, a + 128), V("sm", a, a + 128)
         quant(fc, fs, V("ft", 0, 512))
+        run(ub[4:])
         wc, ws, lo, after = "qp", "sp", 0, [w_here]
         if t == 0:
             wc, ws, after = "qw", "sw", []
-            steps, e16 = entry(t, r, 144)
-            weave(steps[:2], [lambda: fill(V("zt", 0, 512), 0.0)])
         if t == 1:
             fc, fs, tok = exchange(1, a, ahead)
             lo, after = 64, [tok, w_here]
-            ts(V("selo", 16, 32), e16, Q64, A.add)
             for m in (1, 2):
                 quant(V("lq%d" % m, 0, 128), V("ls%d" % m, 0, 128), V("zt", 0, 512))
-            cp(UL, ind(V("cand", 0, 128), V("selo", 16, 17)))
         for b in range(4):
             mm(V("ps%d" % (b + 1), 0, 128), V(wc, 128 * b, 128 * b + 128), V(ws, 128 * b, 128 * b + 128), fc, fs, after)
         for b in range(4):
@@ -597,19 +683,18 @@ def rank_program(g, core, T, topo):
             after, lo = [tok], 64
         if t == 0:
             act(V(old, 0, 1024), ind(V("xn", 0, 1024), XL))
-            quant(V("lq0", 0, 128), V("ls0", 0, 128), V("zt", 0, 512))
-            weave(steps[2:] + [lambda: ts(V("selo", 16, 32), e16, Q64, A.add)], [lambda: fill(V("dh", 0, 320), 0.0)])
-            cp(UL, ind(V("cand", 0, 128), V("selo", 16, 17)))
+            steps, win, sel = entry(t, r, CAND)
+            run(steps + bodies(t, win, sel))
         if t == 1:
+            iota(XQ, [[4, 4], [16, 4], [256, 4]])
             quant(V("qv", 0, 128), V("sv", 0, 128), V("vn", 0, 512))
-            ts(V("ku", 40, 48, 2), row(4), 16.0, A.mult, Q64, A.add)
-            ts(V("ku", 41, 48, 2), row(4), 16.0, A.mult, Q64, A.add)
+            ts(XB1, Q12, 16.0, A.mult, Q3, A.add)
+            ts(XM, XQ, XB1, A.add)
         banks = ["ps5", "ps6", "ps7", "ps0"]
         for b in range(4):
             mm(V(banks[b], 0, 128), ES[b][0], ES[b][1], hc, hs, after)
-        for b in range(2):
-            ts(V("dh", 80 * b, 80 * b + 64), V(banks[b], lo, lo + 64), 2.0, A.mult)
-        for b in range(2, 4):
+        ts(V("dh", 0, 64), V(banks[0], lo, lo + 64), 2.0, A.mult)
+        for b in range(1, 4):
             act(V("dh", 80 * b, 80 * b + 64), V(banks[b], lo, lo + 64), 2.0)
         if t == R - 1:
             old = "tn"
@@ -620,9 +705,9 @@ def rank_program(g, core, T, topo):
         quant(V("qt%d" % (t + 1), 0, 256), V("pt%d" % (t + 1), 0, 256), V(new, 0, 1024))
         old, new = new, "ta" if new == "tb" else "tb"
 
-    QN, SN = V("qt3", 0, 256), V("pt3", 0, 256)
-    mm(V("ps1", 0, 256), V("qv", 0, 128), V("sv", 0, 128), QN, SN)
-    store("s", T.oc[:], u8(ap(QN)), QN)
+    QN_, SN = V("qt3", 0, 256), V("pt3", 0, 256)
+    mm(V("ps1", 0, 256), V("qv", 0, 128), V("sv", 0, 128), QN_, SN)
+    store("s", T.oc[:], u8(ap(QN_)), QN_)
     for k in range(4):
         store("a", T.osc[4 * k:4 * k + 4, 0:256], T.pt3[32 * k:32 * k + 4, 0:256], SN)
     cp(V("ys", 0, 256), V("ps1", 0, 256))

@@ -5,7 +5,7 @@ A = AluOpType
 ACT = ActivationFunctionType
 N, C, R, HOP = 8, 256, 3, [2, 5, 3]
 Q, S, BF, F, I, U = "float8_e4m3fn_x4", "uint8", "bfloat16", "float32", "int32", "uint16"
-HEADS = (1, 3)
+HEADS = (1, 3, 6)
 
 
 def _sb(n, d):
@@ -25,7 +25,7 @@ SCRATCH = {
     "yo": _sb(96, BF), "yt": _sb(160, BF), "offb": _sb(32, U), "dd": _sb(64, F), "xb": _sb(48, BF), "ub": _sb(112, F),
     "ye": _sb(32, F), "offc": _sb(2, U), "xc": _sb(32, BF),
     "la": _sb(64, F), "lu": _sb(16, U), "luo": _sb(16, U), "wf": _sb(384, F), "wi": _sb(64, I), "wp": _sb(384, F),
-    "cand": _sb(64, F), "cando": _sb(64, F), "ca": _sb(192, F), "cb": _sb(64, BF), "eu": _sb(16, U), "selo": _sb(16, U), "ll": _sb(16, U),
+    "cand": _sb(64, F), "cando": _sb(64, F), "cb": _sb(192, BF), "eu": _sb(32, U), "selo": _sb(16, U), "ll": _sb(16, U),
     "sc": _sb(2368, F), "st": _sb(160, F), "fl": _sb(16, U), "vv": _sb(1024, BF), "vl": _sb(1024, BF), "ff": _sb(1024, BF),
     "dh": _sb(512, BF), "ui": _sb(96, I), "ul": _sb(16, U), "ys": _sb(256, F), "olb": _sb(64, F),
 }
@@ -37,7 +37,7 @@ for _t in range(R):
     for _k, _d in (("u", U), ("b", BF)):
         SCRATCH["mo%s%d" % (_k, _t)] = _sb(16, _d)
         SCRATCH["mr%s%d" % (_k, _t)] = _sb(4, _d)
-        SCRATCH["ml%s%d" % (_k, _t)] = _sb(64, _d)
+        SCRATCH["ml%s%d" % (_k, _t)] = _sb(128, _d)
 SCRATCH["qt3"] = _sb(256, Q)
 SCRATCH["pt3"] = _sb(256, S)
 for _t in range(8):
@@ -285,6 +285,8 @@ def rank_program(g, core, T, topo):
 
     iota(V("ci", 0, 1), [[0, 1]], 1, flag=False)
     iota(V("r256", 0, 64), [[1, 64]])
+    iota(V("ci", 12, 13), [[0, 1]], 4, flag=False)
+    iota(V("ci", 13, 14), [[0, 1]], 64, flag=False)
     X3, XA, XB, KR = V("tx", 384, 448), V("io3", 0, 64), V("io3", 64, 128), V("io3", 128, 160)
     I16, D4, EP, XP, XQ, DI = [V("io3", 160 + 64 * k, 224 + 64 * k) for k in range(4)] + [V("wp", 0, 64), V("io3", 416, 480)]
     iota(X3, [[0, 16], [1, 4]])
@@ -296,9 +298,18 @@ def rank_program(g, core, T, topo):
     iota(D4, [[1, 16], [0, 4]])
     iota(EP, [[1, 4], [-1, 16]])
     iota(DI, [[0, 16], [512, 4]], base=512)
+    fill(V("bt", 0, 288), 0.0)
+    fill(V("kh", 0, 96), 2.0)
+    fill(V("kf", 16, 56), 0.0)
     for k, m in enumerate((15, 16, 3, 12, 1, 6, 18, 20, 17)):
         ts(col("ci", k + 1), col("ci", 0), m, A.bitwise_and)
-    cp(V("cf", 0, 10), V("ci", 0, 10))
+    ts(col("ci", 10), col("ci", 12), 48, A.bitwise_and)
+    ts(col("ci", 11), col("ci", 13), 192, A.bitwise_and)
+    fill(V("kh", 0, 64, 8), 0.0)
+    fill(V("kh", 34, 64, 8), 0.0)
+    fill(V("kh", 64, 96, 2), 0.0)
+    cp(V("cf", 0, 12), V("ci", 0, 12))
+    fill(V("ez", 0, 520), 0.0)
     P_, Qc, H16, Q3, Q12, Q1, Q6, Q18, Q20, Q17 = [col("cf", k) for k in range(10)]
     (OH0, OH1, OH2, OH3, NAT, RR, PA17, PA18, PA20, G1, T0, T1, T2, T3, T4, T5, T6, T7, T8, T9, LC, LM, CA, XB0, XB1, TOP, Q15, Q257,
      U0, U1, U2, U3, U4, NMID, HALF) = [col("cc", k) for k in range(35)]
@@ -308,56 +319,43 @@ def rank_program(g, core, T, topo):
     DIAG, KEEP16, HK, NK, POW, DUMP = [V("k64", 64 * k, 64 * k + 64) for k in range(6)]
     LT, KEEP32 = V("k64", 384, 512), V("k64", 512, 640)
     C16, DESC, GATE16, EC = [V("k64", 640 + 16 * k, 656 + 16 * k) for k in range(4)]
-    act(T0, Q12, 0.25)
-    act(PA18, Q18, 1.0, -9.0, ACT.Abs)
-    act(RR, Q3, 4.0, T0)
-    act(T1, Q1, -9.0, 1225.0)
-    act(NAT, RR, 16.0)
-    act(V("tm", 384, 448), XA, 0.0, 8.0)
-    act(V("tm", 320, 384), XA, -8.0, 8.0, ACT.Relu)
-    act(V("tx", 192, 256), XA, 0.0)
-    act(V("tm", 192, 256), XA, 0.0, 1.0)
-    act(V("tm", 320, 384), V("tm", 320, 384), 1.0, 4.0)
-    act(V("tx", 272, 288), V("tx", 384, 400))
-    act(V("tx", 288, 304), row(16), 0.0)
-    act(V("tx", 304, 320), row(16), 0.0, 1.0)
-    act(V("tm", 256, 272), V("tm", 320, 336), 1.0, 2.0)
-    act(V("tm", 272, 288), row(16), 0.0, 10.0)
-    act(V("tm", 288, 320), row(32), 0.0, 2.0)
     tt(XB, XA, XB, A.max)
+    ts(PERM, row(16), col("cf", 10), A.add, col("cf", 11), A.add)
     ts(V("cc", 0, 4), row(4), Q3, A.is_equal)
     ts(V("tx", 320, 384), XB, -1.0, A.add)
-    ts(PERM, row(16), NAT, A.add)
-    act(V("tx", 256, 272), V("tx", 320, 336))
+    act(V("tx", 288, 304), row(16), 0.0)
+    act(V("tx", 304, 320), row(16), 0.0, 1.0)
+    act(V("tx", 192, 256), row(64), 0.0)
+    act(V("tm", 384, 448), row(64), 0.0, 8.0)
+    act(V("tm", 192, 256), row(64), 0.0, 1.0)
+    act(V("tm", 272, 288), row(16), 0.0, 10.0)
+    act(V("tm", 288, 320), row(32), 0.0, 2.0)
+    act(V("tx", 272, 288), V("tx", 384, 400))
+    act(V("tm", 320, 384), XA, -8.0, 8.0, ACT.Relu)
+    act(PA18, Q18, 1.0, -9.0, ACT.Abs)
+    act(T1, Q1, -9.0, 1225.0)
+    act(V("tm", 320, 384), V("tm", 320, 384), 1.0, 4.0)
+    act(T0, Q12, 0.25)
     act(T2, PA18, -136.0, T1)
-    act(V("tx", 0, 192), V("tx", 256, 448))
-    act(G1, Qc, 8.0, T2)
-    act(V("tm", 0, 192), V("tm", 256, 448), 1.0, 1.0)
-    fill(V("bt", 0, 288), 0.0)
-    fill(V("kh", 0, 96), 2.0)
-    fill(V("kf", 16, 56), 0.0)
-    fill(V("kh", 0, 64, 8), 0.0)
-    fill(V("kh", 34, 64, 8), 0.0)
-    fill(V("kh", 64, 96, 2), 0.0)
-    fill(V("ez", 0, 520), 0.0)
-    TS_ = V("te", 256, 320)
-    SA, SB = V("wf", 0, 64), V("wf", 64, 128)
-    ts(SA, V("tx", 256, 320), OH1, A.mult)
-    ts(SB, V("tx", 320, 384), OH2, A.mult)
-    ts(TS_, V("tx", 384, 448), OH3, A.mult)
-    tt(SA, SA, SB, A.add)
-    ts(V("te", 0, 256), V("tx", 0, 256), OH0, A.mult)
-    tt(TS_, TS_, SA, A.add)
-    ts(V("ez", 3, 515, 4), row(128), P_, A.is_equal, 0.5, A.mult)
-    for k in range(4):
-        tt(V("te", 64 * k, 64 * k + 64), V("te", 64 * k, 64 * k + 64), TS_, A.add)
     act(T3, Q3, func=ACT.Sign)
     act(T4, Q12, 2.0, 7.0)
-    act(V("kf", 16, 22, 2), row(3), 0.0, G1)
+    act(V("tx", 256, 272), V("tx", 320, 336))
+    act(G1, Qc, 8.0, T2)
+    act(V("tm", 256, 272), V("tm", 320, 336), 1.0, 2.0)
     act(T5, Q12, 4.0, Q3)
+    act(V("tx", 0, 192), V("tx", 256, 448))
+    TS_ = V("te", 256, 320)
+    SA, SB = V("wf", 0, 64), V("wf", 64, 128)
+    ts(SB, V("tx", 320, 384), OH2, A.mult)
+    ts(TS_, V("tx", 384, 448), OH3, A.mult)
+    ts(SA, V("tx", 256, 320), OH1, A.mult)
+    tt(TS_, TS_, SB, A.add)
+    ts(V("ez", 3, 515, 4), row(128), P_, A.is_equal, 0.5, A.mult)
+    act(V("kf", 16, 22, 2), row(3), 0.0, G1)
     act(col("kf", 22), T3, 32.0, T4)
-    act(V("kf", 17, 22, 2), V("kf", 16, 22, 2), 1.0, 128.0)
+    act(RR, Q3, 4.0, T0)
     act(PA20, Q20, 1.0, -10.0, ACT.Abs)
+    act(V("kf", 17, 22, 2), V("kf", 16, 22, 2), 1.0, 128.0)
     act(T8, T5, 1.0, 200.0)
     act(T7, Q6, 0.5)
     act(T6, PA18, -40.0, 360.0)
@@ -366,10 +364,13 @@ def rank_program(g, core, T, topo):
     act(col("kf", 26), Q6, 8.0, T6)
     QU, SU = V("qu", 0, 128), V("su", 0, 128)
     QX, SX, Q0T, S0T = V("qx", 0, 256), V("sx", 0, 256), V("qt0", 0, 256), V("pt0", 0, 256)
-    quant(QU, SU, V("un", 0, 512))
     quant(QX, SX, V("xn", 0, 1024))
-    op("v", lambda: g.vector.tensor_copy(ap(Q0T).bitcast(dt.uint32), ap(QX).bitcast(dt.uint32).indirect(ap(PERM))), [Q0T], [QX, PERM])
-    op("a", lambda: g.scalar.activation(ap(S0T), ap(SX).indirect(ap(PERM)), ACT.Copy), [S0T], [SX, PERM])
+    quant(QU, SU, V("un", 0, 512))
+    for h in range(2):
+        qh, sh, ph = V("qt0", 128 * h, 128 * h + 128), V("pt0", 128 * h, 128 * h + 128), V("ku", 8 * h, 8 * h + 8)
+        op("v", lambda: g.vector.tensor_copy(ap(qh).bitcast(dt.uint32), ap(QX).bitcast(dt.uint32).indirect(ap(ph))), [qh], [QX, ph])
+        op("a", lambda: g.scalar.activation(ap(sh), ap(SX).indirect(ap(ph)), ACT.Copy), [sh], [SX, ph])
+    act(V("tm", 0, 192), V("tm", 256, 448), 1.0, 1.0)
     act(V("k64", 688, 704, 4), row(4), 0.0)
     for e in range(1, 4):
         act(V("k64", 688 + e, 704, 4), row(4), 0.0, 192.0 + 64 * e)
@@ -417,9 +418,10 @@ def rank_program(g, core, T, topo):
 
     def later():
         return [
-            lambda: cp(V("ku", 16, 28), V("kf", 16, 28)), lambda: ts(DIAG, D4, Qc, A.is_equal), lambda: ts(GATE16, row(16), Qc, A.is_ge),
-            lambda: fill(V("ft", 256, 512), 0.0), lambda: fill(V("ht", 256, 512), 0.0), lambda: cp(V("ku", 28, 56), V("kf", 28, 56))] + [
+            lambda: tt(TS_, TS_, SA, A.add), lambda: ts(V("te", 0, 256), V("tx", 0, 256), OH0, A.mult), lambda: cp(V("ku", 16, 28), V("kf", 16, 28))] + [
+            lambda k=k: tt(V("te", 64 * k, 64 * k + 64), V("te", 64 * k, 64 * k + 64), TS_, A.add) for k in range(4)] + [
             lambda b=b: quant(V("qe", 128 * b, 128 * b + 128), V("se", 128 * b, 128 * b + 128), V("ez", 3 - b, 515 - b)) for b in range(4)] + [
+            lambda: ts(DIAG, D4, Qc, A.is_equal), lambda: cp(V("ku", 28, 56), V("kf", 28, 56)), lambda: ts(GATE16, row(16), Qc, A.is_ge),
             lambda: scan(POW, HK, NK, A.mult, A.add), lambda: ts(DUMP, EP, 0.0, A.is_gt, Q257, A.mult), lambda: tt(DUMP, DUMP, DI, A.add)]
 
     ahead, behind = cores[(r + HOP[0]) % N], cores[(r - HOP[0]) % N]
@@ -481,7 +483,7 @@ def rank_program(g, core, T, topo):
         return [lambda b=b: tt(V("ff", 256 * b, 256 * b + 256), V("vl", 256 * b, 256 * b + 256), V("ps%d" % (b + 1), 0, 256), A.add)
                 for b in range(4)]
 
-    def entry(t, upto, cand, after=()):
+    def entry(t, upto):
         def named(k):
             return slot("mo" if k == r else "ml", k, t)
 
@@ -489,21 +491,22 @@ def rank_program(g, core, T, topo):
             v = named(k)
             return V(v[0], v[1], v[1] + 1)
         here = [maps(t)]
-        SELO, Z = V("selo", 0, 16), V("k64", 640, 644)
+        SELO, Z, sel = V("selo", 0, 16), V("k64", 640, 644), V("selo", 0, 2)
         if upto == 0:
-            return [lambda: wait("v", here[0])], cand, QU16
+            return [[lambda: wait("v", here[0])]], QU16
         if upto < 3:
-            return [lambda: ts(SELO, ind(Z if upto == 1 else named(1), first(0)), Qc, A.add, after=here)], cand, V("selo", 0, 2)
-        a = [lambda: cp(V("eu", 0, 16), ind(named(1), first(0)), here),
-             lambda: cp(V("cb", 0, 64), ind(Z if upto == 3 else named(3), named(2))),
-             lambda: ts(SELO, ind(V("cb", 0, 64), col("eu", 0)), Qc, A.add)]
-        b = []
-        for k in range(upto - 1, 3, -1):
-            o = V("ca", 64 * (k - 4), 64 * (k - 4) + 64)
-            b.append(lambda o=o, cand=cand, k=k: cp(o, ind(cand, named(k)), here + list(after)))
-            cand = o
-        b += [lambda: None] * 3
-        return [a[0], a[1], b[0], a[2], b[1], b[2]], cand, V("selo", 0, 2)
+            return [[lambda: ts(SELO, ind(Z if upto == 1 else named(1), first(0)), Qc, A.add, after=here)]], sel
+        CB, CC, CD = [V("cb", 64 * k, 64 * k + 64) for k in range(3)]
+        one_ = [lambda: cp(V("eu", 0, 16), ind(named(1), first(0)), here), lambda: cp(CB, ind(Z if upto == 3 else named(3), named(2)))]
+        if upto < 5:
+            return [one_, [lambda: ts(SELO, ind(CB, col("eu", 0)), Qc, A.add)]], sel
+        two_ = [lambda: cp(V("eu", 16, 32), ind(CB, col("eu", 0)))]
+        if upto == 5:
+            one_.append(lambda: cp(CD, ind(row(64), named(4))))
+        else:
+            one_.insert(0, lambda: cp(CC, ind(Z if upto == 6 else named(6), named(5)), here))
+            two_.insert(0, lambda: cp(CD, ind(CC, named(4))))
+        return [one_, two_, [lambda: ts(SELO, ind(CD, col("eu", 16)), Qc, A.add)]], sel
 
     def bodies(t, win, sel):
         if t < R - 1:
@@ -525,7 +528,8 @@ def rank_program(g, core, T, topo):
             for k in range(min(n, len(spare))):
                 spare.pop(0)()
         QT, PT = V("qt%d" % t, 0, 256), V("pt%d" % t, 0, 256)
-        mm(V("ps0", 0, 256), QU, SU, QT, PT)
+        for h, bank in enumerate(("ps0", "ps5")):
+            mm(V(bank, 0, 128), QU, SU, V(QT[0], 128 * h, 128 * h + 128), V(PT[0], 128 * h, 128 * h + 128))
 
         def unpack(QT, PT, after):
             for b in range(4):
@@ -533,10 +537,12 @@ def rank_program(g, core, T, topo):
         if t > 0:
             unpack(QT, PT, [])
         gap(4)
-        ts(V("bt", 16, 272), V("ps0", 0, 256), 0.0, A.is_gt)
-        gap()
-        turn(V("tt", 0, 256), V("bt", 16, 272))
-        turn(V("tt", 256, 544), V("bt", 0, 288))
+        ts(V("bt", 16, 144), V("ps0", 0, 128), 0.0, A.is_gt)
+        ts(V("bt", 144, 272), V("ps5", 0, 128), 0.0, A.is_gt)
+        turn(V("tt", 0, 128), V("bt", 16, 144))
+        turn(V("tt", 256, 384), V("bt", 0, 128))
+        turn(V("tt", 128, 256), V("bt", 144, 272))
+        turn(V("tt", 384, 544), V("bt", 128, 288))
         gap()
         if t > 0:
             for b in range(4):
@@ -547,8 +553,12 @@ def rank_program(g, core, T, topo):
         gap()
         cp(V("idx", 0, 4), V("sg", 7, 32, 8))
         tt(V("tmp", 0, 16), ind(V("sg", 0, 64), LMI), EC, A.add)
+        if t > 0:
+            spare += lasts() + [lambda: fetch(V("lu", 0, 16))]
+        gap()
         cp(V("eo", 16, 80), ind(V("te", 0, 256), V("idx", 0, 4)))
         cp(V("offm", 0, 16), V("tmp", 0, 16))
+        gap()
         turn(V("et", 0, 64), V("eo", 16, 80))
         turn(V("et", 64, 160), V("eo", 0, 96))
         act(V("xa", 128, 192), ind(V("tx", 0, 448), V("offm", 12, 16)))
@@ -565,6 +575,7 @@ def rank_program(g, core, T, topo):
             cp(V("xa", 64 * i - 64, 64 * i), ind(V("xa", 64 * i, 64 * i + 64), o))
             tt(V("mb", 64 * i, 64 * i + 64), ind(mk, o), V("ma", 64 * i, 64 * i + 64), A.add)
             mk = V("mb", 64 * i, 64 * i + 64)
+            gap(3 - i)
         for e in range(4):
             cp(V("yo", 16 + e, 80, 4), ind(V("xa", 0, 64), col("offa", 16 + 2 * e)))
         tt(V("mb", 0, 64), ind(mk, V("offa", 0, 4)), V("ma", 0, 64), A.add)
@@ -577,7 +588,7 @@ def rank_program(g, core, T, topo):
             unpack(V("qo", 0, 256), V("so", 0, 256), [("qo", 2 * len(off), {})])
             for b in range(4):
                 act(V("vv", 256 * b, 256 * b + 256), V("ps%d" % (b + 1), 0, 256))
-            spare += lasts()
+            spare[:] = lasts() + spare
         x, m = V("yo", 64, 80), V("dd", 48, 64)
         for i in (2, 1):
             o = col("offb", 4 * i)
@@ -598,18 +609,13 @@ def rank_program(g, core, T, topo):
         for i in (0, 1):
             cp(V("xc", 16 * i, 16 * i + 16), ind(x, o))
             tt(V("ub", 48 + 16 * i, 64 + 16 * i), ind(m, o), V("ub", 0, 16), A.add)
-            gap(2)
+            gap()
             x, m = V("xc", 16 * i, 16 * i + 16), V("ub", 48 + 16 * i, 64 + 16 * i)
         p = plans[t][r]
         mo = slot("mo", r, t)
         if p["first"] or p["dirs"]:
             wide = V(mo[0], 0, 16)
-            if r in HEADS:
-                ts(wide, ind(x, o), 16.0, A.mult)
-            elif r < 4:
-                cp(wide, ind(x, o))
-            else:
-                ts(wide, ind(x, o), 16.0, A.mult, Qc, A.add)
+            ts(wide, ind(x, o), 16.0 if r in HEADS or r == 4 else 1.0, A.mult)
         MK = V("ub", 80, 96)
         tt(MK, ind(m, o), V("ub", 0, 16), A.add)
         if p["first"]:
@@ -629,22 +635,26 @@ def rank_program(g, core, T, topo):
             fetch(V("luo", 0, 16), [("luo", len(off), {})])
             ts(XB0, Q12, 64.0, A.mult, Q3, A.add)
             fill(V("zt", 0, 512), 0.0)
+            fill(V("ft", 256, 512), 0.0)
+            fill(V("ht", 256, 512), 0.0)
             ts(XL, XP, XB0, A.add)
             fill(V("dh", 0, 320), 0.0)
             quant(V("lq0", 0, 128), V("ls0", 0, 128), V("zt", 0, 512))
-            run(sums())
-            theirs = [("cando", len(off), {})]
-            steps, win, sel = entry(t, (r - HOP[0]) % N, V("cando", 0, 64), theirs)
+            theirs, win, half = [("cando", len(off), {})], V("cando", 0, 64), sums()
+            steps, sel = entry(t, (r - HOP[0]) % N)
+            for s in steps:
+                run(s + half[:1])
+                half = half[1:]
+            run(half[:-1])
         else:
-            weave(lasts(), own[:5])
-            fetch(V("lu", 0, 16))
             if t == R - 1:
                 act(V("tn", 0, 1024), ind(V(old, 0, 1024), XM))
-            weave(own[5:], [lambda: None] * 3 + sums())
-            theirs = []
-            steps, win, sel = entry(t, r, CAND)
-        run(steps)
+            theirs, win, half = [], CAND, sums()
+            steps, sel = entry(t, r)
+            steps = [[]] * (3 - len(steps)) + steps
+            run(half[:1] + own[:2] + half[1:2] + own[2:10] + steps[0] + own[10:11] + steps[1] + own[11:] + steps[2] + half[2:3])
         cp(V("ll", 0, 16), ind(win, V(sel[0], sel[1], sel[1] + 1)), theirs)
+        run(half[-1:])
         op("v", lambda: g.vector.tensor_copy(ap(ind(V("sc", 32, 2368), V("ll", 0, 16))), ap(row(256))),
            [V("sc", 32, 2368)], [V("ll", 0, 16), row(256)])
         ub = bodies(t, win, sel) if t > 0 else []
@@ -657,11 +667,10 @@ def rank_program(g, core, T, topo):
         run(ub[2:3])
         for b in range(4):
             (act if b % 2 else cp)(V("ft", b, 256, 4), ind(V("ff", 256 * b, 256 * b + 256), FL))
-        run(ub[3:4])
         a = [384, 128, 512][t]
         fc, fs = V("qm", a, a + 128), V("sm", a, a + 128)
         quant(fc, fs, V("ft", 0, 512))
-        run(ub[4:])
+        run(ub[3:])
         wc, ws, lo, after = "qp", "sp", 0, [w_here]
         if t == 0:
             wc, ws, after = "qw", "sw", []
@@ -683,8 +692,8 @@ def rank_program(g, core, T, topo):
             after, lo = [tok], 64
         if t == 0:
             act(V(old, 0, 1024), ind(V("xn", 0, 1024), XL))
-            steps, win, sel = entry(t, r, CAND)
-            run(steps + bodies(t, win, sel))
+            steps, sel = entry(t, r)
+            run(sum(steps, []) + bodies(t, CAND, sel))
         if t == 1:
             iota(XQ, [[4, 4], [16, 4], [256, 4]])
             quant(V("qv", 0, 128), V("sv", 0, 128), V("vn", 0, 512))
@@ -702,15 +711,18 @@ def rank_program(g, core, T, topo):
             store("s", T.ol[:], T.olb[0:128:16, 0:64], V("olb", 0, 64))
         for b in range(4):
             tt(V(new, b, 1024, 4), ind(V("dh", 80 * b, 80 * b + 80), UL), V(old, b, 1024, 4), A.add)
-        quant(V("qt%d" % (t + 1), 0, 256), V("pt%d" % (t + 1), 0, 256), V(new, 0, 1024))
+        for h in range(2):
+            quant(V("qt%d" % (t + 1), 128 * h, 128 * h + 128), V("pt%d" % (t + 1), 128 * h, 128 * h + 128), V(new, 512 * h, 512 * h + 512))
         old, new = new, "ta" if new == "tb" else "tb"
 
     QN_, SN = V("qt3", 0, 256), V("pt3", 0, 256)
-    mm(V("ps1", 0, 256), V("qv", 0, 128), V("sv", 0, 128), QN_, SN)
+    for h in range(2):
+        mm(V("ps%d" % (h + 1), 0, 128), V("qv", 0, 128), V("sv", 0, 128), V("qt3", 128 * h, 128 * h + 128), V("pt3", 128 * h, 128 * h + 128))
     store("s", T.oc[:], u8(ap(QN_)), QN_)
     for k in range(4):
         store("a", T.osc[4 * k:4 * k + 4, 0:256], T.pt3[32 * k:32 * k + 4, 0:256], SN)
-    cp(V("ys", 0, 256), V("ps1", 0, 256))
+    for h in range(2):
+        cp(V("ys", 128 * h, 128 * h + 128), V("ps%d" % (h + 1), 0, 128))
     store("s", T.y[:], T.ys[:, 0:256], V("ys", 0, 256))
     for q in ("v", "a", "p", "gp"):
         g.wait_ge(T.sem[q], count[q])

@@ -5,7 +5,6 @@ A = AluOpType
 ACT = ActivationFunctionType
 N, C, R, HOP = 8, 256, 3, [2, 5, 3]
 Q, S, BF, F, I, U = "float8_e4m3fn_x4", "uint8", "bfloat16", "float32", "int32", "uint16"
-HEADS = (1, 3, 6)
 
 
 def _sb(n, d):
@@ -19,14 +18,14 @@ SCRATCH = {
     "rq": _sb(256, Q), "rs": _sb(256, S), "ez": _sb(520, BF), "qe": _sb(512, Q), "se": _sb(512, S),
     "qm": _sb(768, Q), "sm": _sb(768, S), "zt": _sb(512, BF), "ft": _sb(512, BF), "ht": _sb(512, BF),
     "ci": _sb(16, I), "kf": _sb(64, F), "cf": _sb(16, F), "cc": _sb(40, F), "ku": _sb(192, U), "r256": _sb(256, F), "jrow": _sb(256, F),
-    "io3": _sb(480, F), "k64": _sb(768, F), "kh": _sb(96, BF), "tx": _sb(448, BF), "tm": _sb(448, BF), "te": _sb(320, BF),
+    "tc": _sb(448, BF), "na": _sb(448, BF), "nb": _sb(176, BF), "io3": _sb(544, F), "k64": _sb(768, F), "kh": _sb(96, BF), "tx": _sb(448, BF), "tm": _sb(448, BF), "te": _sb(320, BF),
     "bt": _sb(288, BF), "tt": _sb(544, BF), "gb": _sb(96, BF), "sg": _sb(96, F), "idx": _sb(4, U), "tmp": _sb(16, F), "offm": _sb(16, U),
     "eo": _sb(96, BF), "et": _sb(160, BF), "offa": _sb(32, U), "xa": _sb(192, BF), "ma": _sb(256, F), "mb": _sb(192, F),
     "yo": _sb(96, BF), "yt": _sb(160, BF), "offb": _sb(32, U), "dd": _sb(64, F), "xb": _sb(48, BF), "ub": _sb(112, F),
-    "ye": _sb(32, F), "offc": _sb(2, U), "xc": _sb(32, BF),
+    "ye": _sb(32, F), "offc": _sb(4, U), "offr": _sb(32, U), "xc": _sb(128, BF),
     "la": _sb(64, F), "lu": _sb(16, U), "luo": _sb(16, U), "wf": _sb(384, F), "wi": _sb(64, I), "wp": _sb(384, F),
-    "cand": _sb(64, F), "cando": _sb(64, F), "cb": _sb(192, BF), "eu": _sb(32, U), "selo": _sb(16, U), "ll": _sb(16, U),
-    "sc": _sb(2368, F), "st": _sb(160, F), "fl": _sb(16, U), "vv": _sb(1024, BF), "vl": _sb(1024, BF), "ff": _sb(1024, BF),
+    "cand": _sb(64, F), "cando": _sb(64, F), "ca": _sb(192, F), "cb": _sb(192, BF), "eu": _sb(48, U), "selo": _sb(16, U), "ll": _sb(16, U),
+    "sc": _sb(2368, BF), "st": _sb(160, BF), "fl": _sb(16, U), "vv": _sb(1024, BF), "vl": _sb(1024, BF), "ff": _sb(1024, BF),
     "dh": _sb(512, BF), "ui": _sb(96, I), "ul": _sb(16, U), "ys": _sb(256, F), "olb": _sb(64, F),
 }
 for _t in range(R):
@@ -34,15 +33,15 @@ for _t in range(R):
     SCRATCH["pt%d" % _t] = _sb(256, S)
     SCRATCH["lq%d" % _t] = _sb(192, Q)
     SCRATCH["ls%d" % _t] = _sb(384, S)
-    for _k, _d in (("u", U), ("b", BF)):
-        SCRATCH["mo%s%d" % (_k, _t)] = _sb(16, _d)
-        SCRATCH["mr%s%d" % (_k, _t)] = _sb(4, _d)
-        SCRATCH["ml%s%d" % (_k, _t)] = _sb(128, _d)
+for _k, _d in (("u", U), ("b", BF)):
+    SCRATCH["mo" + _k] = _sb(16 * R, _d)
+    SCRATCH["mr" + _k] = _sb(16 * R, _d)
+    SCRATCH["ml" + _k] = _sb(16 * N * R, _d)
 SCRATCH["qt3"] = _sb(256, Q)
 SCRATCH["pt3"] = _sb(256, S)
 for _t in range(8):
     SCRATCH["ps%d" % _t] = ("psum", [128, 512], F)
-SEMAPHORES = ["v", "a", "p", "gp", "dx", "du", "dv", "dwc", "dws", "out", "sent", "wp", "rw", "qo", "luo", "cando",
+SEMAPHORES = ["v", "a", "p", "gp", "dx", "du", "dv", "dwc", "dws", "out", "sent", "wp", "rw", "qo", "luo", "cando", "near",
               "m0", "m1", "m2", "r0", "r1", "r2", "e0", "e1", "e2"]
 
 
@@ -82,13 +81,17 @@ def plan(r, t, cores, topo):
     off = topo.engines(c, cores[(r + HOP[0]) % N])
     on = topo.engines(c, near[0])
     use = near[:len(cross)]
+    if t > 0 and len(cross) > len(near):
+        cross, direct = direct[len(near):] + cross, direct[:len(near)]
+        use = (near + far)[:len(cross)]
     first = list(zip(use, share(on, len(use)))) if use else []
     dirs = list(zip(direct, share(off, len(direct)))) if direct else []
     second = {}
     for i, k in enumerate(use):
         ds = cross[i::len(use)]
         second[k] = list(zip(ds, share(topo.engines(k, cores[ds[0]]), len(ds))))
-    return {"wd": wd, "near": near, "far": far, "first": first, "dirs": dirs, "second": second, "off": off}
+    return {"wd": wd, "near": near, "far": far, "first": first, "dirs": dirs, "second": second, "off": off,
+            "inner": share([e for e in on if e not in off], len(near))}
 
 
 def transfer(topo, src_core, dst_core, engines, sem, src, dst):
@@ -100,10 +103,21 @@ def u8(ap):
     return ap.bitcast(dt.uint8)
 
 
-def slot(kind, k, t):
-    name = "%s%s%d" % (kind, "b" if k in HEADS else "u", t)
-    at = 0 if kind != "ml" else 16 * k if k in HEADS else 4 * k
-    return (name, at, at + 4, 1)
+def slot(kind, k, t, d):
+    at = 16 * (N * t + k) if kind == "ml" else 16 * t
+    return (kind + ("b" if head(k, t, d) else "u"), at, at + 4, 1)
+
+
+def last(k, t, d):
+    return t == R - 1 and k > 3 and d == k + 1
+
+
+def head(k, t, d):
+    return k in (1, 3) or (k == 6 and t == 0) or last(k, t, d)
+
+
+def landed(T, k, t, d):
+    return T.sem["near" if last(k, t, d) else "m%d" % t]
 
 
 def relay_program(g, core, T, topo, r):
@@ -113,7 +127,7 @@ def relay_program(g, core, T, topo, r):
     half = len(topo.engines(cores[r], core)) // 2
     if core in p["far"] or core in p["near"]:
         eng = topo.engines(core, p["wd"])
-        g.wait_ge(T.sem.rw, half)
+        g.wait_ge(T.sem.rw, half if core in p["far"] else len(p["inner"][p["near"].index(core)]))
         if core in p["far"]:
             k = p["far"].index(core)
             tr = transfer(topo, core, p["wd"], eng, T.sem.wp, u8(T.rq[:, 0:256]), u8(T.qp[:, 256 * k:256 * k + 256]))
@@ -126,9 +140,10 @@ def relay_program(g, core, T, topo, r):
         p = plan(r, t, cores, topo)
         if core in p["second"]:
             g.wait_ge(T.sem["r%d" % t], len(dict(p["first"])[core]))
-            a, b = slot("mr", r, t), slot("ml", r, t)
-            trs = [transfer(topo, core, cores[d], e, T.sem["m%d" % t], T[a[0]][:, a[1]:a[2]], T[b[0]][:, b[1]:b[2]])
-                   for d, e in p["second"][core]]
+            trs = []
+            for d, e in p["second"][core]:
+                a, b = slot("mr", r, t, d), slot("ml", r, t, d)
+                trs.append(transfer(topo, core, cores[d], e, landed(T, r, t, d), T[a[0]][:, a[1]:a[2]], T[b[0]][:, b[1]:b[2]]))
             g.remote_dma_fused(trs, local_sem=T.sem.sent)
             sent += sum(len(e) for d, e in p["second"][core])
     if sent:
@@ -225,8 +240,8 @@ def rank_program(g, core, T, topo):
     def fill(o, c):
         return op("v", lambda: g.vector.memset(ap(o), c), [o], [])
 
-    def scan(o, a, b, o0, o1):
-        return op("v", lambda: g.vector.tensor_tensor_scan(ap(o), ap(a), ap(b), 0.0, o0, o1), [o], [a, b])
+    def scan(o, a, b, o0, o1, first=0.0):
+        return op("v", lambda: g.vector.tensor_tensor_scan(ap(o), ap(a), ap(b), arg(first), o0, o1), [o], [a, b, first])
 
     def turn(o, i):
         return op("v", lambda: g.vector.transpose(ap(o), ap(i)), [o], [i])
@@ -281,23 +296,24 @@ def rank_program(g, core, T, topo):
 
     load("s", "dx", V("xn", 0, 1024), T.x[:])
     load("a", "du", V("un", 0, 512), T.u[:])
-    load("a", "dws", V("sw", 0, 512), T.ws[:])
+    wait("s", ("dx", 16, {}))
+    wait("s", ("du", 16, {}))
+    load("s", "dws", V("sw", 0, 512), T.ws[:])
+    load("s", "dwc", V("qw", 0, 512), T.wc[:], codes=True)
 
     iota(V("ci", 0, 1), [[0, 1]], 1, flag=False)
     iota(V("r256", 0, 64), [[1, 64]])
     iota(V("ci", 12, 13), [[0, 1]], 4, flag=False)
     iota(V("ci", 13, 14), [[0, 1]], 64, flag=False)
-    X3, XA, XB, KR = V("tx", 384, 448), V("io3", 0, 64), V("io3", 64, 128), V("io3", 128, 160)
+    X3, XA, XB, KR = V("tx", 384, 448), V("io3", 0, 64), V("io3", 64, 128), V("io3", 480, 544)
     I16, D4, EP, XP, XQ, DI = [V("io3", 160 + 64 * k, 224 + 64 * k) for k in range(4)] + [V("wp", 0, 64), V("io3", 416, 480)]
     iota(X3, [[0, 16], [1, 4]])
     iota(XA, [[0, 4], [1, 4], [0, 4]])
     iota(XB, [[0, 4], [-4, 4], [1, 4]], base=1)
+    iota(V("k64", 688, 704), [[0, 4], [64, 4]], base=192)
+    iota(V("eo", 0, 96), [[0, 96]])
     iota(V("r256", 64, 256), [[1, 192]], base=64)
-    iota(I16, [[0, 4], [1, 16]])
-    iota(KR, [[16, 2], [1, 4], [4, 4]])
     iota(D4, [[1, 16], [0, 4]])
-    iota(EP, [[1, 4], [-1, 16]])
-    iota(DI, [[0, 16], [512, 4]], base=512)
     fill(V("bt", 0, 288), 0.0)
     fill(V("kh", 0, 96), 2.0)
     fill(V("kf", 16, 56), 0.0)
@@ -312,17 +328,22 @@ def rank_program(g, core, T, topo):
     fill(V("ez", 0, 520), 0.0)
     P_, Qc, H16, Q3, Q12, Q1, Q6, Q18, Q20, Q17 = [col("cf", k) for k in range(10)]
     (OH0, OH1, OH2, OH3, NAT, RR, PA17, PA18, PA20, G1, T0, T1, T2, T3, T4, T5, T6, T7, T8, T9, LC, LM, CA, XB0, XB1, TOP, Q15, Q257,
-     U0, U1, U2, U3, U4, NMID, HALF) = [col("cc", k) for k in range(35)]
+     U0, U1, U2, U3, U4, NMID, HALF, CD) = [col("cc", k) for k in range(36)]
     PERM, LG, LMI, LA, LB, GL, PC, REP, REPT, REPK, NL, QU16, XL, XM = (
         V("ku", 0, 16), V("ku", 16, 22), V("ku", 22, 23), V("ku", 24, 26), V("ku", 26, 27), V("ku", 28, 29), V("ku", 30, 34),
         V("ku", 34, 38), V("ku", 38, 46), V("ku", 46, 50), V("ku", 50, 51), V("ku", 52, 54), V("ku", 64, 128), V("ku", 128, 192))
     DIAG, KEEP16, HK, NK, POW, DUMP = [V("k64", 64 * k, 64 * k + 64) for k in range(6)]
-    LT, KEEP32 = V("k64", 384, 512), V("k64", 512, 640)
+    LT, ONES = V("k64", 384, 448), V("k64", 448, 464)
     C16, DESC, GATE16, EC = [V("k64", 640 + 16 * k, 656 + 16 * k) for k in range(4)]
-    tt(XB, XA, XB, A.max)
     ts(PERM, row(16), col("cf", 10), A.add, col("cf", 11), A.add)
+    tt(XB, XA, XB, A.max)
     ts(V("cc", 0, 4), row(4), Q3, A.is_equal)
+    ts(V("ez", 3, 259, 4), row(64), P_, A.is_equal, 0.5, A.mult)
     ts(V("tx", 320, 384), XB, -1.0, A.add)
+    ts(GATE16, row(16), Qc, A.is_ge)
+    act(V("k64", 128, 144), row(16), 0.0, 0.5)
+    act(V("k64", 192, 208), row(16), 0.0)
+    scan(V("k64", 256, 272), V("k64", 128, 144), V("k64", 192, 208), A.mult, A.add, 1.0)
     act(V("tx", 288, 304), row(16), 0.0)
     act(V("tx", 304, 320), row(16), 0.0, 1.0)
     act(V("tx", 192, 256), row(64), 0.0)
@@ -339,90 +360,84 @@ def rank_program(g, core, T, topo):
     act(T2, PA18, -136.0, T1)
     act(T3, Q3, func=ACT.Sign)
     act(T4, Q12, 2.0, 7.0)
-    act(V("tx", 256, 272), V("tx", 320, 336))
     act(G1, Qc, 8.0, T2)
+    act(V("tx", 256, 272), V("tx", 320, 336))
+    act(V("kf", 16, 22, 2), row(3), 0.0, G1)
+    act(col("kf", 22), T3, 32.0, T4)
     act(V("tm", 256, 272), V("tm", 320, 336), 1.0, 2.0)
-    act(T5, Q12, 4.0, Q3)
     act(V("tx", 0, 192), V("tx", 256, 448))
     TS_ = V("te", 256, 320)
     SA, SB = V("wf", 0, 64), V("wf", 64, 128)
-    ts(SB, V("tx", 320, 384), OH2, A.mult)
-    ts(TS_, V("tx", 384, 448), OH3, A.mult)
-    ts(SA, V("tx", 256, 320), OH1, A.mult)
-    tt(TS_, TS_, SB, A.add)
-    ts(V("ez", 3, 515, 4), row(128), P_, A.is_equal, 0.5, A.mult)
-    act(V("kf", 16, 22, 2), row(3), 0.0, G1)
-    act(col("kf", 22), T3, 32.0, T4)
-    act(RR, Q3, 4.0, T0)
-    act(PA20, Q20, 1.0, -10.0, ACT.Abs)
-    act(V("kf", 17, 22, 2), V("kf", 16, 22, 2), 1.0, 128.0)
-    act(T8, T5, 1.0, 200.0)
-    act(T7, Q6, 0.5)
-    act(T6, PA18, -40.0, 360.0)
-    act(col("kf", 24), PA20, -20.0, T8)
-    act(col("kf", 25), H16, 5.0, T7)
-    act(col("kf", 26), Q6, 8.0, T6)
     QU, SU = V("qu", 0, 128), V("su", 0, 128)
     QX, SX, Q0T, S0T = V("qx", 0, 256), V("sx", 0, 256), V("qt0", 0, 256), V("pt0", 0, 256)
     quant(QX, SX, V("xn", 0, 1024))
     quant(QU, SU, V("un", 0, 512))
+    act(SA, V("tx", 256, 320), OH1)
     for h in range(2):
         qh, sh, ph = V("qt0", 128 * h, 128 * h + 128), V("pt0", 128 * h, 128 * h + 128), V("ku", 8 * h, 8 * h + 8)
         op("v", lambda: g.vector.tensor_copy(ap(qh).bitcast(dt.uint32), ap(QX).bitcast(dt.uint32).indirect(ap(ph))), [qh], [QX, ph])
         op("a", lambda: g.scalar.activation(ap(sh), ap(SX).indirect(ap(ph)), ACT.Copy), [sh], [SX, ph])
+    act(V("kf", 17, 22, 2), V("kf", 16, 22, 2), 1.0, 128.0)
+    act(T5, Q12, 4.0, Q3)
+    act(PA20, Q20, 1.0, -10.0, ACT.Abs)
+    act(T7, Q6, 0.5)
+    act(T8, T5, 1.0, 200.0)
+    act(T6, PA18, -40.0, 360.0)
+    act(col("kf", 24), PA20, -20.0, T8)
+    act(col("kf", 25), H16, 5.0, T7)
+    act(col("kf", 26), Q6, 8.0, T6)
     act(V("tm", 0, 192), V("tm", 256, 448), 1.0, 1.0)
     act(V("k64", 688, 704, 4), row(4), 0.0)
-    for e in range(1, 4):
-        act(V("k64", 688 + e, 704, 4), row(4), 0.0, 192.0 + 64 * e)
-    act(V("eo", 0, 96), row(96), 0.0)
     act(T9, Q3, 16.0, T0)
+    act(RR, Q3, 4.0, T0)
     act(PA17, Q17, 1.0, -8.5, ACT.Abs)
     act(U0, Q3, 16.0, 680.0)
     act(V("kf", 30, 34), row(4), 4.0, T9)
     act(col("kf", 28), PA17, -80.0, U0)
-    act(V("kf", 34, 38), row(4))
-    act(V("kf", 38, 46, 2), row(4), 16.0, 15.0)
-    act(V("kf", 39, 46, 2), row(4), 16.0, 15.0)
-    act(V("kf", 46, 50), row(4), 32.0, 31.0)
+    act(V("kf", 34, 46), row(12))
+    act(V("tc", 320, 384), XA, -1.0, 1.0, ACT.Relu)
+    for a, b, c in ((384, 448, 1.0), (272, 288, 2.0), (288, 320, 1.0)):
+        act(V("tc", a, b), row(b - a), 0.0, c)
+    act(V("tc", 320, 384), V("tc", 320, 384), 1.0, 1.0)
+    act(V("tc", 192, 256), row(64), 0.0, 1.0)
+    act(V("yo", 0, 96), row(96), 0.0)
     act(col("kf", 50), RR, 1.0, H16)
     act(V("kf", 52, 54), row(2), 0.0, Qc)
-    act(V("yo", 0, 96), row(96), 0.0)
+    act(V("tc", 256, 272), V("tc", 320, 336), 1.0, 1.0)
     act(TOP, Q12, 1.0, -11.0, ACT.Relu)
     act(U1, Qc, 4.0, -56.0)
-    act(DESC, row(16), -4.0, 60.0)
-    act(U2, Q12, 1.0, U1)
-    act(KEEP16, I16, func=ACT.Sign)
-    act(CA, TOP, -16.0, U2)
-    act(HK, KEEP16, 0.5)
-    act(NK, KEEP16, -0.5, 0.5)
+    act(V("tc", 0, 192), V("tc", 256, 448), 1.0, 1.0)
 
     def more():
+        act(CD, Qc, 4.0, -60.0)
+        act(DESC, row(16), -4.0, 60.0)
+        act(U2, Q12, 1.0, U1)
+        act(V("k64", 272, 288), V("k64", 256, 272))
+        act(Q257, Qc, -257.0, 257.0, ACT.Relu)
+        act(CA, TOP, -16.0, U2)
         act(Q15, Qc, 1.0, -14.0, ACT.Relu)
         act(U3, TOP, -15.0, -252.0)
         act(C16, row(16), 16.0)
+        act(V("k64", 288, 320), V("k64", 256, 288))
+        act(U4, Q257, -1.0, 512.0)
         act(LC, Q15, 267.0, U3)
         act(LM, Q15, -1000.0, 1255.0)
-        act(U4, RR, -0.5, -8.0)
-        act(HALF, RR, -0.5, 8.0)
-        act(NMID, H16, -1.0, U4)
-        act(Q257, Qc, -257.0, 257.0, ACT.Relu)
-        act(V("k64", 416, 448), KR, 1.0, NMID, ACT.Abs)
-        act(KEEP32, row(128), func=ACT.Sign)
-        act(V("k64", 448, 480), V("k64", 416, 448), -1.0, HALF, ACT.Relu)
-        act(V("k64", 544, 640, 32), row(3), 0.0)
-        act(V("k64", 384, 416), V("k64", 448, 480), func=ACT.Sign)
-        act(V("sc", 16, 112), row(96), 0.0)
-        act(V("k64", 416, 448), V("k64", 384, 416))
-        act(V("k64", 448, 480), V("k64", 384, 416))
-        act(V("k64", 480, 512), V("k64", 384, 416))
+        act(U3, Q257, 1.0, 512.0)
+        act(V("sc", 16, 128), row(112), 0.0)
+
+    def spread_(k):
+        tt(V("te", 64 * k, 64 * k + 64), V("te", 64 * k, 64 * k + 64), TS_, A.add)
 
     def later():
         return [
-            lambda: tt(TS_, TS_, SA, A.add), lambda: ts(V("te", 0, 256), V("tx", 0, 256), OH0, A.mult), lambda: cp(V("ku", 16, 28), V("kf", 16, 28))] + [
-            lambda k=k: tt(V("te", 64 * k, 64 * k + 64), V("te", 64 * k, 64 * k + 64), TS_, A.add) for k in range(4)] + [
+            lambda: [ts(SB, V("tx", 320, 384), OH2, A.mult), ts(TS_, V("tx", 384, 448), OH3, A.mult)],
+            lambda: ts(V("te", 0, 256), V("tx", 0, 256), OH0, A.mult), lambda: tt(SA, SA, SB, A.add),
+            lambda: cp(V("ku", 16, 22), V("kf", 16, 22)), lambda: tt(TS_, TS_, SA, A.add),
+            lambda: [spread_(0), spread_(1)], lambda: [cp(V("ku", 22, 28), V("kf", 22, 28)), spread_(2)],
+            lambda: [spread_(3), ts(V("ez", 259, 515, 4), V("r256", 64, 128), P_, A.is_equal, 0.5, A.mult)]] + [
             lambda b=b: quant(V("qe", 128 * b, 128 * b + 128), V("se", 128 * b, 128 * b + 128), V("ez", 3 - b, 515 - b)) for b in range(4)] + [
-            lambda: ts(DIAG, D4, Qc, A.is_equal), lambda: cp(V("ku", 28, 56), V("kf", 28, 56)), lambda: ts(GATE16, row(16), Qc, A.is_ge),
-            lambda: scan(POW, HK, NK, A.mult, A.add), lambda: ts(DUMP, EP, 0.0, A.is_gt, Q257, A.mult), lambda: tt(DUMP, DUMP, DI, A.add)]
+            lambda: [ts(DIAG, D4, Qc, A.is_equal), cp(V("ku", 28, 56), V("kf", 28, 56))],
+            lambda: ts(LT, KR, RR, A.is_lt)]
 
     ahead, behind = cores[(r + HOP[0]) % N], cores[(r - HOP[0]) % N]
     off = me["off"]
@@ -433,24 +448,26 @@ def rank_program(g, core, T, topo):
     def one(to, sem, src, dst, v):
         send([transfer(topo, core, to, off, T.sem[sem], src, dst)], [v], len(off))
 
-    send([transfer(topo, core, k, two[i], T.sem.rw, T.sw[:, 256 * i:256 * i + 256], T.rs[:, 0:256]) for i, k in enumerate(me["near"])],
-         [V("sw", 0, 512)], len(on))
+    iota(KR, [[1, 4], [4, 4], [0, 4]])
     one(ahead, "qo", u8(ap(Q0T)), u8(T.qo[:, 0:256]), Q0T)
     one(ahead, "qo", ap(S0T), T.so[:, 0:256], S0T)
+    send([transfer(topo, core, k, me["inner"][i], T.sem.rw, T.sw[:, 256 * i:256 * i + 256], T.rs[:, 0:256]) for i, k in enumerate(me["near"])],
+         [V("sw", 0, 512)], sum(len(e) for e in me["inner"]))
+    iota(DUMP, [[0, 16], [512, 4]], base=512)
+    iota(V("k64", 464, 528), [[0, 64]], base=512)
     iota(XP, [[4, 16], [64, 4]])
-    iota(V("jrow", 0, 256), [[1, 16], [16, 4], [64, 4]])
-    wait("s", ("qo", 2 * len(off), {}))
-    load("s", "dwc", V("qw", 0, 512), T.wc[:], codes=True)
+    wait("s", ("cando", len(off), {}))
     load("s", "dv", V("vn", 0, 512), T.v[:])
     src = plans[0][(r + HOP[2]) % N]
     w_here = ("wp", sum(len(topo.engines(k, core)) for k in src["near"] + src["far"]), {})
 
-    def maps(t):
+    def maps(t, near=False):
         n = 0
-        for p in plans[t]:
-            n += sum(len(e) for d, e in p["dirs"] if d == r)
-            n += sum(len(e) for rel in p["second"].values() for d, e in rel if d == r)
-        return ("m%d" % t, n, {})
+        for k, p in enumerate(plans[t]):
+            if last(k, t, r) == near:
+                n += sum(len(e) for d, e in p["dirs"] if d == r)
+                n += sum(len(e) for rel in p["second"].values() for d, e in rel if d == r)
+        return ("near" if near else "m%d" % t, n, {})
 
     ES = [(V("qe", 128 * b, 128 * b + 128), V("se", 128 * b, 128 * b + 128)) for b in range(4)]
 
@@ -468,24 +485,21 @@ def rank_program(g, core, T, topo):
         for b in range(4):
             act(V("vl", 256 * b, 256 * b + 256), ind(V("vv", 256 * b, 256 * b + 256), lu), after=after)
 
-    def lists(mk):
-        W0, BITS, NB, LCN, D1, LP = [V("wf", 64 * k, 64 * k + 64) for k in range(6)]
+    def lists(mk, before_):
+        W0, BITS, NB, LCN, D1 = [V("wf", 64 * k, 64 * k + 64) for k in range(5)]
         RI = V("wi", 0, 64)
-        TA, TB, TC = [V("wp", 128 * k, 128 * k + 128) for k in range(3)]
-        return [lambda: tt(W0, ind(mk, REP), POW, A.mult), lambda: tt(RI, ind(mk, REP), POW, A.mult),
-                lambda: tt(BITS, RI, W0, A.is_gt), lambda: tt(NB, RI, W0, A.is_lt),
-                lambda: scan(LCN, KEEP16, BITS, A.mult, A.add), lambda: tt(D1, NB, DUMP, A.mult),
-                lambda: tt(TA, ind(LCN, REPT), LT, A.mult), lambda: tt(LP, LCN, D1, A.add),
-                lambda: turn(TB, TA), lambda: ts(LP, LP, -1.0, A.add),
-                lambda: scan(TC, KEEP32, TB, A.mult, A.add), lambda: tt(V("cand", 0, 64), ind(TC, REPK), LP, A.add)]
+        count_ = [lambda e=e: scan(V("wf", 192 + 16 * e, 208 + 16 * e), V("k64", 464 + 16 * e, 480 + 16 * e), V("wf", 64 + 16 * e, 80 + 16 * e),
+                                   A.add, A.add, col(before_[0], before_[1] + e)) for e in range(4)]
+        return [[lambda: tt(W0, mk, POW, A.mult), lambda: tt(RI, mk, POW, A.mult)], [lambda: tt(BITS, RI, W0, A.is_gt)],
+                [lambda: tt(D1, BITS, DUMP, A.mult)] + count_, [lambda: tt(V("cand", 0, 64), LCN, D1, A.subtract)]]
 
     def sums():
         return [lambda b=b: tt(V("ff", 256 * b, 256 * b + 256), V("vl", 256 * b, 256 * b + 256), V("ps%d" % (b + 1), 0, 256), A.add)
                 for b in range(4)]
 
-    def entry(t, upto):
+    def entry(t, upto, cand):
         def named(k):
-            return slot("mo" if k == r else "ml", k, t)
+            return slot("mo" if k == r else "ml", k, t, r)
 
         def first(k):
             v = named(k)
@@ -493,27 +507,44 @@ def rank_program(g, core, T, topo):
         here = [maps(t)]
         SELO, Z, sel = V("selo", 0, 16), V("k64", 640, 644), V("selo", 0, 2)
         if upto == 0:
-            return [[lambda: wait("v", here[0])]], QU16
+            return [[lambda: wait("v", here[0])]], cand, QU16
         if upto < 3:
-            return [[lambda: ts(SELO, ind(Z if upto == 1 else named(1), first(0)), Qc, A.add, after=here)]], sel
+            return [[lambda: ts(SELO, ind(Z if upto == 1 else named(1), first(0)), Qc, A.add, after=here)]], cand, sel
         CB, CC, CD = [V("cb", 64 * k, 64 * k + 64) for k in range(3)]
-        one_ = [lambda: cp(V("eu", 0, 16), ind(named(1), first(0)), here), lambda: cp(CB, ind(Z if upto == 3 else named(3), named(2)))]
-        if upto < 5:
-            return [one_, [lambda: ts(SELO, ind(CB, col("eu", 0)), Qc, A.add)]], sel
+        join = act if t > 0 else cp
+        one_ = [lambda: cp(V("eu", 0, 16), ind(named(1), first(0)), here), lambda: join(CB, ind(Z if upto == 3 else named(3), named(2)), after=here)]
+        if last(upto - 1, t, r):
+            E2, E4, E6 = [V("eu", 16 * k, 16 * k + 16) for k in range(3)]
+            if upto == 6:
+                one_.append(lambda: act(CD, ind(row(64), named(4))))
+            if upto == 7:
+                one_ += [lambda: act(CC, ind(Z, named(5))), lambda: act(CD, ind(CC, named(4)))]
+            steps = [one_, [lambda: ts(E4, ind(CB, col("eu", 0)), 1.0 if upto > 5 else 0.0625, A.mult)]]
+            if upto > 5:
+                steps.append([lambda: ts(E6, ind(CD, col("eu", 16)), 0.0625, A.mult)])
+            steps.append([lambda: ts(SELO, ind(named(upto - 1), col("eu", 16 * len(steps) - 32)), Qc, A.add, after=[maps(t, True)])])
+            return steps, cand, sel
+        if upto < 5 or t > 0:
+            steps = [one_, [lambda: ts(SELO, ind(CB, col("eu", 0)), Qc, A.add)], []]
+            for i, k in enumerate(range(upto - 1, 3, -1)):
+                o = V("ca", 64 * i, 64 * i + 64)
+                steps[i].insert(0, lambda o=o, c=cand, k=k: cp(o, ind(c, named(k)), here))
+                cand = o
+            return [s for s in steps if s], cand, sel
         two_ = [lambda: cp(V("eu", 16, 32), ind(CB, col("eu", 0)))]
         if upto == 5:
-            one_.append(lambda: cp(CD, ind(row(64), named(4))))
+            one_.append(lambda: join(CD, ind(row(64), named(4))))
         else:
-            one_.insert(0, lambda: cp(CC, ind(Z if upto == 6 else named(6), named(5)), here))
-            two_.insert(0, lambda: cp(CD, ind(CC, named(4))))
-        return [one_, two_, [lambda: ts(SELO, ind(CD, col("eu", 16)), Qc, A.add)]], sel
+            one_.insert(0, lambda: join(CC, ind(Z if upto == 6 else named(6), named(5)), after=here))
+            (one_ if t > 0 else two_).append(lambda: join(CD, ind(CC, named(4))))
+        return [one_, two_, [lambda: ts(SELO, ind(CD, col("eu", 16)), Qc, A.add)]], cand, sel
 
     def bodies(t, win, sel):
         if t < R - 1:
-            return [lambda: cp(V("ui", 0, 16), ind(win, V(sel[0], sel[1], sel[1] + 1))), lambda: ts(V("ui", 32, 48), V("ui", 0, 16), 319, A.bitwise_and),
+            return [lambda: ts(V("ui", 0, 16), ind(win, V(sel[0], sel[1], sel[1] + 1)), -1.0, A.add), lambda: ts(V("ui", 32, 48), V("ui", 0, 16), 319, A.bitwise_and),
                     lambda: ts(V("ul", 0, 16), V("ui", 32, 48), 64.0, A.min)]
         return [lambda: cp(V("la", 0, 32), ind(win, sel)), lambda: turn(V("la", 32, 64), V("la", 0, 32)),
-                lambda: cp(V("ui", 0, 16), ind(V("la", 32, 64), NL)), lambda: ts(V("ui", 32, 48), V("ui", 0, 16), 319, A.bitwise_and),
+                lambda: ts(V("ui", 0, 16), ind(V("la", 32, 64), NL), -1.0, A.add), lambda: ts(V("ui", 32, 48), V("ui", 0, 16), 319, A.bitwise_and),
                 lambda: ts(V("ul", 0, 16), V("ui", 32, 48), 64.0, A.min)]
 
     def run(c):
@@ -536,7 +567,7 @@ def rank_program(g, core, T, topo):
                 mm(V("ps%d" % (b + 1), 0, 256), ES[b][0], ES[b][1], QT, PT, after)
         if t > 0:
             unpack(QT, PT, [])
-        gap(4)
+        gap(5)
         ts(V("bt", 16, 144), V("ps0", 0, 128), 0.0, A.is_gt)
         ts(V("bt", 144, 272), V("ps5", 0, 128), 0.0, A.is_gt)
         turn(V("tt", 0, 128), V("bt", 16, 144))
@@ -547,14 +578,15 @@ def rank_program(g, core, T, topo):
         if t > 0:
             for b in range(4):
                 act(V("vv", 256 * b, 256 * b + 256), V("ps%d" % (b + 1), 0, 256))
-        cp(V("gb", 0, 96), ind(V("tt", 0, 544), LG))
+        cp(V("gb", 0, 64), ind(V("tt", 0, 544), V("ku", 16, 20)))
         gap()
-        scan(V("sg", 0, 96), V("kh", 0, 96), V("gb", 0, 96), A.mult, A.add)
+        scan(V("sg", 0, 64), V("kh", 0, 64), V("gb", 0, 64), A.mult, A.add)
+        scan(V("sg", 64, 96), V("kh", 64, 96), V("gb", 0, 32), A.mult, A.add)
         gap()
         cp(V("idx", 0, 4), V("sg", 7, 32, 8))
         tt(V("tmp", 0, 16), ind(V("sg", 0, 64), LMI), EC, A.add)
         if t > 0:
-            spare += lasts() + [lambda: fetch(V("lu", 0, 16))]
+            spare += lasts()
         gap()
         cp(V("eo", 16, 80), ind(V("te", 0, 256), V("idx", 0, 4)))
         cp(V("offm", 0, 16), V("tmp", 0, 16))
@@ -564,8 +596,7 @@ def rank_program(g, core, T, topo):
         act(V("xa", 128, 192), ind(V("tx", 0, 448), V("offm", 12, 16)))
         for i in range(3, -1, -1):
             act(V("ma", 64 * i, 64 * i + 64), ind(V("tm", 0, 448), V("offm", 4 * i, 4 * i + 4)), 16.0 ** i, 0.5 if i == 3 else None)
-        if t == 0:
-            more()
+        act(V("na", 0, 256), ind(V("tc", 0, 448), V("offm", 0, 16)))
         gap()
         ts(V("offa", 0, 32), ind(V("et", 0, 160), LA), 16.0, A.mult, Qc, A.add)
         gap()
@@ -575,94 +606,129 @@ def rank_program(g, core, T, topo):
             cp(V("xa", 64 * i - 64, 64 * i), ind(V("xa", 64 * i, 64 * i + 64), o))
             tt(V("mb", 64 * i, 64 * i + 64), ind(mk, o), V("ma", 64 * i, 64 * i + 64), A.add)
             mk = V("mb", 64 * i, 64 * i + 64)
-            gap(3 - i)
+            gap()
         for e in range(4):
-            cp(V("yo", 16 + e, 80, 4), ind(V("xa", 0, 64), col("offa", 16 + 2 * e)))
+            (act if e % 2 else cp)(V("yo", 16 + e, 80, 4), ind(V("xa", 0, 64), col("offa", 16 + 2 * e)))
         tt(V("mb", 0, 64), ind(mk, V("offa", 0, 4)), V("ma", 0, 64), A.add)
+        NB_ = [V("nb", 16 * k, 16 * k + 16) for k in range(11)]
+        spare += [lambda: tt(V("na", 384, 448), ind(V("na", 192, 256), V("offa", 8, 12)), V("na", 128, 192), A.add),
+                  lambda: tt(V("na", 320, 384), ind(V("na", 384, 448), V("offa", 4, 8)), V("na", 64, 128), A.add),
+                  lambda: tt(V("na", 256, 320), ind(V("na", 320, 384), V("offa", 0, 4)), V("na", 0, 64), A.add),
+                  lambda: tt(V("nb", 0, 64), ind(V("na", 256, 320), PC), LT, A.mult),
+                  lambda: tt(NB_[4], ind(NB_[3], col("offb", 8)), NB_[2], A.add),
+                  lambda: tt(NB_[5], ind(NB_[4], col("offb", 4)), NB_[1], A.add),
+                  lambda: [tt(NB_[k], ind(NB_[5], col("offb", 0)), NB_[0], A.add) for k in (6, 7)]]
+        spare += [lambda k=k: tt(NB_[k + 1], ind(NB_[k], col("offc", 0)), NB_[6], A.add) for k in (7, 8, 9)]
+        gap()
         turn(V("yt", 0, 64), V("yo", 16, 80))
         turn(V("yt", 64, 160), V("yo", 0, 96))
         tt(V("dd", 0, 64), ind(V("mb", 0, 64), PC), DIAG, A.mult)
         ts(V("offb", 0, 32, 2), ind(V("yt", 0, 160), LB), Q12, A.add)
         gap()
         if t == 0:
+            more()
             unpack(V("qo", 0, 256), V("so", 0, 256), [("qo", 2 * len(off), {})])
-            for b in range(4):
-                act(V("vv", 256 * b, 256 * b + 256), V("ps%d" % (b + 1), 0, 256))
-            spare[:] = lasts() + spare
+            extra = lasts()
+            spare[:] = [lambda a=a, b=b: [a(), b()] for a, b in zip(spare, extra)] + spare[len(extra):]
         x, m = V("yo", 64, 80), V("dd", 48, 64)
         for i in (2, 1):
             o = col("offb", 4 * i)
-            cp(V("xb", 16 * i, 16 * i + 16), ind(x, o))
+            (act if t > 0 else cp)(V("xb", 16 * i, 16 * i + 16), ind(x, o))
             tt(V("ub", 16 * i, 16 * i + 16), ind(m, o), V("dd", 16 * i, 16 * i + 16), A.add)
             gap()
             x, m = V("xb", 16 * i, 16 * i + 16), V("ub", 16 * i, 16 * i + 16)
         o = col("offb", 0)
-        tt(V("ye", 0, 16), ind(x, o), DESC, A.add)
-        cp(V("xb", 0, 16), ind(x, o))
-        scan(V("ye", 16, 32), V("ye", 0, 16), GATE16, A.max, A.mult)
-        tt(V("ub", 0, 16), ind(m, o), V("dd", 0, 16), A.add)
-        ts(col("offc", 0), col("ye", 31), CA, A.add)
-        tt(V("ub", 96, 112), ind(m, o), V("dd", 0, 16), A.add)
-        gap()
-        o = col("offc", 0)
-        x, m = V("xb", 0, 16), V("ub", 96, 112)
-        for i in (0, 1):
-            cp(V("xc", 16 * i, 16 * i + 16), ind(x, o))
-            tt(V("ub", 48 + 16 * i, 64 + 16 * i), ind(m, o), V("ub", 0, 16), A.add)
-            gap()
-            x, m = V("xc", 16 * i, 16 * i + 16), V("ub", 48 + 16 * i, 64 + 16 * i)
         p = plans[t][r]
-        mo = slot("mo", r, t)
+        forms, exits = sorted(set(slot("mo", r, t, d) for d in range(r + 1, N))), [lambda: None] * 5
+        if r == N - 2:
+            forms = [slot("mo", r, t, N - 1)]
+
+        def form(mo):
+            o, i = V(mo[0], mo[1], mo[1] + 16), ind(V("xc", 64, 128), col("offc", 2))
+            if mo[0] == "mou" and t == 1 and r > 3:
+                return ts(o, i, 16.0, A.mult, Qc, A.add)
+            return ts(o, i, 16.0 if mo[0] == "mob" or r == 4 else 1.0, A.mult)
         if p["first"] or p["dirs"]:
-            wide = V(mo[0], 0, 16)
-            ts(wide, ind(x, o), 16.0 if r in HEADS or r == 4 else 1.0, A.mult)
-        MK = V("ub", 80, 96)
-        tt(MK, ind(m, o), V("ub", 0, 16), A.add)
+            exits = [lambda: act(V("xb", 0, 16), ind(x, o)),
+                     lambda: act(V("xc", 0, 64), ind(V("xb", 0, 16), V("offr", 8, 12))),
+                     lambda: act(V("xc", 64, 128), ind(V("xc", 0, 64), V("offr", 20, 24))),
+                     lambda: ts(col("offc", 2), col("ye", 31), CD, A.add, 16.0, A.mult),
+                     lambda: [form(mo) for mo in forms]]
+        exits[0]()
+        ts(V("offr", 0, 16), ind(x, o), 12.0, A.add)
+        tt(V("ye", 0, 16), ind(x, o), DESC, A.add)
+        tt(V("ub", 0, 16), ind(m, o), V("dd", 0, 16), A.add)
+        ts(V("offr", 16, 32), ind(x, o), 16.0, A.mult)
+        spread = [lambda k=k: act(V("mb", 64 * k, 64 * k + 64), ind(V("ub", 0, 16), V("ku", 34 + 4 * k, 38 + 4 * k))) for k in (2, 1, 0)]
+        weave(exits[1:3], spread)
+        if t > 0:
+            fetch(V("lu", 0, 16))
+        else:
+            act(V("k64", 468, 528, 4), row(15), 0.0, -1536.0)
+            for s in range(3):
+                act(V("k64", 336 + 17 * s, 384, 16), V("k64", 336 + 17 * s, 384, 16), 1.0, Q257)
+            act(V("k64", 480, 528, 16), row(3), 0.0, U3)
+            act(V("k64", 481, 516, 17), row(3), 0.0, U4)
+            for b in range(4):
+                act(V("vv", 256 * b, 256 * b + 256), V("ps%d" % (b + 1), 0, 256))
+        gap()
+        scan(V("ye", 16, 32), V("ye", 0, 16), GATE16, A.max, A.mult)
+        gap()
+        exits[3]()
+        tt(V("ma", 128, 192), ind(V("ub", 0, 16), V("offr", 8, 12)), V("mb", 128, 192), A.add)
+        ts(col("offc", 0), col("ye", 31), CA, A.add)
+        exits[4]()
+        gap()
+        tt(V("ma", 64, 128), ind(V("ma", 128, 192), V("offr", 20, 24)), V("mb", 64, 128), A.add)
         if p["first"]:
-            send([transfer(topo, core, k, e, T.sem["r%d" % t], ap(mo), ap(slot("mr", r, t))) for k, e in p["first"]],
-                 [mo], sum(len(e) for k, e in p["first"]))
+            ways = [(k, e, p["second"][k][0][0]) for k, e in p["first"]]
+            send([transfer(topo, core, k, e, T.sem["r%d" % t], ap(slot("mo", r, t, d)), ap(slot("mr", r, t, d))) for k, e, d in ways],
+                 forms, sum(len(e) for k, e in p["first"]))
         if p["dirs"]:
-            send([transfer(topo, core, cores[d], e, T.sem["m%d" % t], ap(mo), ap(slot("ml", r, t))) for d, e in p["dirs"]],
-                 [mo], sum(len(e) for k, e in p["dirs"]))
-        gap(99)
-        own, CAND = lists(MK), V("cand", 0, 64)
+            send([transfer(topo, core, cores[d], e, landed(T, r, t, d), ap(slot("mo", r, t, d)), ap(slot("ml", r, t, d))) for d, e in p["dirs"]],
+                 forms, sum(len(e) for k, e in p["dirs"]))
+        gap()
+        tt(V("ma", 0, 64), ind(V("ma", 64, 128), V("offr", 16, 20)), V("mb", 0, 64), A.add)
+        gap()
+        own, CAND = lists(V("ma", 0, 64), NB_[10]), V("cand", 0, 64)
+        run(own[0][:1])
+        gap()
+        run(own[0][1:])
+        gap()
         if t == 0:
             one(ahead, "luo", T.lu[:, 0:16], T.luo[:, 0:16], V("lu", 0, 16))
-            run(own)
+            run(own[1] + own[2] + own[3])
             one(ahead, "cando", T.cand[:, 0:64], T.cando[:, 0:64], CAND)
             send([transfer(topo, core, k, two[i], T.sem.rw, u8(T.qw[:, 256 * i:256 * i + 256]), u8(T.rq[:, 0:256]))
                   for i, k in enumerate(me["far"])], [V("qw", 0, 512)], len(on))
             fetch(V("luo", 0, 16), [("luo", len(off), {})])
+            theirs, half = [("cando", len(off), {})], sums()
+            steps, win, sel = entry(t, (r - HOP[0]) % N, V("cando", 0, 64))
+            pads = [lambda: fill(V("ft", 256, 512), 0.0), lambda: fill(V("ht", 256, 512), 0.0), lambda: ts(XL, XP, XB0, A.add)]
             ts(XB0, Q12, 64.0, A.mult, Q3, A.add)
-            fill(V("zt", 0, 512), 0.0)
-            fill(V("ft", 256, 512), 0.0)
-            fill(V("ht", 256, 512), 0.0)
-            ts(XL, XP, XB0, A.add)
-            fill(V("dh", 0, 320), 0.0)
-            quant(V("lq0", 0, 128), V("ls0", 0, 128), V("zt", 0, 512))
-            theirs, win, half = [("cando", len(off), {})], V("cando", 0, 64), sums()
-            steps, sel = entry(t, (r - HOP[0]) % N)
-            for s in steps:
-                run(s + half[:1])
-                half = half[1:]
-            run(half[:-1])
+            weave([lambda s=s: run(s) for s in steps], pads)
+            run(half[:2])
+            half = half[2:]
         else:
+            theirs, half = [], sums()
+            steps, win, sel = entry(t, r, CAND)
+            if last(r - 1, t, r):
+                run(half[:1] + own[1] + half[1:2] + own[2] + steps[0] + half[2:3] + own[3] + steps[1] + half[3:] + sum(steps[2:], []))
+            else:
+                run(half[:1] + own[1] + half[1:2] + own[2] + half[2:3] + own[3] + half[3:] + sum(steps, []))
+            half = []
             if t == R - 1:
                 act(V("tn", 0, 1024), ind(V(old, 0, 1024), XM))
-            theirs, win, half = [], CAND, sums()
-            steps, sel = entry(t, r)
-            steps = [[]] * (3 - len(steps)) + steps
-            run(half[:1] + own[:2] + half[1:2] + own[2:10] + steps[0] + own[10:11] + steps[1] + own[11:] + steps[2] + half[2:3])
         cp(V("ll", 0, 16), ind(win, V(sel[0], sel[1], sel[1] + 1)), theirs)
-        run(half[-1:])
+        run(half[:1])
         op("v", lambda: g.vector.tensor_copy(ap(ind(V("sc", 32, 2368), V("ll", 0, 16))), ap(row(256))),
            [V("sc", 32, 2368)], [V("ll", 0, 16), row(256)])
-        ub = bodies(t, win, sel) if t > 0 else []
+        ub = [[], [lambda: None] * 3, []][t] + (bodies(t, win, sel) if t > 0 else [])
         FL, UL = V("fl", 0, 4), V("ul", 0, 16)
-        run(ub[:1])
-        turn(V("st", 0, 64), V("sc", 32, 96))
-        turn(V("st", 64, 160), V("sc", 16, 112))
-        run(ub[1:2])
+        run(half[1:2] + ub[:1])
+        turn(V("st", 0, 64), V("sc", 33, 97))
+        turn(V("st", 64, 160), V("sc", 17, 113))
+        run(half[2:] + ub[1:2])
         cp(V("fl", 0, 16), ind(V("st", 0, 160), GL))
         run(ub[2:3])
         for b in range(4):
@@ -692,10 +758,13 @@ def rank_program(g, core, T, topo):
             after, lo = [tok], 64
         if t == 0:
             act(V(old, 0, 1024), ind(V("xn", 0, 1024), XL))
-            steps, sel = entry(t, r)
-            run(sum(steps, []) + bodies(t, CAND, sel))
+            steps, win, sel = entry(t, r, CAND)
+            weave([lambda s=s: run(s) for s in steps] + bodies(t, win, sel),
+                  [lambda: fill(V("zt", 0, 512), 0.0), lambda: fill(V("dh", 0, 320), 0.0),
+                   lambda: quant(V("lq0", 0, 128), V("ls0", 0, 128), V("zt", 0, 512))])
         if t == 1:
             iota(XQ, [[4, 4], [16, 4], [256, 4]])
+            iota(V("jrow", 0, 256), [[1, 16], [16, 4], [64, 4]])
             quant(V("qv", 0, 128), V("sv", 0, 128), V("vn", 0, 512))
             ts(XB1, Q12, 16.0, A.mult, Q3, A.add)
             ts(XM, XQ, XB1, A.add)
@@ -709,21 +778,28 @@ def rank_program(g, core, T, topo):
             old = "tn"
             act(V("olb", 0, 64), ind(V("jrow", 0, 256), FL))
             store("s", T.ol[:], T.olb[0:128:16, 0:64], V("olb", 0, 64))
-        for b in range(4):
-            tt(V(new, b, 1024, 4), ind(V("dh", 80 * b, 80 * b + 80), UL), V(old, b, 1024, 4), A.add)
-        for h in range(2):
-            quant(V("qt%d" % (t + 1), 128 * h, 128 * h + 128), V("pt%d" % (t + 1), 128 * h, 128 * h + 128), V(new, 512 * h, 512 * h + 512))
+        def update(a, b):
+            return [lambda k=k: tt(V(new, 4 * a + k, 4 * b, 4), ind(V("dh", 80 * k, 80 * k + 80), V("ul", a // 16, b // 16)),
+                                   V(old, 4 * a + k, 4 * b, 4), A.add) for k in range(4)]
+        requant = [lambda h=h: quant(V("qt%d" % (t + 1), 128 * h, 128 * h + 128), V("pt%d" % (t + 1), 128 * h, 128 * h + 128),
+                                     V(new, 512 * h, 512 * h + 512)) for h in range(2)]
+        if t < R - 1:
+            run(update(0, 256) + requant)
+        else:
+            second = update(128, 256)
+            run(update(0, 128) + second[:1] + requant[:1] + second[1:] + requant[1:])
         old, new = new, "ta" if new == "tb" else "tb"
 
-    QN_, SN = V("qt3", 0, 256), V("pt3", 0, 256)
+    SN = V("pt3", 0, 256)
     for h in range(2):
-        mm(V("ps%d" % (h + 1), 0, 128), V("qv", 0, 128), V("sv", 0, 128), V("qt3", 128 * h, 128 * h + 128), V("pt3", 128 * h, 128 * h + 128))
-    store("s", T.oc[:], u8(ap(QN_)), QN_)
-    for k in range(4):
-        store("a", T.osc[4 * k:4 * k + 4, 0:256], T.pt3[32 * k:32 * k + 4, 0:256], SN)
-    for h in range(2):
-        cp(V("ys", 128 * h, 128 * h + 128), V("ps%d" % (h + 1), 0, 128))
-    store("s", T.y[:], T.ys[:, 0:256], V("ys", 0, 256))
+        qh, yh = V("qt3", 128 * h, 128 * h + 128), V("ys", 128 * h, 128 * h + 128)
+        mm(V("ps%d" % (h + 1), 0, 128), V("qv", 0, 128), V("sv", 0, 128), qh, V("pt3", 128 * h, 128 * h + 128))
+        store("s", T.oc[:, 512 * h:512 * h + 512], u8(ap(qh)), qh)
+        if h == 1:
+            for k in range(4):
+                store("a" if k else "s", T.osc[4 * k:4 * k + 4, 0:256], T.pt3[32 * k:32 * k + 4, 0:256], SN)
+        (cp if h else act)(yh, V("ps%d" % (h + 1), 0, 128))
+        store("s", T.y[:, 128 * h:128 * h + 128], ap(yh), yh)
     for q in ("v", "a", "p", "gp"):
         g.wait_ge(T.sem[q], count[q])
     g.wait_ge(T.sem.sent, sent[0])

from concourse.bass import DstId, RemoteDMATransfer
from concourse.mybir import dt, AluOpType, ActivationFunctionType

A = AluOpType
ACT = ActivationFunctionType
N, C, R, HOP = 8, 256, 3, [2, 5, 3]
Q, S, BF, F, I, U = "float8_e4m3fn_x4", "uint8", "bfloat16", "float32", "int32", "uint16"


def _sb(n, d):
    return ("sbuf", [128, n], d)


SCRATCH = {
    "xn": _sb(1024, BF), "un": _sb(512, BF), "vn": _sb(512, BF), "ta": _sb(1024, BF), "tb": _sb(1024, BF), "tn": _sb(1024, BF),
    "qx": _sb(256, Q), "sx": _sb(256, S), "qu": _sb(128, Q), "su": _sb(128, S), "qv": _sb(128, Q), "sv": _sb(128, S),
    "qo": _sb(256, Q), "so": _sb(256, S), "qw": _sb(512, Q), "sw": _sb(512, S), "qp": _sb(512, Q), "sp": _sb(512, S),
    "rq": _sb(256, Q), "rs": _sb(256, S), "ez": _sb(520, BF), "qe": _sb(512, Q), "se": _sb(512, S),
    "qm": _sb(768, Q), "sm": _sb(768, S), "zt": _sb(512, BF), "ft": _sb(512, BF), "ht": _sb(512, BF),
    "ci": _sb(16, I), "kf": _sb(64, F), "cf": _sb(16, F), "cc": _sb(40, F), "ku": _sb(192, U), "r256": _sb(256, F), "jrow": _sb(256, F),
    "tc": _sb(448, BF), "na": _sb(448, BF), "nb": _sb(176, BF), "io3": _sb(544, F), "k64": _sb(768, F), "kh": _sb(96, BF), "tx": _sb(448, BF), "tm": _sb(448, BF), "te": _sb(320, BF),
    "bt": _sb(288, BF), "tt": _sb(544, BF), "gb": _sb(96, BF), "sg": _sb(96, F), "idx": _sb(4, U), "tmp": _sb(16, F), "offm": _sb(16, U),
    "eo": _sb(96, BF), "et": _sb(160, BF), "offa": _sb(32, U), "xa": _sb(192, BF), "ma": _sb(256, F), "mb": _sb(192, F),
    "yo": _sb(96, BF), "yt": _sb(160, BF), "offb": _sb(32, U), "dd": _sb(64, F), "xb": _sb(48, BF), "ub": _sb(112, F),
    "ye": _sb(32, F), "offc": _sb(4, U), "offr": _sb(32, U), "xc": _sb(128, BF),
    "la": _sb(64, F), "lu": _sb(16, U), "luo": _sb(16, U), "wf": _sb(384, F), "wi": _sb(64, I), "wp": _sb(384, F),
    "cand": _sb(64, F), "cando": _sb(64, F), "ca": _sb(192, F), "cb": _sb(192, BF), "eu": _sb(48, U), "selo": _sb(16, U), "ll": _sb(16, U),
    "sc": _sb(2368, BF), "st": _sb(160, BF), "fl": _sb(16, U), "vv": _sb(1024, BF), "vl": _sb(1024, BF), "ff": _sb(1024, BF),
    "dh": _sb(512, BF), "ui": _sb(96, I), "ul": _sb(16, U), "ys": _sb(256, F), "olb": _sb(64, F),
}
for _t in range(R):
    SCRATCH["qt%d" % _t] = _sb(256, Q)
    SCRATCH["pt%d" % _t] = _sb(256, S)
    SCRATCH["lq%d" % _t] = _sb(192, Q)
    SCRATCH["ls%d" % _t] = _sb(384, S)
for _k, _d in (("u", U), ("b", BF)):
    SCRATCH["mo" + _k] = _sb(16 * R, _d)
    SCRATCH["mr" + _k] = _sb(16 * R, _d)
    SCRATCH["ml" + _k] = _sb(16 * N * R, _d)
SCRATCH["qt3"] = _sb(256, Q)
SCRATCH["pt3"] = _sb(256, S)
for _t in range(8):
    SCRATCH["ps%d" % _t] = ("psum", [128, 512], F)
SEMAPHORES = ["v", "a", "p", "gp", "dx", "du", "dv", "dwc", "dws", "out", "sent", "wp", "rw", "qo", "luo", "cando", "near",
              "m0", "m1", "m2", "r0", "r1", "r2", "e0", "e1", "e2"]


def bits(engines):
    m = 0
    for e in engines:
        m |= 1 << e
    return m


def share(engines, n):
    k = 1
    while 2 * k * n <= len(engines):
        k *= 2
    sizes = [k] * n
    left = len(engines) - k * n
    for i in range(n):
        if left >= k:
            sizes[i] += k
            left -= k
    out, at = [], 0
    for s in sizes:
        out.append(engines[at:at + s])
        at += s
    return out


def plan(r, t, cores, topo):
    c = cores[r]
    wd = cores[(r - HOP[2]) % N]
    rel = [k for k in topo.cores_of(c) if k != c and topo.may_write(k, wd)]
    near = [k for k in rel if topo.die(k) == topo.die(c)]
    far = [k for k in rel if topo.die(k) != topo.die(c)]
    up = [d for d in range(N) if d != r and (r < d or (t == 0 and r < (d - HOP[0]) % N))]
    direct = [d for d in up if topo.may_write(c, cores[d])]
    cross = [d for d in up if d not in direct]
    off = topo.engines(c, cores[(r + HOP[0]) % N])
    on = topo.engines(c, near[0])
    use = near[:len(cross)]
    if t > 0 and len(cross) > len(near):
        cross, direct = direct[len(near):] + cross, direct[:len(near)]
        use = (near + far)[:len(cross)]
    first = list(zip(use, share(on, len(use)))) if use else []
    dirs = list(zip(direct, share(off, len(direct)))) if direct else []
    second = {}
    for i, k in enumerate(use):
        ds = cross[i::len(use)]
        second[k] = list(zip(ds, share(topo.engines(k, cores[ds[0]]), len(ds))))
    return {"wd": wd, "near": near, "far": far, "first": first, "dirs": dirs, "second": second, "off": off,
            "inner": share([e for e in on if e not in off], len(near))}


def transfer(topo, src_core, dst_core, engines, sem, src, dst):
    rid, pid = topo.addr(dst_core, src_core)
    return RemoteDMATransfer(dst_ids=[DstId(rid=rid, pnc=pid)], dma_engine_mask=bits(engines), remote_sem=sem, src=src, dst=dst)


def u8(ap):
    return ap.bitcast(dt.uint8)


def slot(kind, k, t, d):
    at = 16 * (N * t + k) if kind == "ml" else 16 * t
    return (kind + ("b" if head(k, t, d) else "u"), at, at + 4, 1)


def last(k, t, d):
    return t == R - 1 and k > 3 and d == k + 1


def head(k, t, d):
    return k in (1, 3) or (k == 6 and t == 0) or last(k, t, d)


def landed(T, k, t, d):
    return T.sem["near" if last(k, t, d) else "m%d" % t]


def relay_program(g, core, T, topo, r):
    cores = list(T.cores)
    p = plan(r, 0, cores, topo)
    sent = 0
    half = len(topo.engines(cores[r], core)) // 2
    if core in p["far"] or core in p["near"]:
        eng = topo.engines(core, p["wd"])
        g.wait_ge(T.sem.rw, half if core in p["far"] else len(p["inner"][p["near"].index(core)]))
        if core in p["far"]:
            k = p["far"].index(core)
            tr = transfer(topo, core, p["wd"], eng, T.sem.wp, u8(T.rq[:, 0:256]), u8(T.qp[:, 256 * k:256 * k + 256]))
        else:
            k = p["near"].index(core)
            tr = transfer(topo, core, p["wd"], eng, T.sem.wp, T.rs[:, 0:256], T.sp[:, 256 * k:256 * k + 256])
        g.remote_dma_fused([tr], local_sem=T.sem.sent)
        sent += len(eng)
    for t in range(R):
        p = plan(r, t, cores, topo)
        if core in p["second"]:
            g.wait_ge(T.sem["r%d" % t], len(dict(p["first"])[core]))
            trs = []
            for d, e in p["second"][core]:
                a, b = slot("mr", r, t, d), slot("ml", r, t, d)
                trs.append(transfer(topo, core, cores[d], e, landed(T, r, t, d), T[a[0]][:, a[1]:a[2]], T[b[0]][:, b[1]:b[2]]))
            g.remote_dma_fused(trs, local_sem=T.sem.sent)
            sent += sum(len(e) for d, e in p["second"][core])
    if sent:
        g.wait_ge(T.sem.sent, sent)


def rank_program(g, core, T, topo):
    r = T.rank_of(core)
    cores = list(T.cores)
    if r is None:
        mates = [c for c in topo.cores_of(core) if c in cores]
        if mates:
            relay_program(g, core, T, topo, cores.index(mates[0]))
        return
    plans = [[plan(k, t, cores, topo) for k in range(N)] for t in range(R)]
    me = plans[0][r]
    qs = {"v": g.vector, "a": g.scalar, "p": g.tensor, "gp": g, "s": g.sync}
    count = {"v": 0, "a": 0, "p": 0, "gp": 0}
    clock = {k: {} for k in qs}
    log = {}

    def V(name, a, b, s=1):
        return (name, a, b, s)

    def ap(v):
        if v[0] == "ind":
            return ap(v[1]).indirect(ap(v[2]))
        if v[3] == 1:
            return T[v[0]][:, v[1]:v[2]]
        return T[v[0]][:, v[1]:v[2]:v[3]]

    def ind(win, off):
        return ("ind", win, off)

    def meets(x, y):
        if x[2] <= y[1] or y[2] <= x[1]:
            return False
        return not (x[3] == y[3] and x[3] > 1 and (x[1] - y[1]) % x[3] != 0)

    def wait(q, tok):
        sem, val, known = tok
        if clock[q].get(sem, 0) < val:
            qs[q].wait_ge(T.sem[sem], val)
            clock[q][sem] = val
        for k, x in known.items():
            if clock[q].get(k, 0) < x:
                clock[q][k] = x

    def before(q, outs, ins, after):
        toks = list(after)
        for v, w in [(o, True) for o in outs] + [(i, False) for i in ins]:
            bank = v[0].startswith("ps")
            for pv, pw, pq, tok in log.get(v[0], []):
                if (bank and pq != q) or ((w or pw) and meets(v, pv)):
                    toks.append(tok)
        toks.sort(key=lambda t: -t[1])
        for tok in toks:
            wait(q, tok)

    def note(q, outs, ins, tok):
        for v, w in [(o, True) for o in outs] + [(i, False) for i in ins]:
            log.setdefault(v[0], []).append((v, w, q, tok))

    def flat(vs):
        out = []
        for v in vs:
            if isinstance(v, tuple):
                out += [v[1], v[2]] if v[0] == "ind" else [v]
        return out

    def op(q, call, outs, ins, after=()):
        outs, ins = list(outs), flat(ins)
        before(q, outs, ins, after)
        count[q] += 1
        call().then_inc(T.sem[q], 1)
        tok = (q, count[q], dict(clock[q]))
        note(q, outs, ins, tok)
        return tok

    def arg(x):
        return ap(x) if isinstance(x, tuple) else x

    def ts(o, i, s1, o0, s2=None, o1=None, after=()):
        if o1 is None:
            return op("v", lambda: g.vector.tensor_scalar(ap(o), ap(i), arg(s1), None, o0), [o], [i, s1], after)
        return op("v", lambda: g.vector.tensor_scalar(ap(o), ap(i), arg(s1), arg(s2), o0, o1), [o], [i, s1, s2], after)

    def tt(o, a, b, o0, after=()):
        return op("v", lambda: g.vector.tensor_tensor(ap(o), ap(a), ap(b), o0), [o], [a, b], after)

    def cp(o, i, after=()):
        return op("v", lambda: g.vector.tensor_copy(ap(o), ap(i)), [o], [i], after)

    def fill(o, c):
        return op("v", lambda: g.vector.memset(ap(o), c), [o], [])

    def scan(o, a, b, o0, o1, first=0.0):
        return op("v", lambda: g.vector.tensor_tensor_scan(ap(o), ap(a), ap(b), arg(first), o0, o1), [o], [a, b, first])

    def turn(o, i):
        return op("v", lambda: g.vector.transpose(ap(o), ap(i)), [o], [i])

    def quant(c, s, i):
        return op("v", lambda: g.vector.quantize_mx(ap(c), ap(s), ap(i)), [c, s], [i])

    def act(o, i, scale=None, bias=None, func=None, after=()):
        if bias is not None:
            return op("a", lambda: g.scalar.activation(ap(o), ap(i), func or ACT.Identity, bias=arg(bias), scale=arg(scale)), [o], [i, bias, scale], after)
        if scale is not None:
            return op("a", lambda: g.scalar.activation(ap(o), ap(i), ACT.Copy, scale=arg(scale)), [o], [i, scale], after)
        return op("a", lambda: g.scalar.activation(ap(o), ap(i), func or ACT.Copy), [o], [i], after)

    def mm(o, lc, ls, rc, rs, after=()):
        return op("p", lambda: g.tensor.matmul_mx(ap(o), ap(lc), ap(ls), ap(rc), ap(rs), True, True), [o], [lc, ls, rc, rs], after)

    def iota(o, pattern, mult=0, base=0, flag=True):
        if flag:
            return op("gp", lambda: g.iota(ap(o), pattern, base, mult, allow_small_or_imprecise_dtypes=True), [o], [])
        return op("gp", lambda: g.iota(ap(o), pattern, base, mult), [o], [])

    def load(q, sem, v, src, codes=False):
        qs[q].dma_start(u8(ap(v)) if codes else ap(v), src).then_inc(T.sem[sem], 16)
        note(q, [v], [], (sem, 16, {}))

    stores = [0]

    def store(q, dst, src_ap, v):
        before(q, [], [v], ())
        qs[q].dma_start(dst, src_ap).then_inc(T.sem.out, 16)
        stores[0] += 16

    sent = [0]

    def send(trs, ins, engines):
        before("gp", [], ins, ())
        g.remote_dma_fused(trs, local_sem=T.sem.sent)
        sent[0] += engines

    def col(name, k):
        return V(name, k, k + 1)

    def row(n):
        return V("r256", 0, n)

    def weave(*chains):
        for k in range(max(len(c) for c in chains)):
            for c in chains:
                if k < len(c):
                    c[k]()

    load("s", "dx", V("xn", 0, 1024), T.x[:])
    load("a", "du", V("un", 0, 512), T.u[:])
    wait("s", ("dx", 16, {}))
    wait("s", ("du", 16, {}))
    load("s", "dws", V("sw", 0, 512), T.ws[:])
    load("s", "dwc", V("qw", 0, 512), T.wc[:], codes=True)

    iota(V("ci", 0, 1), [[0, 1]], 1, flag=False)
    iota(V("r256", 0, 64), [[1, 64]])
    iota(V("ci", 12, 13), [[0, 1]], 4, flag=False)
    iota(V("ci", 13, 14), [[0, 1]], 64, flag=False)
    X3, XA, XB, KR = V("tx", 384, 448), V("io3", 0, 64), V("io3", 64, 128), V("io3", 480, 544)
    I16, D4, EP, XP, XQ, DI = [V("io3", 160 + 64 * k, 224 + 64 * k) for k in range(4)] + [V("wp", 0, 64), V("io3", 416, 480)]
    iota(X3, [[0, 16], [1, 4]])
    iota(XA, [[0, 4], [1, 4], [0, 4]])
    iota(XB, [[0, 4], [-4, 4], [1, 4]], base=1)
    iota(V("k64", 688, 704), [[0, 4], [64, 4]], base=192)
    iota(V("eo", 0, 96), [[0, 96]])
    iota(V("r256", 64, 256), [[1, 192]], base=64)
    iota(D4, [[1, 16], [0, 4]])
    fill(V("bt", 0, 288), 0.0)
    fill(V("kh", 0, 96), 2.0)
    fill(V("kf", 16, 56), 0.0)
    for k, m in enumerate((15, 16, 3, 12, 1, 6, 18, 20, 17)):
        ts(col("ci", k + 1), col("ci", 0), m, A.bitwise_and)
    ts(col("ci", 10), col("ci", 12), 48, A.bitwise_and)
    ts(col("ci", 11), col("ci", 13), 192, A.bitwise_and)
    fill(V("kh", 0, 64, 8), 0.0)
    fill(V("kh", 34, 64, 8), 0.0)
    fill(V("kh", 64, 96, 2), 0.0)
    cp(V("cf", 0, 12), V("ci", 0, 12))
    fill(V("ez", 0, 520), 0.0)
    P_, Qc, H16, Q3, Q12, Q1, Q6, Q18, Q20, Q17 = [col("cf", k) for k in range(10)]
    (OH0, OH1, OH2, OH3, NAT, RR, PA17, PA18, PA20, G1, T0, T1, T2, T3, T4, T5, T6, T7, T8, T9, LC, LM, CA, XB0, XB1, TOP, Q15, Q257,
     U0, U1, U2, U3, U4, NMID, HALF, CD) = [col("cc", k) for k in range(36)]
    PERM, LG, LMI, LA, LB, GL, PC, REP, REPT, REPK, NL, QU16, XL, XM = (
        V("ku", 0, 16), V("ku", 16, 22), V("ku", 22, 23), V("ku", 24, 26), V("ku", 26, 27), V("ku", 28, 29), V("ku", 30, 34),
        V("ku", 34, 38), V("ku", 38, 46), V("ku", 46, 50), V("ku", 50, 51), V("ku", 52, 54), V("ku", 64, 128), V("ku", 128, 192))
    DIAG, KEEP16, HK, NK, POW, DUMP = [V("k64", 64 * k, 64 * k + 64) for k in range(6)]
    LT, ONES = V("k64", 384, 448), V("k64", 448, 464)
    C16, DESC, GATE16, EC = [V("k64", 640 + 16 * k, 656 + 16 * k) for k in range(4)]
    ts(PERM, row(16), col("cf", 10), A.add, col("cf", 11), A.add)
    tt(XB, XA, XB, A.max)
    ts(V("cc", 0, 4), row(4), Q3, A.is_equal)
    ts(V("ez", 3, 259, 4), row(64), P_, A.is_equal, 0.5, A.mult)
    ts(V("tx", 320, 384), XB, -1.0, A.add)
    ts(GATE16, row(16), Qc, A.is_ge)
    act(V("k64", 128, 144), row(16), 0.0, 0.5)
    act(V("k64", 192, 208), row(16), 0.0)
    scan(V("k64", 256, 272), V("k64", 128, 144), V("k64", 192, 208), A.mult, A.add, 1.0)
    act(V("tx", 288, 304), row(16), 0.0)
    act(V("tx", 304, 320), row(16), 0.0, 1.0)
    act(V("tx", 192, 256), row(64), 0.0)
    act(V("tm", 384, 448), row(64), 0.0, 8.0)
    act(V("tm", 192, 256), row(64), 0.0, 1.0)
    act(V("tm", 272, 288), row(16), 0.0, 10.0)
    act(V("tm", 288, 320), row(32), 0.0, 2.0)
    act(V("tx", 272, 288), V("tx", 384, 400))
    act(V("tm", 320, 384), XA, -8.0, 8.0, ACT.Relu)
    act(PA18, Q18, 1.0, -9.0, ACT.Abs)
    act(T1, Q1, -9.0, 1225.0)
    act(V("tm", 320, 384), V("tm", 320, 384), 1.0, 4.0)
    act(T0, Q12, 0.25)
    act(T2, PA18, -136.0, T1)
    act(T3, Q3, func=ACT.Sign)
    act(T4, Q12, 2.0, 7.0)
    act(G1, Qc, 8.0, T2)
    act(V("tx", 256, 272), V("tx", 320, 336))
    act(V("kf", 16, 22, 2), row(3), 0.0, G1)
    act(col("kf", 22), T3, 32.0, T4)
    act(V("tm", 256, 272), V("tm", 320, 336), 1.0, 2.0)
    act(V("tx", 0, 192), V("tx", 256, 448))
    TS_ = V("te", 256, 320)
    SA, SB = V("wf", 0, 64), V("wf", 64, 128)
    QU, SU = V("qu", 0, 128), V("su", 0, 128)
    QX, SX, Q0T, S0T = V("qx", 0, 256), V("sx", 0, 256), V("qt0", 0, 256), V("pt0", 0, 256)
    quant(QX, SX, V("xn", 0, 1024))
    quant(QU, SU, V("un", 0, 512))
    act(SA, V("tx", 256, 320), OH1)
    for h in range(2):
        qh, sh, ph = V("qt0", 128 * h, 128 * h + 128), V("pt0", 128 * h, 128 * h + 128), V("ku", 8 * h, 8 * h + 8)
        op("v", lambda: g.vector.tensor_copy(ap(qh).bitcast(dt.uint32), ap(QX).bitcast(dt.uint32).indirect(ap(ph))), [qh], [QX, ph])
        op("a", lambda: g.scalar.activation(ap(sh), ap(SX).indirect(ap(ph)), ACT.Copy), [sh], [SX, ph])
    act(V("kf", 17, 22, 2), V("kf", 16, 22, 2), 1.0, 128.0)
    act(T5, Q12, 4.0, Q3)
    act(PA20, Q20, 1.0, -10.0, ACT.Abs)
    act(T7, Q6, 0.5)
    act(T8, T5, 1.0, 200.0)
    act(T6, PA18, -40.0, 360.0)
    act(col("kf", 24), PA20, -20.0, T8)
    act(col("kf", 25), H16, 5.0, T7)
    act(col("kf", 26), Q6, 8.0, T6)
    act(V("tm", 0, 192), V("tm", 256, 448), 1.0, 1.0)
    act(V("k64", 688, 704, 4), row(4), 0.0)
    act(T9, Q3, 16.0, T0)
    act(RR, Q3, 4.0, T0)
    act(PA17, Q17, 1.0, -8.5, ACT.Abs)
    act(U0, Q3, 16.0, 680.0)
    act(V("kf", 30, 34), row(4), 4.0, T9)
    act(col("kf", 28), PA17, -80.0, U0)
    act(V("kf", 34, 46), row(12))
    act(V("tc", 320, 384), XA, -1.0, 1.0, ACT.Relu)
    for a, b, c in ((384, 448, 1.0), (272, 288, 2.0), (288, 320, 1.0)):
        act(V("tc", a, b), row(b - a), 0.0, c)
    act(V("tc", 320, 384), V("tc", 320, 384), 1.0, 1.0)
    act(V("tc", 192, 256), row(64), 0.0, 1.0)
    act(V("yo", 0, 96), row(96), 0.0)
    act(col("kf", 50), RR, 1.0, H16)
    act(V("kf", 52, 54), row(2), 0.0, Qc)
    act(V("tc", 256, 272), V("tc", 320, 336), 1.0, 1.0)
    act(TOP, Q12, 1.0, -11.0, ACT.Relu)
    act(U1, Qc, 4.0, -56.0)
    act(V("tc", 0, 192), V("tc", 256, 448), 1.0, 1.0)

    def more():
        act(CD, Qc, 4.0, -60.0)
        act(DESC, row(16), -4.0, 60.0)
        act(U2, Q12, 1.0, U1)
        act(V("k64", 272, 288), V("k64", 256, 272))
        act(Q257, Qc, -257.0, 257.0, ACT.Relu)
        act(CA, TOP, -16.0, U2)
        act(Q15, Qc, 1.0, -14.0, ACT.Relu)
        act(U3, TOP, -15.0, -252.0)
        act(C16, row(16), 16.0)
        act(V("k64", 288, 320), V("k64", 256, 288))
        act(U4, Q257, -1.0, 512.0)
        act(LC, Q15, 267.0, U3)
        act(LM, Q15, -1000.0, 1255.0)
        act(U3, Q257, 1.0, 512.0)
        act(V("sc", 16, 128), row(112), 0.0)

    def spread_(k):
        tt(V("te", 64 * k, 64 * k + 64), V("te", 64 * k, 64 * k + 64), TS_, A.add)

    def later():
        return [
            lambda: [ts(SB, V("tx", 320, 384), OH2, A.mult), ts(TS_, V("tx", 384, 448), OH3, A.mult)],
            lambda: ts(V("te", 0, 256), V("tx", 0, 256), OH0, A.mult), lambda: tt(SA, SA, SB, A.add),
            lambda: cp(V("ku", 16, 22), V("kf", 16, 22)), lambda: tt(TS_, TS_, SA, A.add),
            lambda: [spread_(0), spread_(1)], lambda: [cp(V("ku", 22, 28), V("kf", 22, 28)), spread_(2)],
            lambda: [spread_(3), ts(V("ez", 259, 515, 4), V("r256", 64, 128), P_, A.is_equal, 0.5, A.mult)]] + [
            lambda b=b: quant(V("qe", 128 * b, 128 * b + 128), V("se", 128 * b, 128 * b + 128), V("ez", 3 - b, 515 - b)) for b in range(4)] + [
            lambda: [ts(DIAG, D4, Qc, A.is_equal), cp(V("ku", 28, 56), V("kf", 28, 56))],
            lambda: ts(LT, KR, RR, A.is_lt)]

    ahead, behind = cores[(r + HOP[0]) % N], cores[(r - HOP[0]) % N]
    off = me["off"]
    halves = share(off, 2)
    on = topo.engines(core, me["near"][0])
    two = share(on, 2)

    def one(to, sem, src, dst, v):
        send([transfer(topo, core, to, off, T.sem[sem], src, dst)], [v], len(off))

    iota(KR, [[1, 4], [4, 4], [0, 4]])
    one(ahead, "qo", u8(ap(Q0T)), u8(T.qo[:, 0:256]), Q0T)
    one(ahead, "qo", ap(S0T), T.so[:, 0:256], S0T)
    send([transfer(topo, core, k, me["inner"][i], T.sem.rw, T.sw[:, 256 * i:256 * i + 256], T.rs[:, 0:256]) for i, k in enumerate(me["near"])],
         [V("sw", 0, 512)], sum(len(e) for e in me["inner"]))
    iota(DUMP, [[0, 16], [512, 4]], base=512)
    iota(V("k64", 464, 528), [[0, 64]], base=512)
    iota(XP, [[4, 16], [64, 4]])
    wait("s", ("cando", len(off), {}))
    load("s", "dv", V("vn", 0, 512), T.v[:])
    src = plans[0][(r + HOP[2]) % N]
    w_here = ("wp", sum(len(topo.engines(k, core)) for k in src["near"] + src["far"]), {})

    def maps(t, near=False):
        n = 0
        for k, p in enumerate(plans[t]):
            if last(k, t, r) == near:
                n += sum(len(e) for d, e in p["dirs"] if d == r)
                n += sum(len(e) for rel in p["second"].values() for d, e in rel if d == r)
        return ("near" if near else "m%d" % t, n, {})

    ES = [(V("qe", 128 * b, 128 * b + 128), V("se", 128 * b, 128 * b + 128)) for b in range(4)]

    def exchange(m, a, to):
        one(to, "e%d" % m, u8(T.qm[:, a:a + 64]), u8(T["lq%d" % m][:, 128:192]), V("qm", a, a + 64))
        one(to, "e%d" % m, T.sm[:, a:a + 64], T["ls%d" % m][:, 128:192], V("sm", a, a + 64))
        return V("lq%d" % m, 64, 192), V("ls%d" % m, 64, 192), ("e%d" % m, 2 * len(off), {})

    def lasts():
        L0, L1, L2, L3 = [V("la", 16 * k, 16 * k + 16) for k in range(4)]
        return [lambda: ts(L3, V("sg", 65, 96, 2), 16.0, A.mult, Qc, A.add), lambda: tt(L0, L3, C16, A.add),
                lambda: ts(L1, L0, 256.0, A.is_ge, LC, A.mult), lambda: tt(L2, L0, L1, A.add), lambda: ts(V("lu", 0, 16), L2, LM, A.min)]

    def fetch(lu, after=()):
        for b in range(4):
            act(V("vl", 256 * b, 256 * b + 256), ind(V("vv", 256 * b, 256 * b + 256), lu), after=after)

    def lists(mk, before_):
        W0, BITS, NB, LCN, D1 = [V("wf", 64 * k, 64 * k + 64) for k in range(5)]
        RI = V("wi", 0, 64)
        count_ = [lambda e=e: scan(V("wf", 192 + 16 * e, 208 + 16 * e), V("k64", 464 + 16 * e, 480 + 16 * e), V("wf", 64 + 16 * e, 80 + 16 * e),
                                   A.add, A.add, col(before_[0], before_[1] + e)) for e in range(4)]
        return [[lambda: tt(W0, mk, POW, A.mult), lambda: tt(RI, mk, POW, A.mult)], [lambda: tt(BITS, RI, W0, A.is_gt)],
                [lambda: tt(D1, BITS, DUMP, A.mult)] + count_, [lambda: tt(V("cand", 0, 64), LCN, D1, A.subtract)]]

    def sums():
        return [lambda b=b: tt(V("ff", 256 * b, 256 * b + 256), V("vl", 256 * b, 256 * b + 256), V("ps%d" % (b + 1), 0, 256), A.add)
                for b in range(4)]

    def entry(t, upto, cand):
        def named(k):
            return slot("mo" if k == r else "ml", k, t, r)

        def first(k):
            v = named(k)
            return V(v[0], v[1], v[1] + 1)
        here = [maps(t)]
        SELO, Z, sel = V("selo", 0, 16), V("k64", 640, 644), V("selo", 0, 2)
        if upto == 0:
            return [[lambda: wait("v", here[0])]], cand, QU16
        if upto < 3:
            return [[lambda: ts(SELO, ind(Z if upto == 1 else named(1), first(0)), Qc, A.add, after=here)]], cand, sel
        CB, CC, CD = [V("cb", 64 * k, 64 * k + 64) for k in range(3)]
        join = act if t > 0 else cp
        one_ = [lambda: cp(V("eu", 0, 16), ind(named(1), first(0)), here), lambda: join(CB, ind(Z if upto == 3 else named(3), named(2)), after=here)]
        if last(upto - 1, t, r):
            E2, E4, E6 = [V("eu", 16 * k, 16 * k + 16) for k in range(3)]
            if upto == 6:
                one_.append(lambda: act(CD, ind(row(64), named(4))))
            if upto == 7:
                one_ += [lambda: act(CC, ind(Z, named(5))), lambda: act(CD, ind(CC, named(4)))]
            steps = [one_, [lambda: ts(E4, ind(CB, col("eu", 0)), 1.0 if upto > 5 else 0.0625, A.mult)]]
            if upto > 5:
                steps.append([lambda: ts(E6, ind(CD, col("eu", 16)), 0.0625, A.mult)])
            steps.append([lambda: ts(SELO, ind(named(upto - 1), col("eu", 16 * len(steps) - 32)), Qc, A.add, after=[maps(t, True)])])
            return steps, cand, sel
        if upto < 5 or t > 0:
            steps = [one_, [lambda: ts(SELO, ind(CB, col("eu", 0)), Qc, A.add)], []]
            for i, k in enumerate(range(upto - 1, 3, -1)):
                o = V("ca", 64 * i, 64 * i + 64)
                steps[i].insert(0, lambda o=o, c=cand, k=k: cp(o, ind(c, named(k)), here))
                cand = o
            return [s for s in steps if s], cand, sel
        two_ = [lambda: cp(V("eu", 16, 32), ind(CB, col("eu", 0)))]
        if upto == 5:
            one_.append(lambda: join(CD, ind(row(64), named(4))))
        else:
            one_.insert(0, lambda: join(CC, ind(Z if upto == 6 else named(6), named(5)), after=here))
            (one_ if t > 0 else two_).append(lambda: join(CD, ind(CC, named(4))))
        return [one_, two_, [lambda: ts(SELO, ind(CD, col("eu", 16)), Qc, A.add)]], cand, sel

    def bodies(t, win, sel):
        if t < R - 1:
            return [lambda: ts(V("ui", 0, 16), ind(win, V(sel[0], sel[1], sel[1] + 1)), -1.0, A.add), lambda: ts(V("ui", 32, 48), V("ui", 0, 16), 319, A.bitwise_and),
                    lambda: ts(V("ul", 0, 16), V("ui", 32, 48), 64.0, A.min)]
        return [lambda: cp(V("la", 0, 32), ind(win, sel)), lambda: turn(V("la", 32, 64), V("la", 0, 32)),
                lambda: ts(V("ui", 0, 16), ind(V("la", 32, 64), NL), -1.0, A.add), lambda: ts(V("ui", 32, 48), V("ui", 0, 16), 319, A.bitwise_and),
                lambda: ts(V("ul", 0, 16), V("ui", 32, 48), 64.0, A.min)]

    def run(c):
        for f in c:
            f()

    old, new = "ta", "tb"
    for t in range(R):
        spare = later() if t == 0 else []

        def gap(n=1):
            for k in range(min(n, len(spare))):
                spare.pop(0)()
        QT, PT = V("qt%d" % t, 0, 256), V("pt%d" % t, 0, 256)
        for h, bank in enumerate(("ps0", "ps5")):
            mm(V(bank, 0, 128), QU, SU, V(QT[0], 128 * h, 128 * h + 128), V(PT[0], 128 * h, 128 * h + 128))

        def unpack(QT, PT, after):
            for b in range(4):
                mm(V("ps%d" % (b + 1), 0, 256), ES[b][0], ES[b][1], QT, PT, after)
        if t > 0:
            unpack(QT, PT, [])
        gap(5)
        ts(V("bt", 16, 144), V("ps0", 0, 128), 0.0, A.is_gt)
        ts(V("bt", 144, 272), V("ps5", 0, 128), 0.0, A.is_gt)
        turn(V("tt", 0, 128), V("bt", 16, 144))
        turn(V("tt", 256, 384), V("bt", 0, 128))
        turn(V("tt", 128, 256), V("bt", 144, 272))
        turn(V("tt", 384, 544), V("bt", 128, 288))
        gap()
        if t > 0:
            for b in range(4):
                act(V("vv", 256 * b, 256 * b + 256), V("ps%d" % (b + 1), 0, 256))
        cp(V("gb", 0, 64), ind(V("tt", 0, 544), V("ku", 16, 20)))
        gap()
        scan(V("sg", 0, 64), V("kh", 0, 64), V("gb", 0, 64), A.mult, A.add)
        scan(V("sg", 64, 96), V("kh", 64, 96), V("gb", 0, 32), A.mult, A.add)
        gap()
        cp(V("idx", 0, 4), V("sg", 7, 32, 8))
        tt(V("tmp", 0, 16), ind(V("sg", 0, 64), LMI), EC, A.add)
        if t > 0:
            spare += lasts()
        gap()
        cp(V("eo", 16, 80), ind(V("te", 0, 256), V("idx", 0, 4)))
        cp(V("offm", 0, 16), V("tmp", 0, 16))
        gap()
        turn(V("et", 0, 64), V("eo", 16, 80))
        turn(V("et", 64, 160), V("eo", 0, 96))
        act(V("xa", 128, 192), ind(V("tx", 0, 448), V("offm", 12, 16)))
        for i in range(3, -1, -1):
            act(V("ma", 64 * i, 64 * i + 64), ind(V("tm", 0, 448), V("offm", 4 * i, 4 * i + 4)), 16.0 ** i, 0.5 if i == 3 else None)
        act(V("na", 0, 256), ind(V("tc", 0, 448), V("offm", 0, 16)))
        gap()
        ts(V("offa", 0, 32), ind(V("et", 0, 160), LA), 16.0, A.mult, Qc, A.add)
        gap()
        mk = V("ma", 192, 256)
        for i in (2, 1):
            o = V("offa", 4 * i, 4 * i + 4)
            cp(V("xa", 64 * i - 64, 64 * i), ind(V("xa", 64 * i, 64 * i + 64), o))
            tt(V("mb", 64 * i, 64 * i + 64), ind(mk, o), V("ma", 64 * i, 64 * i + 64), A.add)
            mk = V("mb", 64 * i, 64 * i + 64)
            gap()
        for e in range(4):
            (act if e % 2 else cp)(V("yo", 16 + e, 80, 4), ind(V("xa", 0, 64), col("offa", 16 + 2 * e)))
        tt(V("mb", 0, 64), ind(mk, V("offa", 0, 4)), V("ma", 0, 64), A.add)
        NB_ = [V("nb", 16 * k, 16 * k + 16) for k in range(11)]
        spare += [lambda: tt(V("na", 384, 448), ind(V("na", 192, 256), V("offa", 8, 12)), V("na", 128, 192), A.add),
                  lambda: tt(V("na", 320, 384), ind(V("na", 384, 448), V("offa", 4, 8)), V("na", 64, 128), A.add),
                  lambda: tt(V("na", 256, 320), ind(V("na", 320, 384), V("offa", 0, 4)), V("na", 0, 64), A.add),
                  lambda: tt(V("nb", 0, 64), ind(V("na", 256, 320), PC), LT, A.mult),
                  lambda: tt(NB_[4], ind(NB_[3], col("offb", 8)), NB_[2], A.add),
                  lambda: tt(NB_[5], ind(NB_[4], col("offb", 4)), NB_[1], A.add),
                  lambda: [tt(NB_[k], ind(NB_[5], col("offb", 0)), NB_[0], A.add) for k in (6, 7)]]
        spare += [lambda k=k: tt(NB_[k + 1], ind(NB_[k], col("offc", 0)), NB_[6], A.add) for k in (7, 8, 9)]
        gap()
        turn(V("yt", 0, 64), V("yo", 16, 80))
        turn(V("yt", 64, 160), V("yo", 0, 96))
        tt(V("dd", 0, 64), ind(V("mb", 0, 64), PC), DIAG, A.mult)
        ts(V("offb", 0, 32, 2), ind(V("yt", 0, 160), LB), Q12, A.add)
        gap()
        if t == 0:
            more()
            unpack(V("qo", 0, 256), V("so", 0, 256), [("qo", 2 * len(off), {})])
            extra = lasts()
            spare[:] = [lambda a=a, b=b: [a(), b()] for a, b in zip(spare, extra)] + spare[len(extra):]
        x, m = V("yo", 64, 80), V("dd", 48, 64)
        for i in (2, 1):
            o = col("offb", 4 * i)
            (act if t > 0 else cp)(V("xb", 16 * i, 16 * i + 16), ind(x, o))
            tt(V("ub", 16 * i, 16 * i + 16), ind(m, o), V("dd", 16 * i, 16 * i + 16), A.add)
            gap()
            x, m = V("xb", 16 * i, 16 * i + 16), V("ub", 16 * i, 16 * i + 16)
        o = col("offb", 0)
        p = plans[t][r]
        forms, exits = sorted(set(slot("mo", r, t, d) for d in range(r + 1, N))), [lambda: None] * 5
        if r == N - 2:
            forms = [slot("mo", r, t, N - 1)]

        def form(mo):
            o, i = V(mo[0], mo[1], mo[1] + 16), ind(V("xc", 64, 128), col("offc", 2))
            if mo[0] == "mou" and t == 1 and r > 3:
                return ts(o, i, 16.0, A.mult, Qc, A.add)
            return ts(o, i, 16.0 if mo[0] == "mob" or r == 4 else 1.0, A.mult)
        if p["first"] or p["dirs"]:
            exits = [lambda: act(V("xb", 0, 16), ind(x, o)),
                     lambda: act(V("xc", 0, 64), ind(V("xb", 0, 16), V("offr", 8, 12))),
                     lambda: act(V("xc", 64, 128), ind(V("xc", 0, 64), V("offr", 20, 24))),
                     lambda: ts(col("offc", 2), col("ye", 31), CD, A.add, 16.0, A.mult),
                     lambda: [form(mo) for mo in forms]]
        exits[0]()
        ts(V("offr", 0, 16), ind(x, o), 12.0, A.add)
        tt(V("ye", 0, 16), ind(x, o), DESC, A.add)
        tt(V("ub", 0, 16), ind(m, o), V("dd", 0, 16), A.add)
        ts(V("offr", 16, 32), ind(x, o), 16.0, A.mult)
        spread = [lambda k=k: act(V("mb", 64 * k, 64 * k + 64), ind(V("ub", 0, 16), V("ku", 34 + 4 * k, 38 + 4 * k))) for k in (2, 1, 0)]
        weave(exits[1:3], spread)
        if t > 0:
            fetch(V("lu", 0, 16))
        else:
            act(V("k64", 468, 528, 4), row(15), 0.0, -1536.0)
            for s in range(3):
                act(V("k64", 336 + 17 * s, 384, 16), V("k64", 336 + 17 * s, 384, 16), 1.0, Q257)
            act(V("k64", 480, 528, 16), row(3), 0.0, U3)
            act(V("k64", 481, 516, 17), row(3), 0.0, U4)
            for b in range(4):
                act(V("vv", 256 * b, 256 * b + 256), V("ps%d" % (b + 1), 0, 256))
        gap()
        scan(V("ye", 16, 32), V("ye", 0, 16), GATE16, A.max, A.mult)
        gap()
        exits[3]()
        tt(V("ma", 128, 192), ind(V("ub", 0, 16), V("offr", 8, 12)), V("mb", 128, 192), A.add)
        ts(col("offc", 0), col("ye", 31), CA, A.add)
        exits[4]()
        gap()
        tt(V("ma", 64, 128), ind(V("ma", 128, 192), V("offr", 20, 24)), V("mb", 64, 128), A.add)
        if p["first"]:
            ways = [(k, e, p["second"][k][0][0]) for k, e in p["first"]]
            send([transfer(topo, core, k, e, T.sem["r%d" % t], ap(slot("mo", r, t, d)), ap(slot("mr", r, t, d))) for k, e, d in ways],
                 forms, sum(len(e) for k, e in p["first"]))
        if p["dirs"]:
            send([transfer(topo, core, cores[d], e, landed(T, r, t, d), ap(slot("mo", r, t, d)), ap(slot("ml", r, t, d))) for d, e in p["dirs"]],
                 forms, sum(len(e) for k, e in p["dirs"]))
        gap()
        tt(V("ma", 0, 64), ind(V("ma", 64, 128), V("offr", 16, 20)), V("mb", 0, 64), A.add)
        gap()
        own, CAND = lists(V("ma", 0, 64), NB_[10]), V("cand", 0, 64)
        run(own[0][:1])
        gap()
        run(own[0][1:])
        gap()
        if t == 0:
            one(ahead, "luo", T.lu[:, 0:16], T.luo[:, 0:16], V("lu", 0, 16))
            run(own[1] + own[2] + own[3])
            one(ahead, "cando", T.cand[:, 0:64], T.cando[:, 0:64], CAND)
            send([transfer(topo, core, k, two[i], T.sem.rw, u8(T.qw[:, 256 * i:256 * i + 256]), u8(T.rq[:, 0:256]))
                  for i, k in enumerate(me["far"])], [V("qw", 0, 512)], len(on))
            fetch(V("luo", 0, 16), [("luo", len(off), {})])
            theirs, half = [("cando", len(off), {})], sums()
            steps, win, sel = entry(t, (r - HOP[0]) % N, V("cando", 0, 64))
            pads = [lambda: fill(V("ft", 256, 512), 0.0), lambda: fill(V("ht", 256, 512), 0.0), lambda: ts(XL, XP, XB0, A.add)]
            ts(XB0, Q12, 64.0, A.mult, Q3, A.add)
            weave([lambda s=s: run(s) for s in steps], pads)
            run(half[:2])
            half = half[2:]
        else:
            theirs, half = [], sums()
            steps, win, sel = entry(t, r, CAND)
            if last(r - 1, t, r):
                run(half[:1] + own[1] + half[1:2] + own[2] + steps[0] + half[2:3] + own[3] + steps[1] + half[3:] + sum(steps[2:], []))
            else:
                run(half[:1] + own[1] + half[1:2] + own[2] + half[2:3] + own[3] + half[3:] + sum(steps, []))
            half = []
            if t == R - 1:
                act(V("tn", 0, 1024), ind(V(old, 0, 1024), XM))
        cp(V("ll", 0, 16), ind(win, V(sel[0], sel[1], sel[1] + 1)), theirs)
        run(half[:1])
        op("v", lambda: g.vector.tensor_copy(ap(ind(V("sc", 32, 2368), V("ll", 0, 16))), ap(row(256))),
           [V("sc", 32, 2368)], [V("ll", 0, 16), row(256)])
        ub = [[], [lambda: None] * 3, []][t] + (bodies(t, win, sel) if t > 0 else [])
        FL, UL = V("fl", 0, 4), V("ul", 0, 16)
        run(half[1:2] + ub[:1])
        turn(V("st", 0, 64), V("sc", 33, 97))
        turn(V("st", 64, 160), V("sc", 17, 113))
        run(half[2:] + ub[1:2])
        cp(V("fl", 0, 16), ind(V("st", 0, 160), GL))
        run(ub[2:3])
        for b in range(4):
            (act if b % 2 else cp)(V("ft", b, 256, 4), ind(V("ff", 256 * b, 256 * b + 256), FL))
        a = [384, 128, 512][t]
        fc, fs = V("qm", a, a + 128), V("sm", a, a + 128)
        quant(fc, fs, V("ft", 0, 512))
        run(ub[3:])
        wc, ws, lo, after = "qp", "sp", 0, [w_here]
        if t == 0:
            wc, ws, after = "qw", "sw", []
        if t == 1:
            fc, fs, tok = exchange(1, a, ahead)
            lo, after = 64, [tok, w_here]
            for m in (1, 2):
                quant(V("lq%d" % m, 0, 128), V("ls%d" % m, 0, 128), V("zt", 0, 512))
        for b in range(4):
            mm(V("ps%d" % (b + 1), 0, 128), V(wc, 128 * b, 128 * b + 128), V(ws, 128 * b, 128 * b + 128), fc, fs, after)
        for b in range(4):
            ts(V("ht", b, 256, 4), V("ps%d" % (b + 1), lo, lo + 64), 0.03125, A.mult)
        a = [256, 0, 640][t]
        hc, hs = V("qm", a, a + 128), V("sm", a, a + 128)
        quant(hc, hs, V("ht", 0, 512))
        after, lo = [], 0
        if t < 2:
            hc, hs, tok = exchange(2 * t, a, behind)
            after, lo = [tok], 64
        if t == 0:
            act(V(old, 0, 1024), ind(V("xn", 0, 1024), XL))
            steps, win, sel = entry(t, r, CAND)
            weave([lambda s=s: run(s) for s in steps] + bodies(t, win, sel),
                  [lambda: fill(V("zt", 0, 512), 0.0), lambda: fill(V("dh", 0, 320), 0.0),
                   lambda: quant(V("lq0", 0, 128), V("ls0", 0, 128), V("zt", 0, 512))])
        if t == 1:
            iota(XQ, [[4, 4], [16, 4], [256, 4]])
            iota(V("jrow", 0, 256), [[1, 16], [16, 4], [64, 4]])
            quant(V("qv", 0, 128), V("sv", 0, 128), V("vn", 0, 512))
            ts(XB1, Q12, 16.0, A.mult, Q3, A.add)
            ts(XM, XQ, XB1, A.add)
        banks = ["ps5", "ps6", "ps7", "ps0"]
        for b in range(4):
            mm(V(banks[b], 0, 128), ES[b][0], ES[b][1], hc, hs, after)
        ts(V("dh", 0, 64), V(banks[0], lo, lo + 64), 2.0, A.mult)
        for b in range(1, 4):
            act(V("dh", 80 * b, 80 * b + 64), V(banks[b], lo, lo + 64), 2.0)
        if t == R - 1:
            old = "tn"
            act(V("olb", 0, 64), ind(V("jrow", 0, 256), FL))
            store("s", T.ol[:], T.olb[0:128:16, 0:64], V("olb", 0, 64))
        def update(a, b):
            return [lambda k=k: tt(V(new, 4 * a + k, 4 * b, 4), ind(V("dh", 80 * k, 80 * k + 80), V("ul", a // 16, b // 16)),
                                   V(old, 4 * a + k, 4 * b, 4), A.add) for k in range(4)]
        requant = [lambda h=h: quant(V("qt%d" % (t + 1), 128 * h, 128 * h + 128), V("pt%d" % (t + 1), 128 * h, 128 * h + 128),
                                     V(new, 512 * h, 512 * h + 512)) for h in range(2)]
        if t < R - 1:
            run(update(0, 256) + requant)
        else:
            second = update(128, 256)
            run(update(0, 128) + second[:1] + requant[:1] + second[1:] + requant[1:])
        old, new = new, "ta" if new == "tb" else "tb"

    SN = V("pt3", 0, 256)
    for h in range(2):
        qh, yh = V("qt3", 128 * h, 128 * h + 128), V("ys", 128 * h, 128 * h + 128)
        mm(V("ps%d" % (h + 1), 0, 128), V("qv", 0, 128), V("sv", 0, 128), qh, V("pt3", 128 * h, 128 * h + 128))
        store("s", T.oc[:, 512 * h:512 * h + 512], u8(ap(qh)), qh)
        if h == 1:
            for k in range(4):
                store("a" if k else "s", T.osc[4 * k:4 * k + 4, 0:256], T.pt3[32 * k:32 * k + 4, 0:256], SN)
        (cp if h else act)(yh, V("ps%d" % (h + 1), 0, 128))
        store("s", T.y[:, 128 * h:128 * h + 128], ap(yh), yh)
    for q in ("v", "a", "p", "gp"):
        g.wait_ge(T.sem[q], count[q])
    g.wait_ge(T.sem.sent, sent[0])
    g.wait_ge(T.sem.out, stores[0])
